import numpy as np, ml_dtypes
CORES = [5,29,101,125,133,157,229,253]
N = 8
import mx_ref
BF = ml_dtypes.bfloat16
def pick(q, e):
    c = np.concatenate([q[0].reshape(128, -1, 4), np.zeros((128, 1, 4), np.uint8)], axis=1); s = np.concatenate([q[1], np.ones((16, 1), np.uint8)], axis=1)
    return (np.ascontiguousarray(c[:, e].reshape(128, -1)), np.ascontiguousarray(s[:, e]))
def join(*qs):
    return (np.concatenate([q[0] for q in qs], axis=1), np.concatenate([q[1] for q in qs], axis=1))
def put(q, e, v):
    c, s = q[0].reshape(128, -1, 4).copy(), q[1].copy(); c[:, e] = v[0].reshape(128, -1, 4); s[:, e] = v[1]
    return (c.reshape(128, -1), s)
def pk(c, s):
    return (np.ascontiguousarray(c), mx_ref.live(s))
def emit(q):
    return q[0], q[1]
def tile(rs):
    return np.stack(rs, axis=2).reshape(128, -1).astype(BF)
def cut(t, i, w=512):
    return t[:, w * i:w * i + w]
def f(rng, *shape):
    return mx_ref.flush((rng.standard_normal(shape, dtype=np.float32) * np.exp2(rng.integers(-2, 3, shape[:-1] + (1,)))).astype(BF))
def wide(rng, *shape, cols=0):
    v = rng.standard_normal(shape, dtype=np.float32) * np.exp2(rng.integers(-12, 13, shape)).astype(np.float32)
    if cols: v *= np.repeat(np.exp2(rng.integers(-cols, cols + 1, shape[:-2] + (1, shape[-1] // 4))) * (rng.random(shape[:-2] + (1, shape[-1] // 4)) > 0.0625), 4, axis=-1).astype(np.float32)
    return mx_ref.flush(v.astype(BF))
T, CAPP, CAPR = 128, 48, 32
def same(t):
    return np.stack([np.concatenate([t, np.zeros((128, 512 - t.shape[1]), BF)], axis=1)] * N)
def bf(t):
    return np.asarray(t, np.float32).astype(BF)
def sized(rng, *shape):
    return 1 + rng.random(shape)
def signs(rng, *shape):
    return 1 - 2 * rng.integers(0, 2, shape)
def setup_inputs(rng):
    return {"x": f(rng, N, 128, 4 * T), "rt": same(f(rng, 128, 4 * N)), "w": f(rng, N, 128, 2048), "u": same(f(rng, 128, 4)), "v": f(rng, N, 128, 512)}
def planted(rng, a, b, own=1.0, off=1.0, way=1):
    d = setup_inputs(rng)
    at = np.arange(128) // (128 // N)
    big, mid = at[None, :, None] == a[:, None, :], at[None, :, None] == b[:, None, :]
    k = np.where(big, 16.0, np.where(mid, 4.0, 1.0))[..., None]
    g = np.where((big | mid)[..., None], 1, signs(rng, N, 128, T, 4))
    d["x"] = bf(sized(rng, N, 128, T, 4) * k * g).reshape(N, 128, 4 * T)
    d["rt"] = same(bf(sized(rng, 128, N, 4) * (at[:, None] == np.arange(N))[..., None]).reshape(128, 4 * N))
    d["w"] = bf(sized(rng, N, 128, 2048) * signs(rng, N, 128, 2048) * np.where(at == np.arange(N)[:, None], own, off)[..., None])
    d["u"] = same(bf(way * sized(rng, 128, 4)))
    return d
def setup_inputs_crowd(rng):
    a, b = np.zeros((N, T), int), np.zeros((N, T), int)
    for s in range(N):
        h, k = (s + (0, 1, 1)[s % 3]) % N, (s + (1, 0, 2)[s % 3]) % N
        rest = rng.permutation(np.array([e for e in range(N) if e not in (h, k)]))
        m, n = rest[np.arange(T) % rest.size], rest[np.arange(1, T + 1) % rest.size]
        p = rng.permutation(T)
        p[:CAPP + 16] = np.sort(p[:CAPP + 16])
        m[:CAPP + 16] = h
        m[CAPP + 16:CAPP + 16 + CAPR] = k
        n[np.concatenate([np.arange(CAPP + 16 + CAPR, T), np.arange(CAPP)])[:CAPP - CAPR]] = k
        a[s, p], b[s, p] = m, n
    return planted(rng, a, b, own=2.0 ** -4, way=-2.0 ** 24)
def setup_inputs_second(rng):
    a, b = np.zeros((N, T), int), np.zeros((N, T), int)
    one, i = int(rng.integers(0, N)), np.arange(T)
    half, last = CAPP // 2, CAPP + CAPP // 2 + 16
    for s in range(N):
        g = rng.permutation(N)
        h, k, rest = g[0], g[1], g[2:]
        m, n = rest[i % rest.size], rest[(i + 1) % rest.size]
        if s == one:
            m[:] = h
            n = g[1 + i % (N - 1)]
        else:
            m[:last] = h
            n[half:last] = k
        turn = (i + rng.integers(0, 2)) % 2 == 1
        p = rng.permutation(T)
        p[:last] = np.sort(p[:last])
        a[s, p], b[s, p] = np.where(turn, m, n), np.where(turn, n, m)
    return planted(rng, a, b, own=2.0 ** 4, way=-1)
def setup_inputs_ties(rng):
    kind = np.stack([rng.permutation(T) % N for s in range(N)])
    e = rng.integers(2, N, (N, T))
    a = np.where(kind == 0, 0, e)
    b = np.where(kind == 0, e, np.where(kind == 1, 0, e ^ 1))
    d = planted(rng, a, b)
    d["rt"][:, :, 4:8] = d["rt"][:, :, :4]
    d["w"][1::2] = d["w"][::2]
    d["w"][:2, :, :4] = 0
    d["w"][1, 128 // N, 0] = BF(4)
    return d
def setup_inputs_zero(rng):
    a = rng.integers(0, N, (N, T))
    b = (a + rng.integers(1, N, (N, T))) % N
    d = planted(rng, a, b, way=-1)
    at, late = np.arange(128) // (128 // N), np.arange(128) % (128 // N) >= 128 // N // 2
    kind = np.stack([rng.permutation(T) % 4 for s in range(N)])
    low = (at[None, :, None] == a[:, None, :]) & (kind % 2 == 1)[:, None, :] | (at[None, :, None] == b[:, None, :]) & (kind >= 2)[:, None, :]
    t = d["x"].astype(np.float32).reshape(N, 128, T, 4)
    d["x"] = bf(np.where(late[None, :, None, None], np.abs(t) * np.where(low, -1, 1)[..., None], t)).reshape(N, 128, 4 * T)
    d["rt"] = bf(d["rt"].astype(np.float32) * ~late[None, :, None])
    d["w"] = bf(np.abs(d["w"].astype(np.float32)) * ((at == np.arange(N)[:, None]) & late)[..., None])
    return d
def setup_inputs_spread(rng):
    return {**setup_inputs(rng), "x": wide(rng, N, 128, 4 * T, cols=6)}
def check_inputs(d):
    b = []
    for k in ("x", "rt", "w", "u", "v"):
        t = np.abs(d[k].astype(np.float32))
        if not (np.isfinite(t).all() and ((t == 0) | (t >= 2.0 ** -30) & (t <= 2.0 ** 30)).all()): b.append("a value of " + k)
    for k, n in (("rt", N), ("u", 1)):
        t = d[k].astype(np.float32)
        if (t[:, :, 4 * n:] != 0).any(): b.append(k + " has numbers behind its first columns")
        if (t != t[:1]).any(): b.append(k + " isn't the same on all ranks")
    return b
def reference(x, rt, w, u, v):
    q, a, b = [], [], []
    for s in range(N):
        q.append(mx_ref.quantize(np.ascontiguousarray(x[s])))
        z = mx_ref.matmul(mx_ref.quantize(np.ascontiguousarray(rt[s])), q[s])[:N] + np.float32(0)
        o = np.argsort(-z, axis=0, kind="stable")
        a.append(o[0])
        b.append(o[1])
    took = [[np.flatnonzero((a[s] == e) | (b[s] == e))[:CAPP] for e in range(N)] for s in range(N)]
    good = np.full((N, N, T), -np.inf, np.float32)
    made = []
    for e in range(N):
        t = join(*[pick(q[s], np.concatenate([took[s][e], np.full(CAPP - took[s][e].size, -1)])) for s in range(N)])
        rs = [mx_ref.matmul(mx_ref.quantize(np.ascontiguousarray(cut(w[e], i))), t) for i in range(4)]
        made.append(mx_ref.quantize(tile([np.maximum(k, np.float32(0)) * np.float32(0.0625) for k in rs])))
        z = mx_ref.matmul(mx_ref.quantize(np.ascontiguousarray(u[e])), made[e])[0] + np.float32(0)
        for s in range(N): good[s, e, took[s][e]] = z[s * CAPP:s * CAPP + took[s][e].size]
    every = join(*made)
    oc, osc = np.zeros((N, 128, 4 * T), np.uint8), np.zeros((N, 16, T), np.uint8)
    wn, y = np.zeros((N, 1, T), np.float32), np.zeros((N, 128, T), np.float32)
    for s in range(N):
        ga, gb = good[s, a[s], np.arange(T)], good[s, b[s], np.arange(T)]
        win = np.where(ga >= gb, a[s], b[s])
        none = np.maximum(ga, gb) == -np.inf
        wn[s, 0] = np.where(none, -100, -1 - win)
        at = np.full(T, -1)
        for e in range(N):
            home = np.flatnonzero((win == e) & ~none)[:CAPR]
            wn[s, 0, home] = e
            at[home] = (e * N + s) * CAPP + np.searchsorted(took[s][e], home)
        z = pick(every, at)
        oc[s], osc[s] = emit(z)
        y[s] = mx_ref.matmul(mx_ref.quantize(np.ascontiguousarray(v[s])), z)
    return {"oc": oc, "osc": osc, "wn": wn, "y": y}

@@ -1,0 +1,461 @@
+from concourse.bass import DstId, RemoteDMATransfer
+from concourse.mybir import dt, AluOpType as A, AxisListType, ActivationFunctionType as F
+
+C8, PL, BF, FP, I32, U16 = "float8_e4m3fn_x4", "uint8", "bfloat16", "float32", "int32", "uint16"
+CAPP, CAPR, DUMP = 48, 32, 32
+BIG = 2.0 ** 98
+SCRATCH = {
+    "xt": ("sbuf", [128, 520], BF), "xq": ("sbuf", [128, 130], C8), "xs": ("sbuf", [128, 130], PL),
+    "rtt": ("sbuf", [128, 512], BF), "rq": ("sbuf", [128, 128], C8), "rs": ("sbuf", [128, 128], PL),
+    "rp": ("sbuf", [128, 128], C8), "rps": ("sbuf", [128, 128], PL),
+    "wt": ("sbuf", [128, 2048], BF), "wq": ("sbuf", [128, 512], C8), "ws": ("sbuf", [128, 512], PL),
+    "ut": ("sbuf", [128, 512], BF), "uq": ("sbuf", [128, 128], C8), "us": ("sbuf", [128, 128], PL),
+    "up": ("sbuf", [128, 128], C8), "ups": ("sbuf", [128, 128], PL),
+    "vt": ("sbuf", [128, 512], BF), "vq": ("sbuf", [128, 128], C8), "vs": ("sbuf", [128, 128], PL),
+    "xg": ("sbuf", [128, 336], C8), "xgs": ("sbuf", [128, 336], PL),
+    "hx": ("sbuf", [128, 96], C8), "hxs": ("sbuf", [128, 96], PL),
+    "lx": ("sbuf", [128, 384], C8), "lxs": ("sbuf", [128, 384], PL),
+    "ht": ("sbuf", [128, 1536], BF), "hq": ("sbuf", [128, 384], C8), "hqs": ("sbuf", [128, 384], PL),
+    "hr": ("sbuf", [128, 96], C8), "hrs": ("sbuf", [128, 96], PL),
+    "hb": ("sbuf", [128, 386], C8), "hbs": ("sbuf", [128, 386], PL),
+    "hab": ("sbuf", [128, 258], C8), "habs": ("sbuf", [128, 258], PL),
+    "zq": ("sbuf", [128, 128], C8), "zs": ("sbuf", [128, 128], PL),
+    "yb": ("sbuf", [128, 128], FP),
+    "ip": ("sbuf", [128, 1], I32), "ii": ("sbuf", [128, 4], I32), "ff": ("sbuf", [128, 4], FP),
+    "r8": ("sbuf", [128, 8], FP), "jr": ("sbuf", [128, 128], FP), "jr2": ("sbuf", [128, 128], FP),
+    "q2": ("sbuf", [128, 32], FP), "e4": ("sbuf", [128, 4], FP), "ee": ("sbuf", [128, 4], FP),
+    "lp": ("sbuf", [128, 8], U16), "l0": ("sbuf", [128, 8], U16), "vals": ("sbuf", [128, 32], BF),
+    "th": ("sbuf", [128, 2, 8], FP), "kv": ("sbuf", [128, 32], FP), "kvt": ("sbuf", [128, 32], FP),
+    "kt": ("sbuf", [128, 8], FP), "sign": ("sbuf", [128, 64], FP), "ones": ("sbuf", [128, 128], FP),
+    "cap": ("sbuf", [128, 128], FP), "z32": ("sbuf", [128, 32], FP), "cw": ("sbuf", [128, 2], FP),
+    "dq": ("sbuf", [128, 2], FP),
+    "bs": ("sbuf", [128, 64], FP), "gt": ("sbuf", [128, 64], FP), "rk": ("sbuf", [128, 64], FP),
+    "nn": ("sbuf", [128, 128], BF), "nt": ("sbuf", [128, 128], BF), "cs": ("sbuf", [128, 128], FP),
+    "ct": ("sbuf", [128, 32], FP), "un": ("sbuf", [128, 8], FP), "oh": ("sbuf", [128, 2, 8], FP),
+    "p1": ("sbuf", [128, 2, 8], FP), "pr": ("sbuf", [128, 2, 9], FP),
+    "of": ("sbuf", [128, 2], U16), "win": ("sbuf", [128, 416], BF), "dd": ("sbuf", [128, 8, 3, 2, 16], BF),
+    "ot": ("sbuf", [128, 768], BF), "t1": ("sbuf", [128, 24], FP), "t2": ("sbuf", [128, 24], FP),
+    "od": ("sbuf", [128, 26], U16),
+    "vm": ("sbuf", [128, 2], FP), "tk": ("sbuf", [128, 2], FP), "po": ("sbuf", [128, 2], FP),
+    "mm": ("sbuf", [128, 3], FP), "zst": ("sbuf", [128, 5, 32], FP), "zt": ("sbuf", [128, 5, 32], FP),
+    "rz": ("sbuf", [128, 5, 128], FP), "ka": ("sbuf", [128, 128], FP),
+    "kb": ("sbuf", [128, 128], FP), "kk": ("sbuf", [128, 128], FP), "pa": ("sbuf", [128, 128], FP),
+    "pb": ("sbuf", [128, 128], FP), "pp": ("sbuf", [128, 128], FP), "d2": ("sbuf", [128, 2, 8, 2, 16], FP),
+    "d2t": ("sbuf", [128, 512], FP), "oh2": ("sbuf", [128, 16], U16),
+    "qb": ("sbuf", [128, 128], FP), "ge": ("sbuf", [128, 128], FP), "ww": ("sbuf", [128, 128], FP),
+    "cc": ("sbuf", [128, 132], FP), "fl": ("sbuf", [128, 128], FP), "vv": ("sbuf", [128, 8, 2, 16], BF),
+    "vt2": ("sbuf", [128, 8, 32], BF), "oz": ("sbuf", [128, 8], U16),
+    "g1": ("sbuf", [128, 128], FP), "g2": ("sbuf", [128, 128], FP), "g3": ("sbuf", [128, 128], BF),
+    "g3t": ("sbuf", [128, 4, 32], BF), "g4": ("sbuf", [128, 32], FP), "g5": ("sbuf", [128, 32], FP),
+    "g6": ("sbuf", [128, 32], FP),
+    "psa": ("psum", [128, 2048], "float32"), "psb": ("psum", [128, 2048], "float32"),
+}
+SEMAPHORES = ["v", "gi", "srt", "sx", "sw", "suv", "srq", "srp", "srps", "sxq", "mS", "sod1", "sod2", "sg1", "sg1s", "sg2", "sg2s",
+              "sg3", "sg3s", "loc", "hd", "hret", "dsp", "dcr", "rsp", "rcr", "suq", "sup", "sups", "swq", "sz", "so",
+              "r1s", "r2s", "q1", "q2", "soh", "shab", "shabs", "mq", "sww", "sfl", "sgg", "soz", "szq", "szs",
+              "my", "sy", "swn", "fin", "svq"] + ["m%d" % i for i in range(8)]
+
+
+def rank_program(g, core, T, topo):
+    S = T.sem
+    ranks = list(T.cores)
+    N = len(ranks)
+    u8, u32, X = dt.uint8, dt.uint32, AxisListType.X
+
+    def order(r):
+        rot = [(r + k) % N for k in range(1, N)]
+        far = [q for q in rot if not topo.may_write(ranks[r], ranks[q])]
+        near = [q for q in rot if topo.may_write(ranks[r], ranks[q])]
+        return far, near
+
+    def pos(r, q):
+        far, near = order(r)
+        return (far + near + [r]).index(q)
+
+    def handers(r):
+        c = ranks[r]
+        can = [h for h in topo.cores_of(c) if h != c and all(topo.may_write(h, ranks[q]) for q in order(r)[0])]
+        return sorted(can, key=lambda h: (topo.die(h) == topo.die(c), h))[:2]
+
+    def send(dst_core, es, sem, src, dst):
+        rid, pid = topo.addr(dst_core, core)
+        return RemoteDMATransfer(dst_ids=[DstId(rid=rid, pnc=pid)], dma_engine_mask=sum(1 << e for e in es), remote_sem=sem, src=src, dst=dst)
+
+    def cod(t, a, b):
+        return t[:, a:b].bitcast(u8)
+
+    def w32(t, a, b):
+        return t[:, a:b].bitcast(u32)
+
+    def direct(r, i):
+        es = topo.engines(ranks[r], ranks[order(r)[1][i]])
+        k = len(es) // 4
+        if i == 0:
+            return es[0:k], es[2 * k:3 * k]
+        if i == 1:
+            return es[k:2 * k], es[3 * k:]
+        return es[2 * k:], es[0:2 * k]
+
+    rank = T.rank_of(core)
+
+    if rank is None:
+        mine = [r for r in range(N) if ranks[r] in topo.cores_of(core)]
+        if not mine or core not in handers(mine[0]):
+            return
+        r = mine[0]
+        i = handers(r).index(core)
+        to = order(r)[0][2 * i:2 * i + 2]
+        n = 0
+        for sem_in, sem_out, bc, bp, dc, dp, base in ((S.hd, S.dcr, T.hx, T.hxs, T.lx, T.lxs, 0), (S.hret, S.rcr, T.hr, T.hrs, T.hb, T.hbs, 2)):
+            g.wait_ge(sem_in, 16)
+            for planes in (False, True):
+                t = []
+                for k, q in enumerate(to):
+                    es = topo.engines(core, ranks[q])[4 * k:4 * k + 4]
+                    a, b = base + CAPP * pos(q, r), CAPP * k
+                    if planes:
+                        t.append(send(ranks[q], es, sem_out, bp[:, b:b + CAPP], dp[:, a:a + CAPP]))
+                    else:
+                        t.append(send(ranks[q], es, sem_out, cod(bc, b, b + CAPP), cod(dc, a, a + CAPP)))
+                    n += len(es)
+                g.remote_dma_fused(t, local_sem=S.loc)
+        g.wait_ge(S.loc, n)
+        return
+
+    far, near = order(rank)
+    blocks = far + near + [rank]
+    half, own = CAPP * len(far), CAPP * (N - 1)
+    near_in = sum(len(direct(q, order(q)[1].index(rank))[0]) + len(direct(q, order(q)[1].index(rank))[1]) for q in near)
+    far_in = 8 * len(far)
+    v, sc, te, sy = g.vector, g.scalar, g.tensor, g.sync
+    n, nl = [0], [0]
+
+    def op(c):
+        c.then_inc(S.v, 1)
+        n[0] += 1
+
+    def done():
+        v.wait_ge(S.v, n[0])
+
+    def tt(*a):
+        op(v.tensor_tensor(*a))
+
+    def ts(*a):
+        op(v.tensor_scalar(*a))
+
+    def fused(t, k):
+        g.remote_dma_fused(t, local_sem=S.loc)
+        nl[0] += k
+
+    def to_handers(bc, bp, sem_c, sem_p, sem, dc, dp):
+        es = topo.engines(core, handers(rank)[0])
+        for planes in (False, True):
+            t = []
+            for i, h in enumerate(handers(rank)):
+                a, e = 2 * CAPP * i, es[8 * i:8 * i + 8]
+                t.append(send(h, e, sem, bp[:, a:a + 96], dp[:]) if planes else send(h, e, sem, cod(bc, a, a + 96), cod(dc, 0, 96)))
+            g.wait_ge(sem_p if planes else sem_c, 1)
+            fused(t, 16)
+
+    def to_near(bc, bp, sem_c, sem_p, sem, dc, dp, base):
+        for planes in (False, True):
+            t, k = [], 0
+            for i, q in enumerate(near):
+                e = direct(rank, i)[planes]
+                a, b = half + CAPP * i, base + CAPP * pos(q, rank)
+                t.append(send(ranks[q], e, sem, bp[:, a:a + CAPP], dp[:, b:b + CAPP]) if planes else
+                         send(ranks[q], e, sem, cod(bc, a, a + CAPP), cod(dc, b, b + CAPP)))
+                k += len(e)
+            g.wait_ge(sem_p if planes else sem_c, 1)
+            fused(t, k)
+
+    sc.dma_start(T.rtt[:, 0:32], T.rt[:, 0:32]).then_inc(S.srt, 16)
+    sy.dma_start(T.xt[:, 8:520], T.x[:]).then_inc(S.sx, 16)
+    sc.dma_start(T.wt[:], T.w[:]).then_inc(S.sw, 16)
+    sy.dma_start(T.ut[:], T.u[:]).then_inc(S.suv, 16)
+    sy.dma_start(T.vt[:], T.v[:]).then_inc(S.suv, 16)
+
+    loose = dict(allow_small_or_imprecise_dtypes=True)
+    g.iota(T.ip[:], [[0, 1]], 0, 1).then_inc(S.gi, 1)
+    g.iota(T.e4[:], [[2, 4]], 0, 0, **loose).then_inc(S.gi, 1)
+    g.iota(T.r8[:], [[1, 8]], 0, 0, **loose).then_inc(S.gi, 1)
+    g.iota(T.q2[:], [[0, 2], [1, 16]], 2, 0, **loose).then_inc(S.gi, 1)
+    g.iota(T.jr[:], [[1, 128]], 1, 0, **loose).then_inc(S.gi, 1)
+
+    op(v.memset(T.rtt[:, 32:512], 0.0))
+    op(v.memset(T.xt[:, 0:8], 0.0))
+    op(v.memset(T.sign[:], 1.0))
+    op(v.memset(T.kv[:], 0.0))
+    v.wait_ge(S.gi, 5)
+    ts(T.ii[:, 0:1], T.ip[:], 7, None, A.bitwise_and)
+    ts(T.ii[:, 1:2], T.ip[:], 3, 1, A.logical_shift_right, A.bitwise_and)
+    ts(T.ii[:, 2:3], T.ip[:], 112, None, A.bitwise_and)
+    ts(T.ii[:, 3:4], T.ip[:], 31, None, A.bitwise_and)
+    done()
+    op(v.tensor_copy(T.ff[:], T.ii[:]))
+    op(v.memset(T.sign[:, 0:64:9], -1.0))
+    for i, e in enumerate(blocks):
+        op(v.memset(T.kv[:, e:e + 1], 1.0 * DUMP + CAPP * i - 1))
+    done()
+    ts(T.ee[:], T.e4[:], T.ff[:, 1:2], None, A.add)
+    op(v.memset(T.sign[:, 0:64:8], 0.0))
+    op(v.transpose(T.kvt[:], T.kv[:]))
+    ts(T.kt[:], T.kv[:, 0:8], 1.0 * CAPP, None, A.add)
+    ts(T.vals[:], T.q2[:], T.ff[:, 2:3], None, A.add)
+    ts(T.th[:, 0, :], T.r8[:], -1.0, None, A.mult)
+    ts(T.th[:, 1, :], T.r8[:], -1.0, 1.0, A.mult, A.add)
+    ts(T.dq[:, 0:1], T.ff[:, 1:2], 16.0, None, A.mult)
+    ts(T.dq[:, 1:2], T.ff[:, 1:2], 16.0, 1.0, A.mult, A.add)
+    done()
+    ts(T.lp[:, 0:4], T.ee[:], T.ff[:, 0:1], None, A.max)
+    ts(T.lp[:, 4:8], T.ee[:], T.ff[:, 0:1], None, A.min)
+    for k in range(2):
+        ts(T.pr[:, k, 8:9], T.ff[:, 0:1], 2.0, T.dq[:, k:k + 1], A.mult, A.add)
+    op(v.memset(T.ones[:], 1.0))
+    op(v.memset(T.nn[:], 0.0))
+    done()
+
+    v.wait_ge(S.srt, 16)
+    v.quantize_mx(T.rq[:], T.rs[:], T.rtt[:]).then_inc(S.srq, 1)
+    v.wait_ge(S.srq, 1)
+    v.tensor_copy(w32(T.rp, 0, 128), w32(T.rq, 0, 128).indirect(T.lp[:])).then_inc(S.srp, 1)
+    sc.wait_ge(S.srq, 1)
+    sc.activation(T.rps[:, 0:128], T.rs[:, 0:128].indirect(T.lp[:]), F.Copy).then_inc(S.srps, 1)
+    v.wait_ge(S.sx, 16)
+    v.quantize_mx(T.xq[:], T.xs[:], T.xt[:]).then_inc(S.sxq, 1)
+    te.wait_ge(S.srp, 1)
+    te.wait_ge(S.srps, 1)
+    te.wait_ge(S.sxq, 1)
+    te.matmul_mx(T.psb[:, 0:128], T.xq[:, 2:130], T.xs[:, 2:130], T.rp[:, 0:128], T.rps[:, 0:128], True, True).then_inc(S.mS, 1)
+    op(v.memset(T.win[:], 0.0))
+    sy.wait_ge(S.sxq, 1)
+    for q_, s_, a in ((T.hb, T.hbs, 0), (T.hab, T.habs, 0), (T.hab, T.habs, 256)):
+        sy.dma_start(cod(q_, a, a + 2), cod(T.xq, 0, 2)).then_inc(S.sz, 16)
+        sy.dma_start(s_[:, a:a + 2], T.xs[:, 0:2]).then_inc(S.sz, 16)
+
+    v.wait_ge(S.mS, 1)
+    op(v.tensor_copy(T.bs[:], T.psb[:, 64:128]))
+    done()
+    tt(T.gt[:], T.psb[:, 0:64], T.bs[:], A.is_gt)
+    done()
+    op(v.tensor_tensor_scan(T.rk[:], T.sign[:], T.gt[:], 0.0, A.mult, A.add))
+    done()
+    for b in range(4):
+        for d in range(b + 1, 4):
+            tt(T.nn[32 * d:32 * d + 32, 32 * b:32 * b + 8], T.rk[32 * b:32 * b + 32, 7:64:8], T.th[32 * b:32 * b + 32, 1, :], A.is_le)
+    tt(T.nn[:, 96:104], T.rk[:, 7:64:8], T.th[:, 1, :], A.is_le)
+    done()
+    op(v.transpose(T.nt[:], T.nn[:]))
+    tt(T.oh[:, 0, :], T.rk[:, 7:64:8], T.th[:, 0, :], A.is_equal)
+    tt(T.oh[:, 1, :], T.rk[:, 7:64:8], T.th[:, 1, :], A.is_equal)
+    done()
+    op(v.tensor_tensor_scan(T.cs[:], T.ones[:], T.nt[:], T.kvt[:, 0:1], A.mult, A.add))
+    done()
+    op(v.transpose(T.ct[:], T.cs[:, 96:128]))
+    done()
+    tt(T.un[:], T.ct[:, 0:8], T.kt[:], A.is_le)
+    for k in range(2):
+        tt(T.p1[:, k, :], T.oh[:, k, :], T.ct[:, 0:8], A.mult)
+    done()
+    for k in range(2):
+        tt(T.pr[:, k, 0:8], T.p1[:, k, :], T.un[:], A.mult)
+    done()
+    op(v.tensor_reduce(T.of[:], T.pr[:], X, A.max))
+    done()
+    op(v.tensor_copy(T.win[:].indirect(T.of[:]), T.vals[:]))
+    done()
+    for h in range(2):
+        a, b = 4 * h, 4 * h + 4
+        for d in range(2):
+            op(v.tensor_copy(T.dd[:, a:b, :, d, :], T.win[:, DUMP + CAPP * a:DUMP + CAPP * b]))
+        done()
+        op(v.transpose(T.ot[:, 96 * a:96 * b], T.dd[:, a:b]))
+        done()
+        c = slice(3 * a, 3 * b)
+        tt(T.t1[:, c], T.ot[:, 96 * a:96 * b:32], T.ot[:, 96 * a + 16:96 * b:32], A.add)
+        done()
+        tt(T.t2[0:64, c], T.t1[0:64, c], T.t1[64:128, c], A.add)
+        tt(T.t2[64:128, c], T.t1[64:128, c], T.t1[0:64, c], A.add)
+        done()
+        sem, k = (S.sod1, 0) if h == 0 else (S.sod2, 0)
+        for lo, hi, to in ([(0, 12, 0)] if h == 0 else [(12, 21, 12), (21, 24, 22)]):
+            for p, o in ((0, 32), (32, 0), (64, 96), (96, 64)):
+                v.tensor_tensor(T.od[p:p + 32, to:to + hi - lo], T.t2[p:p + 32, lo:hi], T.t2[o:o + 32, lo:hi], A.add).then_inc(sem, 1)
+                k += 1
+        v.wait_ge(sem, k)
+        sc.wait_ge(sem, k)
+        if h == 0:
+            v.tensor_copy(w32(T.xg, 0, half), w32(T.xq, 0, 130).indirect(T.od[:, 0:12])).then_inc(S.sg1, 1)
+            sc.activation(T.xgs[:, 0:half], T.xs[:, 0:130].indirect(T.od[:, 0:12]), F.Copy).then_inc(S.sg1s, 1)
+        else:
+            v.tensor_copy(w32(T.xg, half, own), w32(T.xq, 0, 130).indirect(T.od[:, 12:21])).then_inc(S.sg2, 1)
+            sc.activation(T.xgs[:, half:own], T.xs[:, 0:130].indirect(T.od[:, 12:21]), F.Copy).then_inc(S.sg2s, 1)
+            v.tensor_copy(w32(T.lx, own, own + CAPP), w32(T.xq, 0, 130).indirect(T.od[:, 22:25])).then_inc(S.sg3, 1)
+            sc.activation(T.lxs[:, own:own + CAPP], T.xs[:, 0:130].indirect(T.od[:, 22:25]), F.Copy).then_inc(S.sg3s, 1)
+
+    to_handers(T.xg, T.xgs, S.sg1, S.sg1s, S.hd, T.hx, T.hxs)
+    to_near(T.xg, T.xgs, S.sg2, S.sg2s, S.dsp, T.lx, T.lxs, 0)
+
+    v.wait_ge(S.sw, 16)
+    for i in range(4):
+        v.quantize_mx(T.wq[:, 128 * i:128 * i + 128], T.ws[:, 128 * i:128 * i + 128], T.wt[:, 512 * i:512 * i + 512]).then_inc(S.swq, 1)
+
+    op(v.memset(T.zst[:], 0.0))
+    op(v.memset(T.z32[:], 0.0))
+    op(v.tensor_reduce(T.vm[:], T.pr[:, :, 0:8], X, A.max))
+    done()
+    for k in range(2):
+        tt(T.zst[:, k, 0:8], T.oh[:, k, :], T.un[:], A.mult)
+    ts(T.tk[:], T.vm[:], 0.0, None, A.is_gt)
+    ts(T.po[:], T.vm[:], 2.0 - DUMP, 0.0, A.add, A.max)
+    done()
+    tt(T.mm[:, 0:1], T.tk[:, 0:1], T.tk[:, 1:2], A.mult)
+    for k in range(2):
+        ts(T.zst[:, 3 + k, :], T.z32[:], T.po[:, k:k + 1], None, A.add)
+    done()
+    ts(T.mm[:, 1:2], T.tk[:, 0:1], 2.0, T.mm[:, 0:1], A.mult, A.subtract)
+    done()
+    ts(T.mm[:, 2:3], T.mm[:, 1:2], -1.0, -BIG, A.add, A.mult)
+    done()
+    ts(T.zst[:, 2, :], T.z32[:], T.mm[:, 2:3], None, A.add)
+    done()
+    op(v.transpose(T.zt[:], T.zst[:]))
+    done()
+    for b in range(4):
+        op(v.tensor_copy(T.rz[0:32, :, 32 * b:32 * b + 32], T.zt[32 * b:32 * b + 32, :, :]))
+    done()
+    op(v.tensor_copy(T.rz[32:64, :, :], T.rz[0:32, :, :]))
+    done()
+    op(v.tensor_copy(T.rz[64:128, :, :], T.rz[0:64, :, :]))
+    done()
+
+    def expert(h):
+        a = half * (1 - h)
+        ps, t0 = (T.psa, 0) if h == 0 else (T.psb, 4 * half)
+        if h == 0:
+            te.wait_ge(S.swq, 4)
+            te.wait_ge(S.sg3, 1)
+            te.wait_ge(S.sg3s, 1)
+            te.wait_ge(S.dsp, near_in)
+        else:
+            te.wait_ge(S.dcr, far_in)
+        for i in range(4):
+            te.matmul_mx(ps[:, 512 * i:512 * i + half], T.wq[:, 128 * i:128 * i + 128], T.ws[:, 128 * i:128 * i + 128],
+                         T.lx[:, a:a + half], T.lxs[:, a:a + half], True, True).then_inc(S["m%d" % (4 * h + i)], 1)
+        rs = S.r1s if h == 0 else S.r2s
+        for i in range(4):
+            src, dst = ps[:, 512 * i:512 * i + half], T.ht[:, t0 + i:t0 + 4 * half:4]
+            if i % 2 == 0:
+                v.wait_ge(S["m%d" % (4 * h + i)], 1)
+                ts(dst, src, 0.0, 0.0625, A.max, A.mult)
+            else:
+                sc.wait_ge(S["m%d" % (4 * h + i)], 1)
+                sc.activation(dst, src, F.Relu, scale=0.0625).then_inc(rs, 1)
+        done()
+        v.wait_ge(rs, 2)
+        v.quantize_mx(T.hq[:, a:a + half], T.hqs[:, a:a + half], T.ht[:, t0:t0 + 4 * half]).then_inc(S.q1 if h == 0 else S.q2, 1)
+
+    expert(0)
+    to_near(T.hq, T.hqs, S.q1, S.q1, S.rsp, T.hb, T.hbs, 2)
+    sy.wait_ge(S.q1, 1)
+    sy.dma_start(cod(T.hb, 2 + own, 2 + own + CAPP), cod(T.hq, own, own + CAPP)).then_inc(S.so, 16)
+    sy.dma_start(T.hbs[:, 2 + own:2 + own + CAPP], T.hqs[:, own:own + CAPP]).then_inc(S.so, 16)
+    expert(1)
+    to_handers(T.hq, T.hqs, S.q2, S.q2, S.hret, T.hr, T.hrs)
+
+    for k in range(2):
+        for d in range(2):
+            op(v.tensor_copy(T.d2[:, k, :, d, :], T.rz[:, 3 + k, :]))
+    op(v.memset(T.l0[:], 0))
+    done()
+    op(v.transpose(T.d2t[:], T.d2[:]))
+    done()
+    v.tensor_copy(T.oh2[:], T.d2t[:, 0:512:32]).then_inc(S.soh, 1)
+    v.wait_ge(S.suv, 32)
+    v.quantize_mx(T.uq[:], T.us[:], T.ut[:]).then_inc(S.suq, 1)
+    v.wait_ge(S.suq, 1)
+    v.tensor_copy(w32(T.up, 0, 128), w32(T.uq, 0, 128).indirect(T.l0[:])).then_inc(S.sup, 1)
+    sc.wait_ge(S.suq, 1)
+    sc.activation(T.ups[:, 0:128], T.us[:, 0:128].indirect(T.l0[:]), F.Copy).then_inc(S.sups, 1)
+    v.quantize_mx(T.vq[:], T.vs[:], T.vt[:]).then_inc(S.svq, 1)
+    ts(T.ka[:], T.rz[:, 0, :], -6.0, 7.0, A.mult, A.add)
+    ts(T.kb[:], T.rz[:, 1, :], -7.0, None, A.mult)
+    ts(T.jr2[:], T.jr[:], 128.0, None, A.add)
+    tt(T.pa[:], T.rz[:, 0, :], T.jr[:], A.mult)
+    op(v.memset(T.cap[:], 1.0 * CAPR))
+    op(v.memset(T.cc[:, 0:1], 0.0))
+    op(v.memset(T.g4[:], 0.0))
+    ts(T.cw[:, 0:1], T.ff[:, 3:4], 2.0, 1.0, A.mult, A.add)
+    ts(T.cw[:, 1:2], T.ff[:, 3:4], -1.0, 99.0, A.mult, A.add)
+    done()
+    tt(T.kk[:], T.ka[:], T.kb[:], A.add)
+    tt(T.pb[:], T.rz[:, 1, :], T.jr2[:], A.mult)
+    done()
+    tt(T.pp[:], T.pa[:], T.pb[:], A.add)
+    done()
+
+    for q in (v, sc):
+        q.wait_ge(S.sz, 96)
+        q.wait_ge(S.soh, 1)
+        q.wait_ge(S.so, 32)
+        q.wait_ge(S.rsp, near_in)
+        q.wait_ge(S.rcr, far_in)
+    v.tensor_copy(w32(T.hab, 1, 257), w32(T.hb, 0, 386).indirect(T.oh2[:])).then_inc(S.shab, 1)
+    sc.activation(T.habs[:, 1:257], T.hbs[:, 0:386].indirect(T.oh2[:]), F.Copy).then_inc(S.shabs, 1)
+    te.wait_ge(S.sup, 1)
+    te.wait_ge(S.sups, 1)
+    te.wait_ge(S.shab, 1)
+    te.wait_ge(S.shabs, 1)
+    te.matmul_mx(T.psa[:, 0:258], T.up[:, 0:128], T.ups[:, 0:128], T.hab[:, 0:258], T.habs[:, 0:258], True, True).then_inc(S.mq, 1)
+    v.wait_ge(S.mq, 1)
+    tt(T.qb[:], T.psa[:, 129:257], T.rz[:, 2, :], A.add)
+    done()
+    tt(T.ge[:], T.psa[:, 1:129], T.qb[:], A.is_ge)
+    done()
+    v.tensor_tensor(T.ww[:], T.ge[:], T.kk[:], A.is_equal).then_inc(S.sww, 1)
+    v.wait_ge(S.sww, 1)
+    op(v.tensor_tensor_scan(T.cc[:, 1:129], T.ww[:], T.cap[:], 0.0, A.add, A.min))
+    done()
+    v.tensor_tensor(T.fl[:], T.cc[:, 1:129], T.cc[:, 0:128], A.subtract).then_inc(S.sfl, 1)
+    v.wait_ge(S.sfl, 1)
+    for d in range(2):
+        tt(T.vv[:, :, d, :], T.fl[:], T.pp[:], A.mult)
+    done()
+    op(v.transpose(T.vt2[:], T.vv[:]))
+    done()
+    v.tensor_reduce(T.oz[:], T.vt2[:, :, 0:8], X, A.max).then_inc(S.soz, 1)
+    sc.wait_ge(S.sww, 1)
+    sc.activation(T.g1[:], T.ww[:], F.Copy, scale=T.cw[:, 1:2]).then_inc(S.sgg, 1)
+    sc.wait_ge(S.sfl, 1)
+    sc.activation(T.g2[:], T.fl[:], F.Copy, scale=T.cw[:, 0:1]).then_inc(S.sgg, 1)
+    v.wait_ge(S.soz, 1)
+    sc.wait_ge(S.soz, 1)
+    v.tensor_copy(w32(T.zq, 0, 128), w32(T.hab, 0, 258).indirect(T.oz[:])).then_inc(S.szq, 1)
+    sc.activation(T.zs[:, 0:128], T.habs[:, 0:258].indirect(T.oz[:]), F.Copy).then_inc(S.szs, 1)
+    te.wait_ge(S.svq, 1)
+    te.wait_ge(S.szq, 1)
+    te.wait_ge(S.szs, 1)
+    te.matmul_mx(T.psa[:, 512:640], T.vq[:, 0:128], T.vs[:, 0:128], T.zq[:, 0:128], T.zs[:, 0:128], True, True).then_inc(S.my, 1)
+    sc.wait_ge(S.my, 1)
+    sc.activation(T.yb[:], T.psa[:, 512:640], F.Copy).then_inc(S.sy, 1)
+    sc.wait_ge(S.sy, 1)
+    sc.dma_start(T.y[:], T.yb[:]).then_inc(S.fin, 16)
+    v.wait_ge(S.sgg, 2)
+    tt(T.g3[:], T.g1[:], T.g2[:], A.add)
+    done()
+    op(v.transpose(T.g3t[:], T.g3[:]))
+    done()
+    op(v.tensor_reduce(T.g4[:, 0:4], T.g3t[:, :, 0:8], X, A.add))
+    done()
+    ts(T.g5[:], T.g4[:], -100.0, None, A.add)
+    done()
+    v.transpose(T.g6[:], T.g5[:]).then_inc(S.swn, 1)
+    sy.wait_ge(S.szq, 1)
+    sy.dma_start(T.oc[:, 0:512], cod(T.zq, 0, 128)).then_inc(S.fin, 16)
+    sy.wait_ge(S.szs, 1)
+    for k in range(4):
+        sy.dma_start(T.osc[4 * k:4 * k + 4, 0:128], T.zs[32 * k:32 * k + 4, 0:128]).then_inc(S.fin, 16)
+    sy.wait_ge(S.swn, 1)
+    sy.dma_start(T.wn[0:1, 0:128], T.g6[0:4, 0:32]).then_inc(S.fin, 16)
+    sy.wait_ge(S.fin, 112)
+    g.wait_ge(S.loc, nl[0])

@@ -4,56 +4,35 @@ from concourse.mybir import dt, AluOpType as A, AxisListType, ActivationFunction
 C8, PL, BF, FP, I32, U16 = "float8_e4m3fn_x4", "uint8", "bfloat16", "float32", "int32", "uint16"
 CAPP, CAPR, DUMP = 48, 32, 32
 BIG = 2.0 ** 98
-SCRATCH = {
-    "xt": ("sbuf", [128, 520], BF), "xq": ("sbuf", [128, 130], C8), "xs": ("sbuf", [128, 130], PL),
-    "rtt": ("sbuf", [128, 512], BF), "rq": ("sbuf", [128, 128], C8), "rs": ("sbuf", [128, 128], PL),
-    "rp": ("sbuf", [128, 128], C8), "rps": ("sbuf", [128, 128], PL),
-    "wt": ("sbuf", [128, 2048], BF), "wq": ("sbuf", [128, 512], C8), "ws": ("sbuf", [128, 512], PL),
-    "ut": ("sbuf", [128, 512], BF), "uq": ("sbuf", [128, 128], C8), "us": ("sbuf", [128, 128], PL),
-    "up": ("sbuf", [128, 128], C8), "ups": ("sbuf", [128, 128], PL),
-    "vt": ("sbuf", [128, 512], BF), "vq": ("sbuf", [128, 128], C8), "vs": ("sbuf", [128, 128], PL),
-    "xg": ("sbuf", [128, 336], C8), "xgs": ("sbuf", [128, 336], PL),
-    "hx": ("sbuf", [128, 96], C8), "hxs": ("sbuf", [128, 96], PL),
-    "lx": ("sbuf", [128, 384], C8), "lxs": ("sbuf", [128, 384], PL),
-    "ht": ("sbuf", [128, 1536], BF), "hq": ("sbuf", [128, 384], C8), "hqs": ("sbuf", [128, 384], PL),
-    "hr": ("sbuf", [128, 96], C8), "hrs": ("sbuf", [128, 96], PL),
-    "hb": ("sbuf", [128, 386], C8), "hbs": ("sbuf", [128, 386], PL),
-    "hab": ("sbuf", [128, 258], C8), "habs": ("sbuf", [128, 258], PL),
-    "zq": ("sbuf", [128, 128], C8), "zs": ("sbuf", [128, 128], PL),
-    "yb": ("sbuf", [128, 128], FP),
-    "ip": ("sbuf", [128, 1], I32), "ii": ("sbuf", [128, 4], I32), "ff": ("sbuf", [128, 4], FP),
-    "r8": ("sbuf", [128, 8], FP), "jr": ("sbuf", [128, 128], FP), "jr2": ("sbuf", [128, 128], FP),
-    "q2": ("sbuf", [128, 32], FP), "e4": ("sbuf", [128, 4], FP), "ee": ("sbuf", [128, 4], FP),
-    "lp": ("sbuf", [128, 8], U16), "l0": ("sbuf", [128, 8], U16), "vals": ("sbuf", [128, 32], BF),
-    "th": ("sbuf", [128, 2, 8], FP), "kv": ("sbuf", [128, 32], FP), "kvt": ("sbuf", [128, 32], FP),
-    "kt": ("sbuf", [128, 8], FP), "sign": ("sbuf", [128, 64], FP), "ones": ("sbuf", [128, 128], FP),
-    "cap": ("sbuf", [128, 128], FP), "z32": ("sbuf", [128, 32], FP), "cw": ("sbuf", [128, 2], FP),
-    "dq": ("sbuf", [128, 2], FP),
-    "bs": ("sbuf", [128, 64], FP), "gt": ("sbuf", [128, 64], FP), "rk": ("sbuf", [128, 64], FP),
-    "nn": ("sbuf", [128, 128], BF), "nt": ("sbuf", [128, 128], BF), "cs": ("sbuf", [128, 128], FP),
-    "ct": ("sbuf", [128, 32], FP), "un": ("sbuf", [128, 8], FP), "oh": ("sbuf", [128, 2, 8], FP),
-    "p1": ("sbuf", [128, 2, 8], FP), "pr": ("sbuf", [128, 2, 9], FP),
-    "of": ("sbuf", [128, 2], U16), "win": ("sbuf", [128, 416], BF), "dd": ("sbuf", [128, 8, 3, 2, 16], BF),
-    "ot": ("sbuf", [128, 768], BF), "t1": ("sbuf", [128, 24], FP), "t2": ("sbuf", [128, 24], FP),
-    "od": ("sbuf", [128, 26], U16),
-    "vm": ("sbuf", [128, 2], FP), "tk": ("sbuf", [128, 2], FP), "po": ("sbuf", [128, 2], FP),
-    "mm": ("sbuf", [128, 3], FP), "zst": ("sbuf", [128, 5, 32], FP), "zt": ("sbuf", [128, 5, 32], FP),
-    "rz": ("sbuf", [128, 5, 128], FP), "ka": ("sbuf", [128, 128], FP),
-    "kb": ("sbuf", [128, 128], FP), "kk": ("sbuf", [128, 128], FP), "pa": ("sbuf", [128, 128], FP),
-    "pb": ("sbuf", [128, 128], FP), "pp": ("sbuf", [128, 128], FP), "d2": ("sbuf", [128, 2, 8, 2, 16], FP),
-    "d2t": ("sbuf", [128, 512], FP), "oh2": ("sbuf", [128, 16], U16),
-    "qb": ("sbuf", [128, 128], FP), "ge": ("sbuf", [128, 128], FP), "ww": ("sbuf", [128, 128], FP),
-    "cc": ("sbuf", [128, 132], FP), "fl": ("sbuf", [128, 128], FP), "vv": ("sbuf", [128, 8, 2, 16], BF),
-    "vt2": ("sbuf", [128, 8, 32], BF), "oz": ("sbuf", [128, 8], U16),
-    "g1": ("sbuf", [128, 128], FP), "g2": ("sbuf", [128, 128], FP), "g3": ("sbuf", [128, 128], BF),
-    "g3t": ("sbuf", [128, 4, 32], BF), "g4": ("sbuf", [128, 32], FP), "g5": ("sbuf", [128, 32], FP),
-    "g6": ("sbuf", [128, 32], FP),
-    "psa": ("psum", [128, 2048], "float32"), "psb": ("psum", [128, 2048], "float32"),
+SHAPES = {
+    C8: "xq130 rq128 rp128 wq512 uq128 up128 vq128 xg336 hx96 lx384 hq384 hr96 hb386 hab258 zq128",
+    PL: "xs130 rs128 rps128 ws512 us128 ups128 vs128 xgs336 hxs96 lxs384 hqs384 hrs96 hbs386 habs258 zs128",
+    BF: "xt520 rtt512 wt2048 ut512 vt512 ht1536 vals32 nn128 nt128 win416 ot768 gg128",
+    FP: "yb128 ya258 ff4 jr128 jra128 e_4 ee4 q_32 kv32 kvt32 kt8 sign64 ones128 cap128 z32 cw3 dq2 bs64 gt64 rk64 cs128 ct32 "
+        "un8 ta24 tb24 vm2 tk2 po2 mm3 ka128 kb128 kk128 pa128 pb128 pp128 dt512 qb128 ge128 ww128 cc132 fl128 g_128 h_128 wa32 wb32",
+    I32: "ip1 ii4",
+    U16: "lp8 lo8 of2 od26 oh16 oz8",
 }
-SEMAPHORES = ["v", "gi", "srt", "sx", "sw", "suv", "srq", "srp", "srps", "sxq", "mS", "sod1", "sod2", "sg1", "sg1s", "sg2", "sg2s",
-              "sg3", "sg3s", "loc", "hd", "hret", "dsp", "dcr", "rsp", "rcr", "suq", "sup", "sups", "swq", "sz", "so",
-              "r1s", "r2s", "q1", "q2", "soh", "shab", "shabs", "mq", "sww", "sfl", "sgg", "soz", "szq", "szs",
-              "my", "sy", "swn", "fin", "svq"] + ["m%d" % i for i in range(8)]
+
+
+def _split(s):
+    k = len(s.rstrip("0123456789"))
+    return s[:k], int(s[k:])
+
+
+SCRATCH = {
+    "th": ("sbuf", [128, 2, 8], FP), "oh2": ("sbuf", [128, 2, 8], FP), "p1": ("sbuf", [128, 2, 8], FP),
+    "pr": ("sbuf", [128, 2, 9], FP), "dd": ("sbuf", [128, 8, 3, 2, 16], BF),
+    "zst": ("sbuf", [128, 5, 32], FP), "zt": ("sbuf", [128, 5, 32], FP), "rz": ("sbuf", [128, 5, 128], FP),
+    "d2": ("sbuf", [128, 2, 8, 2, 16], FP), "vv": ("sbuf", [128, 8, 2, 16], BF), "vvt": ("sbuf", [128, 8, 32], BF),
+    "ggt": ("sbuf", [128, 4, 32], BF),
+    "psa": ("psum", [128, 2048], FP), "psb": ("psum", [128, 2048], FP),
+}
+for _t, _s in SHAPES.items():
+    for _w in _s.split():
+        SCRATCH[_split(_w)[0]] = ("sbuf", [128, _split(_w)[1]], _t)
+SEMAPHORES = ("v gi gl gh srt sx sw suv srq srp srps sxq mS sod1 sod2 sg1 sg1s sg2 sg2s sg3 sg3s loc hd hret dsp dcr rsp rcr suq sup sups "
+              "swq sz so r1s r2s q1 q2 soh shab shabs mq sww sfl sgg soz szq szs my sya sy swn fin svq m0 m1 m2 m3 m4 m5 m6 m7").split()
 
 
 def rank_program(g, core, T, topo):
@@ -75,7 +54,7 @@ def rank_program(g, core, T, topo):
     def handers(r):
         c = ranks[r]
         can = [h for h in topo.cores_of(c) if h != c and all(topo.may_write(h, ranks[q]) for q in order(r)[0])]
-        return sorted(can, key=lambda h: (topo.die(h) == topo.die(c), h))[:2]
+        return sorted(can, key=lambda h: (topo.die(h) == topo.die(c), h))[:4]
 
     def send(dst_core, es, sem, src, dst):
         rid, pid = topo.addr(dst_core, core)
@@ -83,6 +62,9 @@ def rank_program(g, core, T, topo):
 
     def cod(t, a, b):
         return t[:, a:b].bitcast(u8)
+
+    def run(planes, c, p, a, b):
+        return p[:, a:b] if planes else cod(c, a, b)
 
     def w32(t, a, b):
         return t[:, a:b].bitcast(u32)
@@ -96,6 +78,13 @@ def rank_program(g, core, T, topo):
             return es[k:2 * k], es[3 * k:]
         return es[2 * k:], es[0:2 * k]
 
+    def inside(r, back, planes, i):
+        es, off = topo.engines(ranks[r], handers(r)[i]), topo.engines(ranks[r], ranks[order(r)[1][0]])
+        if back:
+            es = [e for e in es if (e in off) == planes]
+        k = len(es) // 2
+        return es[k * i:k * i + k]
+
     rank = T.rank_of(core)
 
     if rank is None:
@@ -104,28 +93,24 @@ def rank_program(g, core, T, topo):
             return
         r = mine[0]
         i = handers(r).index(core)
-        to = order(r)[0][2 * i:2 * i + 2]
+        planes, i = i >= 2, i % 2
         n = 0
-        for sem_in, sem_out, bc, bp, dc, dp, base in ((S.hd, S.dcr, T.hx, T.hxs, T.lx, T.lxs, 0), (S.hret, S.rcr, T.hr, T.hrs, T.hb, T.hbs, 2)):
-            g.wait_ge(sem_in, 16)
-            for planes in (False, True):
-                t = []
-                for k, q in enumerate(to):
-                    es = topo.engines(core, ranks[q])[4 * k:4 * k + 4]
-                    a, b = base + CAPP * pos(q, r), CAPP * k
-                    if planes:
-                        t.append(send(ranks[q], es, sem_out, bp[:, b:b + CAPP], dp[:, a:a + CAPP]))
-                    else:
-                        t.append(send(ranks[q], es, sem_out, cod(bc, b, b + CAPP), cod(dc, a, a + CAPP)))
-                    n += len(es)
-                g.remote_dma_fused(t, local_sem=S.loc)
+        for back, sem_in, sem_out, bc, bp, dc, dp in ((False, S.hd, S.dcr, T.hx, T.hxs, T.lx, T.lxs), (True, S.hret, S.rcr, T.hr, T.hrs, T.hb, T.hbs)):
+            g.wait_ge(sem_in, len(inside(r, back, planes, i)))
+            t = []
+            for k, q in enumerate(order(r)[0][2 * i:2 * i + 2]):
+                es = topo.engines(core, ranks[q])[4 * k:4 * k + 4]
+                a = 2 * back + CAPP * pos(q, r)
+                t.append(send(ranks[q], es, sem_out, run(planes, bc, bp, CAPP * k, CAPP * k + CAPP), run(planes, dc, dp, a, a + CAPP)))
+                n += len(es)
+            g.remote_dma_fused(t, local_sem=S.loc)
         g.wait_ge(S.loc, n)
         return
 
     far, near = order(rank)
     blocks = far + near + [rank]
     half, own = CAPP * len(far), CAPP * (N - 1)
-    near_in = sum(len(direct(q, order(q)[1].index(rank))[0]) + len(direct(q, order(q)[1].index(rank))[1]) for q in near)
+    near_in = sum(len(e) for q in near for e in direct(q, order(q)[1].index(rank)))
     far_in = 8 * len(far)
     v, sc, te, sy = g.vector, g.scalar, g.tensor, g.sync
     n, nl = [0], [0]
@@ -143,31 +128,23 @@ def rank_program(g, core, T, topo):
     def ts(*a):
         op(v.tensor_scalar(*a))
 
-    def fused(t, k):
-        g.remote_dma_fused(t, local_sem=S.loc)
-        nl[0] += k
+    def fused(t, sem):
+        g.wait_ge(sem, 1)
+        g.remote_dma_fused([send(*a) for a in t], local_sem=S.loc)
+        nl[0] += sum(len(a[1]) for a in t)
 
-    def to_handers(bc, bp, sem_c, sem_p, sem, dc, dp):
-        es = topo.engines(core, handers(rank)[0])
+    def to_handers(back, bc, bp, sem_c, sem_p, sem, dc, dp):
+        for planes in (False, True):
+            fused([(handers(rank)[2 * planes + i], inside(rank, back, planes, i), sem, run(planes, bc, bp, 96 * i, 96 * i + 96), run(planes, dc, dp, 0, 96))
+                   for i in range(2)], sem_p if planes else sem_c)
+
+    def to_near(base, bc, bp, sem_c, sem_p, sem, dc, dp):
         for planes in (False, True):
             t = []
-            for i, h in enumerate(handers(rank)):
-                a, e = 2 * CAPP * i, es[8 * i:8 * i + 8]
-                t.append(send(h, e, sem, bp[:, a:a + 96], dp[:]) if planes else send(h, e, sem, cod(bc, a, a + 96), cod(dc, 0, 96)))
-            g.wait_ge(sem_p if planes else sem_c, 1)
-            fused(t, 16)
-
-    def to_near(bc, bp, sem_c, sem_p, sem, dc, dp, base):
-        for planes in (False, True):
-            t, k = [], 0
             for i, q in enumerate(near):
-                e = direct(rank, i)[planes]
                 a, b = half + CAPP * i, base + CAPP * pos(q, rank)
-                t.append(send(ranks[q], e, sem, bp[:, a:a + CAPP], dp[:, b:b + CAPP]) if planes else
-                         send(ranks[q], e, sem, cod(bc, a, a + CAPP), cod(dc, b, b + CAPP)))
-                k += len(e)
-            g.wait_ge(sem_p if planes else sem_c, 1)
-            fused(t, k)
+                t.append((ranks[q], direct(rank, i)[planes], sem, run(planes, bc, bp, a, a + CAPP), run(planes, dc, dp, b, b + CAPP)))
+            fused(t, sem_p if planes else sem_c)
 
     sc.dma_start(T.rtt[:, 0:32], T.rt[:, 0:32]).then_inc(S.srt, 16)
     sy.dma_start(T.xt[:, 8:520], T.x[:]).then_inc(S.sx, 16)
@@ -175,18 +152,25 @@ def rank_program(g, core, T, topo):
     sy.dma_start(T.ut[:], T.u[:]).then_inc(S.suv, 16)
     sy.dma_start(T.vt[:], T.v[:]).then_inc(S.suv, 16)
 
-    loose = dict(allow_small_or_imprecise_dtypes=True)
+    def iota(out, pattern, base, sem):
+        g.iota(out, pattern, base, 0, allow_small_or_imprecise_dtypes=True).then_inc(sem, 1)
     g.iota(T.ip[:], [[0, 1]], 0, 1).then_inc(S.gi, 1)
-    g.iota(T.e4[:], [[2, 4]], 0, 0, **loose).then_inc(S.gi, 1)
-    g.iota(T.r8[:], [[1, 8]], 0, 0, **loose).then_inc(S.gi, 1)
-    g.iota(T.q2[:], [[0, 2], [1, 16]], 2, 0, **loose).then_inc(S.gi, 1)
-    g.iota(T.jr[:], [[1, 128]], 1, 0, **loose).then_inc(S.gi, 1)
+    iota(T.e_[:], [[2, 4]], 0, S.gi)
+    iota(T.q_[:], [[0, 2], [1, 16]], 2, S.gi)
+    iota(T.th[:, 0, :], [[-1, 8]], 0, S.gl)
+    iota(T.th[:, 1, :], [[-1, 8]], 1, S.gl)
+    iota(T.nn[:], [[0, 128]], 0, S.gl)
+    iota(T.ones[:], [[0, 128]], 1, S.gl)
+    iota(T.win[:], [[0, 416]], 0, S.gl)
+    iota(T.jr[:], [[1, 128]], 1, S.gh)
+    iota(T.jra[:], [[1, 128]], 129, S.gh)
+    iota(T.cap[:], [[0, 128]], CAPR, S.gh)
 
     op(v.memset(T.rtt[:, 32:512], 0.0))
     op(v.memset(T.xt[:, 0:8], 0.0))
-    op(v.memset(T.sign[:], 1.0))
     op(v.memset(T.kv[:], 0.0))
-    v.wait_ge(S.gi, 5)
+    op(v.memset(T.sign[:], 1.0))
+    v.wait_ge(S.gi, 3)
     ts(T.ii[:, 0:1], T.ip[:], 7, None, A.bitwise_and)
     ts(T.ii[:, 1:2], T.ip[:], 3, 1, A.logical_shift_right, A.bitwise_and)
     ts(T.ii[:, 2:3], T.ip[:], 112, None, A.bitwise_and)
@@ -194,26 +178,22 @@ def rank_program(g, core, T, topo):
     done()
     op(v.tensor_copy(T.ff[:], T.ii[:]))
     op(v.memset(T.sign[:, 0:64:9], -1.0))
-    for i, e in enumerate(blocks):
-        op(v.memset(T.kv[:, e:e + 1], 1.0 * DUMP + CAPP * i - 1))
     done()
-    ts(T.ee[:], T.e4[:], T.ff[:, 1:2], None, A.add)
-    op(v.memset(T.sign[:, 0:64:8], 0.0))
-    op(v.transpose(T.kvt[:], T.kv[:]))
-    ts(T.kt[:], T.kv[:, 0:8], 1.0 * CAPP, None, A.add)
-    ts(T.vals[:], T.q2[:], T.ff[:, 2:3], None, A.add)
-    ts(T.th[:, 0, :], T.r8[:], -1.0, None, A.mult)
-    ts(T.th[:, 1, :], T.r8[:], -1.0, 1.0, A.mult, A.add)
+    ts(T.ee[:], T.e_[:], T.ff[:, 1:2], None, A.add)
     ts(T.dq[:, 0:1], T.ff[:, 1:2], 16.0, None, A.mult)
     ts(T.dq[:, 1:2], T.ff[:, 1:2], 16.0, 1.0, A.mult, A.add)
+    op(v.memset(T.sign[:, 0:64:8], 0.0))
     done()
     ts(T.lp[:, 0:4], T.ee[:], T.ff[:, 0:1], None, A.max)
     ts(T.lp[:, 4:8], T.ee[:], T.ff[:, 0:1], None, A.min)
+    ts(T.vals[:], T.q_[:], T.ff[:, 2:3], None, A.add)
     for k in range(2):
         ts(T.pr[:, k, 8:9], T.ff[:, 0:1], 2.0, T.dq[:, k:k + 1], A.mult, A.add)
-    op(v.memset(T.ones[:], 1.0))
-    op(v.memset(T.nn[:], 0.0))
+    for i, e in enumerate(blocks):
+        op(v.memset(T.kv[:, e:e + 1], 1.0 * DUMP + CAPP * i - 1))
     done()
+    op(v.transpose(T.kvt[:], T.kv[:]))
+    ts(T.kt[:], T.kv[:, 0:8], 1.0 * CAPP, None, A.add)
 
     v.wait_ge(S.srt, 16)
     v.quantize_mx(T.rq[:], T.rs[:], T.rtt[:]).then_inc(S.srq, 1)
@@ -227,7 +207,6 @@ def rank_program(g, core, T, topo):
     te.wait_ge(S.srps, 1)
     te.wait_ge(S.sxq, 1)
     te.matmul_mx(T.psb[:, 0:128], T.xq[:, 2:130], T.xs[:, 2:130], T.rp[:, 0:128], T.rps[:, 0:128], True, True).then_inc(S.mS, 1)
-    op(v.memset(T.win[:], 0.0))
     sy.wait_ge(S.sxq, 1)
     for q_, s_, a in ((T.hb, T.hbs, 0), (T.hab, T.habs, 0), (T.hab, T.habs, 256)):
         sy.dma_start(cod(q_, a, a + 2), cod(T.xq, 0, 2)).then_inc(S.sz, 16)
@@ -239,6 +218,7 @@ def rank_program(g, core, T, topo):
     tt(T.gt[:], T.psb[:, 0:64], T.bs[:], A.is_gt)
     done()
     op(v.tensor_tensor_scan(T.rk[:], T.sign[:], T.gt[:], 0.0, A.mult, A.add))
+    v.wait_ge(S.gl, 5)
     done()
     for b in range(4):
         for d in range(b + 1, 4):
@@ -246,16 +226,16 @@ def rank_program(g, core, T, topo):
     tt(T.nn[:, 96:104], T.rk[:, 7:64:8], T.th[:, 1, :], A.is_le)
     done()
     op(v.transpose(T.nt[:], T.nn[:]))
-    tt(T.oh[:, 0, :], T.rk[:, 7:64:8], T.th[:, 0, :], A.is_equal)
-    tt(T.oh[:, 1, :], T.rk[:, 7:64:8], T.th[:, 1, :], A.is_equal)
     done()
     op(v.tensor_tensor_scan(T.cs[:], T.ones[:], T.nt[:], T.kvt[:, 0:1], A.mult, A.add))
+    tt(T.oh2[:, 0, :], T.rk[:, 7:64:8], T.th[:, 0, :], A.is_equal)
+    tt(T.oh2[:, 1, :], T.rk[:, 7:64:8], T.th[:, 1, :], A.is_equal)
     done()
     op(v.transpose(T.ct[:], T.cs[:, 96:128]))
     done()
     tt(T.un[:], T.ct[:, 0:8], T.kt[:], A.is_le)
     for k in range(2):
-        tt(T.p1[:, k, :], T.oh[:, k, :], T.ct[:, 0:8], A.mult)
+        tt(T.p1[:, k, :], T.oh2[:, k, :], T.ct[:, 0:8], A.mult)
     done()
     for k in range(2):
         tt(T.pr[:, k, 0:8], T.p1[:, k, :], T.un[:], A.mult)
@@ -272,52 +252,48 @@ def rank_program(g, core, T, topo):
         op(v.transpose(T.ot[:, 96 * a:96 * b], T.dd[:, a:b]))
         done()
         c = slice(3 * a, 3 * b)
-        tt(T.t1[:, c], T.ot[:, 96 * a:96 * b:32], T.ot[:, 96 * a + 16:96 * b:32], A.add)
+        tt(T.ta[:, c], T.ot[:, 96 * a:96 * b:32], T.ot[:, 96 * a + 16:96 * b:32], A.add)
         done()
-        tt(T.t2[0:64, c], T.t1[0:64, c], T.t1[64:128, c], A.add)
-        tt(T.t2[64:128, c], T.t1[64:128, c], T.t1[0:64, c], A.add)
+        tt(T.tb[0:64, c], T.ta[0:64, c], T.ta[64:128, c], A.add)
+        tt(T.tb[64:128, c], T.ta[64:128, c], T.ta[0:64, c], A.add)
         done()
-        sem, k = (S.sod1, 0) if h == 0 else (S.sod2, 0)
-        for lo, hi, to in ([(0, 12, 0)] if h == 0 else [(12, 21, 12), (21, 24, 22)]):
+        sem, k = S.sod2 if h else S.sod1, 0
+        for lo, hi, to in ([(12, 21, 12), (21, 24, 22)] if h else [(0, 12, 0)]):
             for p, o in ((0, 32), (32, 0), (64, 96), (96, 64)):
-                v.tensor_tensor(T.od[p:p + 32, to:to + hi - lo], T.t2[p:p + 32, lo:hi], T.t2[o:o + 32, lo:hi], A.add).then_inc(sem, 1)
+                v.tensor_tensor(T.od[p:p + 32, to:to + hi - lo], T.tb[p:p + 32, lo:hi], T.tb[o:o + 32, lo:hi], A.add).then_inc(sem, 1)
                 k += 1
         v.wait_ge(sem, k)
         sc.wait_ge(sem, k)
-        if h == 0:
-            v.tensor_copy(w32(T.xg, 0, half), w32(T.xq, 0, 130).indirect(T.od[:, 0:12])).then_inc(S.sg1, 1)
-            sc.activation(T.xgs[:, 0:half], T.xs[:, 0:130].indirect(T.od[:, 0:12]), F.Copy).then_inc(S.sg1s, 1)
-        else:
-            v.tensor_copy(w32(T.xg, half, own), w32(T.xq, 0, 130).indirect(T.od[:, 12:21])).then_inc(S.sg2, 1)
-            sc.activation(T.xgs[:, half:own], T.xs[:, 0:130].indirect(T.od[:, 12:21]), F.Copy).then_inc(S.sg2s, 1)
-            v.tensor_copy(w32(T.lx, own, own + CAPP), w32(T.xq, 0, 130).indirect(T.od[:, 22:25])).then_inc(S.sg3, 1)
-            sc.activation(T.lxs[:, own:own + CAPP], T.xs[:, 0:130].indirect(T.od[:, 22:25]), F.Copy).then_inc(S.sg3s, 1)
+        for a, b, c, d, q_, s_, s1, s2 in ([(half, own, 12, 21, T.xg, T.xgs, S.sg2, S.sg2s), (own, own + CAPP, 22, 25, T.lx, T.lxs, S.sg3, S.sg3s)]
+                                           if h else [(0, half, 0, 12, T.xg, T.xgs, S.sg1, S.sg1s)]):
+            v.tensor_copy(w32(q_, a, b), w32(T.xq, 0, 130).indirect(T.od[:, c:d])).then_inc(s1, 1)
+            sc.activation(s_[:, a:b], T.xs[:, 0:130].indirect(T.od[:, c:d]), F.Copy).then_inc(s2, 1)
 
-    to_handers(T.xg, T.xgs, S.sg1, S.sg1s, S.hd, T.hx, T.hxs)
-    to_near(T.xg, T.xgs, S.sg2, S.sg2s, S.dsp, T.lx, T.lxs, 0)
+    to_handers(False, T.xg, T.xgs, S.sg1, S.sg1s, S.hd, T.hx, T.hxs)
+    to_near(0, T.xg, T.xgs, S.sg2, S.sg2s, S.dsp, T.lx, T.lxs)
 
     v.wait_ge(S.sw, 16)
     for i in range(4):
         v.quantize_mx(T.wq[:, 128 * i:128 * i + 128], T.ws[:, 128 * i:128 * i + 128], T.wt[:, 512 * i:512 * i + 512]).then_inc(S.swq, 1)
 
     op(v.memset(T.zst[:], 0.0))
-    op(v.memset(T.z32[:], 0.0))
+    op(v.memset(T.z[:], 0.0))
     op(v.tensor_reduce(T.vm[:], T.pr[:, :, 0:8], X, A.max))
     done()
     for k in range(2):
-        tt(T.zst[:, k, 0:8], T.oh[:, k, :], T.un[:], A.mult)
+        tt(T.zst[:, k, 0:8], T.oh2[:, k, :], T.un[:], A.mult)
     ts(T.tk[:], T.vm[:], 0.0, None, A.is_gt)
     ts(T.po[:], T.vm[:], 2.0 - DUMP, 0.0, A.add, A.max)
     done()
     tt(T.mm[:, 0:1], T.tk[:, 0:1], T.tk[:, 1:2], A.mult)
     for k in range(2):
-        ts(T.zst[:, 3 + k, :], T.z32[:], T.po[:, k:k + 1], None, A.add)
+        ts(T.zst[:, 3 + k, :], T.z[:], T.po[:, k:k + 1], None, A.add)
     done()
     ts(T.mm[:, 1:2], T.tk[:, 0:1], 2.0, T.mm[:, 0:1], A.mult, A.subtract)
     done()
     ts(T.mm[:, 2:3], T.mm[:, 1:2], -1.0, -BIG, A.add, A.mult)
     done()
-    ts(T.zst[:, 2, :], T.z32[:], T.mm[:, 2:3], None, A.add)
+    ts(T.zst[:, 2, :], T.z[:], T.mm[:, 2:3], None, A.add)
     done()
     op(v.transpose(T.zt[:], T.zst[:]))
     done()
@@ -331,66 +307,64 @@ def rank_program(g, core, T, topo):
 
     def expert(h):
         a = half * (1 - h)
-        ps, t0 = (T.psa, 0) if h == 0 else (T.psb, 4 * half)
-        if h == 0:
+        ps, t0, rs = (T.psb, 4 * half, S.r2s) if h else (T.psa, 0, S.r1s)
+        if h:
+            te.wait_ge(S.dcr, far_in)
+        else:
             te.wait_ge(S.swq, 4)
             te.wait_ge(S.sg3, 1)
             te.wait_ge(S.sg3s, 1)
             te.wait_ge(S.dsp, near_in)
-        else:
-            te.wait_ge(S.dcr, far_in)
         for i in range(4):
             te.matmul_mx(ps[:, 512 * i:512 * i + half], T.wq[:, 128 * i:128 * i + 128], T.ws[:, 128 * i:128 * i + 128],
                          T.lx[:, a:a + half], T.lxs[:, a:a + half], True, True).then_inc(S["m%d" % (4 * h + i)], 1)
-        rs = S.r1s if h == 0 else S.r2s
         for i in range(4):
             src, dst = ps[:, 512 * i:512 * i + half], T.ht[:, t0 + i:t0 + 4 * half:4]
-            if i % 2 == 0:
-                v.wait_ge(S["m%d" % (4 * h + i)], 1)
-                ts(dst, src, 0.0, 0.0625, A.max, A.mult)
-            else:
-                sc.wait_ge(S["m%d" % (4 * h + i)], 1)
+            q = sc if i % 2 else v
+            q.wait_ge(S["m%d" % (4 * h + i)], 1)
+            if i % 2:
                 sc.activation(dst, src, F.Relu, scale=0.0625).then_inc(rs, 1)
+            else:
+                ts(dst, src, 0.0, 0.0625, A.max, A.mult)
         done()
         v.wait_ge(rs, 2)
-        v.quantize_mx(T.hq[:, a:a + half], T.hqs[:, a:a + half], T.ht[:, t0:t0 + 4 * half]).then_inc(S.q1 if h == 0 else S.q2, 1)
+        v.quantize_mx(T.hq[:, a:a + half], T.hqs[:, a:a + half], T.ht[:, t0:t0 + 4 * half]).then_inc(S.q2 if h else S.q1, 1)
 
     expert(0)
-    to_near(T.hq, T.hqs, S.q1, S.q1, S.rsp, T.hb, T.hbs, 2)
+    to_near(2, T.hq, T.hqs, S.q1, S.q1, S.rsp, T.hb, T.hbs)
     sy.wait_ge(S.q1, 1)
     sy.dma_start(cod(T.hb, 2 + own, 2 + own + CAPP), cod(T.hq, own, own + CAPP)).then_inc(S.so, 16)
     sy.dma_start(T.hbs[:, 2 + own:2 + own + CAPP], T.hqs[:, own:own + CAPP]).then_inc(S.so, 16)
     expert(1)
-    to_handers(T.hq, T.hqs, S.q2, S.q2, S.hret, T.hr, T.hrs)
+    to_handers(True, T.hq, T.hqs, S.q2, S.q2, S.hret, T.hr, T.hrs)
 
     for k in range(2):
         for d in range(2):
             op(v.tensor_copy(T.d2[:, k, :, d, :], T.rz[:, 3 + k, :]))
-    op(v.memset(T.l0[:], 0))
+    op(v.memset(T.lo[:], 0))
     done()
-    op(v.transpose(T.d2t[:], T.d2[:]))
+    op(v.transpose(T.dt[:], T.d2[:]))
     done()
-    v.tensor_copy(T.oh2[:], T.d2t[:, 0:512:32]).then_inc(S.soh, 1)
+    v.tensor_copy(T.oh[:], T.dt[:, 0:512:32]).then_inc(S.soh, 1)
     v.wait_ge(S.suv, 32)
     v.quantize_mx(T.uq[:], T.us[:], T.ut[:]).then_inc(S.suq, 1)
     v.wait_ge(S.suq, 1)
-    v.tensor_copy(w32(T.up, 0, 128), w32(T.uq, 0, 128).indirect(T.l0[:])).then_inc(S.sup, 1)
+    v.tensor_copy(w32(T.up, 0, 128), w32(T.uq, 0, 128).indirect(T.lo[:])).then_inc(S.sup, 1)
     sc.wait_ge(S.suq, 1)
-    sc.activation(T.ups[:, 0:128], T.us[:, 0:128].indirect(T.l0[:]), F.Copy).then_inc(S.sups, 1)
+    sc.activation(T.ups[:, 0:128], T.us[:, 0:128].indirect(T.lo[:]), F.Copy).then_inc(S.sups, 1)
     v.quantize_mx(T.vq[:], T.vs[:], T.vt[:]).then_inc(S.svq, 1)
+    v.wait_ge(S.gh, 3)
     ts(T.ka[:], T.rz[:, 0, :], -6.0, 7.0, A.mult, A.add)
     ts(T.kb[:], T.rz[:, 1, :], -7.0, None, A.mult)
-    ts(T.jr2[:], T.jr[:], 128.0, None, A.add)
     tt(T.pa[:], T.rz[:, 0, :], T.jr[:], A.mult)
-    op(v.memset(T.cap[:], 1.0 * CAPR))
+    tt(T.pb[:], T.rz[:, 1, :], T.jra[:], A.mult)
     op(v.memset(T.cc[:, 0:1], 0.0))
-    op(v.memset(T.g4[:], 0.0))
+    op(v.memset(T.wa[:], 0.0))
     ts(T.cw[:, 0:1], T.ff[:, 3:4], 2.0, 1.0, A.mult, A.add)
     ts(T.cw[:, 1:2], T.ff[:, 3:4], -1.0, 99.0, A.mult, A.add)
+    ts(T.cw[:, 2:3], T.ff[:, 3:4], 31.0, -100.0, A.is_equal, A.mult)
     done()
     tt(T.kk[:], T.ka[:], T.kb[:], A.add)
-    tt(T.pb[:], T.rz[:, 1, :], T.jr2[:], A.mult)
-    done()
     tt(T.pp[:], T.pa[:], T.pb[:], A.add)
     done()
 
@@ -400,13 +374,12 @@ def rank_program(g, core, T, topo):
         q.wait_ge(S.so, 32)
         q.wait_ge(S.rsp, near_in)
         q.wait_ge(S.rcr, far_in)
-    v.tensor_copy(w32(T.hab, 1, 257), w32(T.hb, 0, 386).indirect(T.oh2[:])).then_inc(S.shab, 1)
-    sc.activation(T.habs[:, 1:257], T.hbs[:, 0:386].indirect(T.oh2[:]), F.Copy).then_inc(S.shabs, 1)
-    te.wait_ge(S.sup, 1)
-    te.wait_ge(S.sups, 1)
-    te.wait_ge(S.shab, 1)
-    te.wait_ge(S.shabs, 1)
+    v.tensor_copy(w32(T.hab, 1, 257), w32(T.hb, 0, 386).indirect(T.oh[:])).then_inc(S.shab, 1)
+    sc.activation(T.habs[:, 1:257], T.hbs[:, 0:386].indirect(T.oh[:]), F.Copy).then_inc(S.shabs, 1)
+    for s in (S.sup, S.sups, S.svq, S.shab, S.shabs):
+        te.wait_ge(s, 1)
     te.matmul_mx(T.psa[:, 0:258], T.up[:, 0:128], T.ups[:, 0:128], T.hab[:, 0:258], T.habs[:, 0:258], True, True).then_inc(S.mq, 1)
+    te.matmul_mx(T.psa[:, 512:770], T.vq[:, 0:128], T.vs[:, 0:128], T.hab[:, 0:258], T.habs[:, 0:258], True, True).then_inc(S.my, 1)
     v.wait_ge(S.mq, 1)
     tt(T.qb[:], T.psa[:, 129:257], T.rz[:, 2, :], A.add)
     done()
@@ -421,41 +394,38 @@ def rank_program(g, core, T, topo):
     for d in range(2):
         tt(T.vv[:, :, d, :], T.fl[:], T.pp[:], A.mult)
     done()
-    op(v.transpose(T.vt2[:], T.vv[:]))
+    op(v.transpose(T.vvt[:], T.vv[:]))
     done()
-    v.tensor_reduce(T.oz[:], T.vt2[:, :, 0:8], X, A.max).then_inc(S.soz, 1)
-    sc.wait_ge(S.sww, 1)
-    sc.activation(T.g1[:], T.ww[:], F.Copy, scale=T.cw[:, 1:2]).then_inc(S.sgg, 1)
-    sc.wait_ge(S.sfl, 1)
-    sc.activation(T.g2[:], T.fl[:], F.Copy, scale=T.cw[:, 0:1]).then_inc(S.sgg, 1)
-    v.wait_ge(S.soz, 1)
-    sc.wait_ge(S.soz, 1)
-    v.tensor_copy(w32(T.zq, 0, 128), w32(T.hab, 0, 258).indirect(T.oz[:])).then_inc(S.szq, 1)
-    sc.activation(T.zs[:, 0:128], T.habs[:, 0:258].indirect(T.oz[:]), F.Copy).then_inc(S.szs, 1)
-    te.wait_ge(S.svq, 1)
-    te.wait_ge(S.szq, 1)
-    te.wait_ge(S.szs, 1)
-    te.matmul_mx(T.psa[:, 512:640], T.vq[:, 0:128], T.vs[:, 0:128], T.zq[:, 0:128], T.zs[:, 0:128], True, True).then_inc(S.my, 1)
+    v.tensor_reduce(T.oz[:], T.vvt[:, :, 0:8], X, A.max).then_inc(S.soz, 1)
     sc.wait_ge(S.my, 1)
-    sc.activation(T.yb[:], T.psa[:, 512:640], F.Copy).then_inc(S.sy, 1)
-    sc.wait_ge(S.sy, 1)
-    sc.dma_start(T.y[:], T.yb[:]).then_inc(S.fin, 16)
+    sc.activation(T.ya[:], T.psa[:, 512:770], F.Copy).then_inc(S.sya, 1)
+    sc.wait_ge(S.sww, 1)
+    sc.activation(T.g_[:], T.ww[:], F.Identity, scale=T.cw[:, 1:2], bias=T.cw[:, 2:3]).then_inc(S.sgg, 1)
+    sc.wait_ge(S.sfl, 1)
+    sc.activation(T.h_[:], T.fl[:], F.Copy, scale=T.cw[:, 0:1]).then_inc(S.sgg, 1)
+    v.wait_ge(S.soz, 1)
+    v.tensor_copy(w32(T.zq, 0, 128), w32(T.hab, 0, 258).indirect(T.oz[:])).then_inc(S.szq, 1)
+    sc.wait_ge(S.sya, 1)
+    sc.wait_ge(S.soz, 1)
+    sc.activation(T.yb[:], T.ya[:, 0:258].indirect(T.oz[:]), F.Copy).then_inc(S.sy, 1)
+    sc.activation(T.zs[:, 0:128], T.habs[:, 0:258].indirect(T.oz[:]), F.Copy).then_inc(S.szs, 1)
     v.wait_ge(S.sgg, 2)
-    tt(T.g3[:], T.g1[:], T.g2[:], A.add)
+    tt(T.gg[:], T.g_[:], T.h_[:], A.add)
     done()
-    op(v.transpose(T.g3t[:], T.g3[:]))
+    op(v.transpose(T.ggt[:], T.gg[:]))
     done()
-    op(v.tensor_reduce(T.g4[:, 0:4], T.g3t[:, :, 0:8], X, A.add))
+    op(v.tensor_reduce(T.wa[:, 0:4], T.ggt[:], X, A.add))
     done()
-    ts(T.g5[:], T.g4[:], -100.0, None, A.add)
-    done()
-    v.transpose(T.g6[:], T.g5[:]).then_inc(S.swn, 1)
+    v.transpose(T.wb[:], T.wa[:]).then_inc(S.swn, 1)
     sy.wait_ge(S.szq, 1)
     sy.dma_start(T.oc[:, 0:512], cod(T.zq, 0, 128)).then_inc(S.fin, 16)
-    sy.wait_ge(S.szs, 1)
+    sy.wait_ge(S.sy, 1)
+    sy.dma_start(T.y[:], T.yb[:]).then_inc(S.fin, 16)
     for k in range(4):
-        sy.dma_start(T.osc[4 * k:4 * k + 4, 0:128], T.zs[32 * k:32 * k + 4, 0:128]).then_inc(S.fin, 16)
+        q = sc if k % 2 else sy
+        q.wait_ge(S.szs, 1)
+        q.dma_start(T.osc[4 * k:4 * k + 4, 0:128], T.zs[32 * k:32 * k + 4, 0:128]).then_inc(S.fin, 16)
     sy.wait_ge(S.swn, 1)
-    sy.dma_start(T.wn[0:1, 0:128], T.g6[0:4, 0:32]).then_inc(S.fin, 16)
+    sy.dma_start(T.wn[0:1, 0:128], T.wb[0:4, 0:32]).then_inc(S.fin, 16)
     sy.wait_ge(S.fin, 112)
     g.wait_ge(S.loc, nl[0])

@@ -7,9 +7,9 @@ BIG = 2.0 ** 98
 SHAPES = {
     C8: "xq130 rq128 rp128 wq512 uq128 up128 vq128 xg336 hx96 lx384 hq384 hr96 hb386 hab258 zq128",
     PL: "xs130 rs128 rps128 ws512 us128 ups128 vs128 xgs336 hxs96 lxs384 hqs384 hrs96 hbs386 habs258 zs128",
-    BF: "xt520 rtt512 wt2048 ut512 vt512 ht1536 vals32 nn128 nt128 win416 ot768 gg128",
-    FP: "yb128 ya258 ff4 jr128 jra128 e_4 ee4 q_32 kv32 kvt32 kt8 sign64 ones128 cap128 z32 cw3 dq2 bs64 gt64 rk64 cs128 ct32 "
-        "un8 ta24 tb24 vm2 tk2 po2 mm3 ka128 kb128 kk128 pa128 pb128 pp128 dt512 qb128 ge128 ww128 cc132 fl128 g_128 h_128 wa32 wb32",
+    BF: "xt520 rtt512 wt2048 ut512 vt512 ht1536 vals32 nn128 nt128 win416 ot768 cap128 ge128 kk128 ww128 cc136",
+    FP: "yb128 ya258 ff4 jr128 jra128 e_4 ee4 q_32 kv32 kvt32 kt8 c2_8 sign64 z32 cw3 dq2 bs64 gt64 rk64 cs128 ct32 "
+        "un8 ta24 tb24 vm2 tk2 po2 mm3 ka128 kb128 pa128 pb128 dt512 qb128 wa32 wb32",
     I32: "ip1 ii4",
     U16: "lp8 lo8 of2 od26 oh16 oz8",
 }
@@ -21,18 +21,20 @@ def _split(s):
 
 
 SCRATCH = {
-    "th": ("sbuf", [128, 2, 8], FP), "oh2": ("sbuf", [128, 2, 8], FP), "p1": ("sbuf", [128, 2, 8], FP),
+    "th": ("sbuf", [128, 2, 8], FP), "oh2": ("sbuf", [128, 2, 8], FP),
     "pr": ("sbuf", [128, 2, 9], FP), "dd": ("sbuf", [128, 8, 3, 2, 16], BF),
     "zst": ("sbuf", [128, 5, 32], FP), "zt": ("sbuf", [128, 5, 32], FP), "rz": ("sbuf", [128, 5, 128], FP),
     "d2": ("sbuf", [128, 2, 8, 2, 16], FP), "vv": ("sbuf", [128, 8, 2, 16], BF), "vvt": ("sbuf", [128, 8, 32], BF),
-    "ggt": ("sbuf", [128, 4, 32], BF),
+    "pp": ("sbuf", [128, 8, 2, 16], FP), "ppt": ("sbuf", [128, 8, 32], FP), "vz": ("sbuf", [128, 8, 8], FP),
+    "gh": ("sbuf", [128, 4, 2, 32], BF), "ght": ("sbuf", [128, 4, 2, 32], BF), "gg": ("sbuf", [128, 4, 8], FP),
     "psa": ("psum", [128, 2048], FP), "psb": ("psum", [128, 2048], FP),
 }
 for _t, _s in SHAPES.items():
     for _w in _s.split():
         SCRATCH[_split(_w)[0]] = ("sbuf", [128, _split(_w)[1]], _t)
-SEMAPHORES = ("v gi gl gh srt sx sw suv srq srp srps sxq mS sod1 sod2 sg1 sg1s sg2 sg2s sg3 sg3s loc hd hret dsp dcr rsp rcr suq sup sups "
-              "swq sz so r1s r2s q1 q2 soh shab shabs mq sww sfl sgg soz szq szs my sya sy swn fin svq m0 m1 m2 m3 m4 m5 m6 m7").split()
+SEMAPHORES = ("v gi ge1 gq gth gk gw gh sff sdq scn srt sx sw su0 sv0 srq srp srps sxq mS sod1 sod2 sg1 sg1s sg2 sg2s sg3 sg3s loc hd hret dsp dcr rsp rcr "
+              "suq sup sups swq sz so r1s r2s q1 q2 soh sba sbas sbb sbbs mqa mqb sww sfl sgg soz szq szs my sya sy swn fin svq srz srd "
+              "m0 m1 m2 m3 m4 m5 m6 m7").split()
 
 
 def rank_program(g, core, T, topo):
@@ -54,7 +56,8 @@ def rank_program(g, core, T, topo):
     def handers(r):
         c = ranks[r]
         can = [h for h in topo.cores_of(c) if h != c and all(topo.may_write(h, ranks[q]) for q in order(r)[0])]
-        return sorted(can, key=lambda h: (topo.die(h) == topo.die(c), h))[:4]
+        can = sorted(can, key=lambda h: (topo.die(h) == topo.die(c), h))[:4]
+        return can + [h for h in topo.cores_of(c) if h != c and topo.die(h) == topo.die(c) and h not in can][:1]
 
     def send(dst_core, es, sem, src, dst):
         rid, pid = topo.addr(dst_core, core)
@@ -72,18 +75,18 @@ def rank_program(g, core, T, topo):
     def direct(r, i):
         es = topo.engines(ranks[r], ranks[order(r)[1][i]])
         k = len(es) // 4
-        if i == 0:
-            return es[0:k], es[2 * k:3 * k]
-        if i == 1:
-            return es[k:2 * k], es[3 * k:]
-        return es[2 * k:], es[0:2 * k]
+        return es[k * i:k * i + k] if i < 2 else es[2 * k:]
 
-    def inside(r, back, planes, i):
-        es, off = topo.engines(ranks[r], handers(r)[i]), topo.engines(ranks[r], ranks[order(r)[1][0]])
-        if back:
-            es = [e for e in es if (e in off) == planes]
-        k = len(es) // 2
-        return es[k * i:k * i + k]
+    def upper(r):
+        es = topo.engines(ranks[r], ranks[order(r)[1][0]])
+        return es[len(es) // 2:]
+
+    def inside(r, k):
+        es, off = topo.engines(ranks[r], handers(r)[k]), topo.engines(ranks[r], ranks[order(r)[1][0]])
+        if k == 4:
+            return [e for e in es if e not in off]
+        m = len(es) // 2
+        return es[m * (k % 2):m * (k % 2) + m]
 
     rank = T.rank_of(core)
 
@@ -92,13 +95,15 @@ def rank_program(g, core, T, topo):
         if not mine or core not in handers(mine[0]):
             return
         r = mine[0]
+        far, near = order(r)
         i = handers(r).index(core)
-        planes, i = i >= 2, i % 2
+        planes = i >= 2
+        to, s_out, s_back = (near[1:], S.dsp, S.rsp) if i == 4 else (far[2 * (i % 2):2 * (i % 2) + 2], S.dcr, S.rcr)
         n = 0
-        for back, sem_in, sem_out, bc, bp, dc, dp in ((False, S.hd, S.dcr, T.hx, T.hxs, T.lx, T.lxs), (True, S.hret, S.rcr, T.hr, T.hrs, T.hb, T.hbs)):
-            g.wait_ge(sem_in, len(inside(r, back, planes, i)))
+        for back, sem_in, sem_out, bc, bp, dc, dp in ((False, S.hd, s_out, T.hx, T.hxs, T.lx, T.lxs), (True, S.hret, s_back, T.hr, T.hrs, T.hb, T.hbs)):
+            g.wait_ge(sem_in, len(inside(r, i)))
             t = []
-            for k, q in enumerate(order(r)[0][2 * i:2 * i + 2]):
+            for k, q in enumerate(to):
                 es = topo.engines(core, ranks[q])[4 * k:4 * k + 4]
                 a = 2 * back + CAPP * pos(q, r)
                 t.append(send(ranks[q], es, sem_out, run(planes, bc, bp, CAPP * k, CAPP * k + CAPP), run(planes, dc, dp, a, a + CAPP)))
@@ -110,7 +115,7 @@ def rank_program(g, core, T, topo):
     far, near = order(rank)
     blocks = far + near + [rank]
     half, own = CAPP * len(far), CAPP * (N - 1)
-    near_in = sum(len(e) for q in near for e in direct(q, order(q)[1].index(rank)))
+    near_in = sum(len(direct(q, order(q)[1].index(rank))) + 4 for q in near)
     far_in = 8 * len(far)
     v, sc, te, sy = g.vector, g.scalar, g.tensor, g.sync
     n, nl = [0], [0]
@@ -133,74 +138,84 @@ def rank_program(g, core, T, topo):
         g.remote_dma_fused([send(*a) for a in t], local_sem=S.loc)
         nl[0] += sum(len(a[1]) for a in t)
 
-    def to_handers(back, bc, bp, sem_c, sem_p, sem, dc, dp):
+    def to_far(bc, bp, sem_c, sem_p, sem, dc, dp):
         for planes in (False, True):
-            fused([(handers(rank)[2 * planes + i], inside(rank, back, planes, i), sem, run(planes, bc, bp, 96 * i, 96 * i + 96), run(planes, dc, dp, 0, 96))
+            fused([(handers(rank)[2 * planes + i], inside(rank, 2 * planes + i), sem, run(planes, bc, bp, 96 * i, 96 * i + 96), run(planes, dc, dp, 0, 96))
                    for i in range(2)], sem_p if planes else sem_c)
 
-    def to_near(base, bc, bp, sem_c, sem_p, sem, dc, dp):
-        for planes in (False, True):
-            t = []
-            for i, q in enumerate(near):
-                a, b = half + CAPP * i, base + CAPP * pos(q, rank)
-                t.append((ranks[q], direct(rank, i)[planes], sem, run(planes, bc, bp, a, a + CAPP), run(planes, dc, dp, b, b + CAPP)))
-            fused(t, sem_p if planes else sem_c)
+    def to_near(base, bc, bp, sem_c, sem_p, sem, dc, dp, sem_h, hp):
+        t = []
+        for i, q in enumerate(near):
+            a, b = half + CAPP * i, base + CAPP * pos(q, rank)
+            t.append((ranks[q], direct(rank, i), sem, cod(bc, a, a + CAPP), cod(dc, b, b + CAPP)))
+        fused(t, sem_c)
+        fused([(handers(rank)[4], inside(rank, 4), sem_h, bp[:, half + CAPP:half + 3 * CAPP], hp[:, 0:96])], sem_p)
+        b = base + CAPP * pos(near[0], rank)
+        fused([(ranks[near[0]], upper(rank), sem, bp[:, half:half + CAPP], dp[:, b:b + CAPP])], sem_p)
 
     sc.dma_start(T.rtt[:, 0:32], T.rt[:, 0:32]).then_inc(S.srt, 16)
     sy.dma_start(T.xt[:, 8:520], T.x[:]).then_inc(S.sx, 16)
     sc.dma_start(T.wt[:], T.w[:]).then_inc(S.sw, 16)
-    sy.dma_start(T.ut[:], T.u[:]).then_inc(S.suv, 16)
-    sy.dma_start(T.vt[:], T.v[:]).then_inc(S.suv, 16)
+    sy.dma_start(T.ut[:, 0:32], T.u[:, 0:32]).then_inc(S.su0, 16)
 
     def iota(out, pattern, base, sem):
         g.iota(out, pattern, base, 0, allow_small_or_imprecise_dtypes=True).then_inc(sem, 1)
     g.iota(T.ip[:], [[0, 1]], 0, 1).then_inc(S.gi, 1)
-    iota(T.e_[:], [[2, 4]], 0, S.gi)
-    iota(T.q_[:], [[0, 2], [1, 16]], 2, S.gi)
-    iota(T.th[:, 0, :], [[-1, 8]], 0, S.gl)
-    iota(T.th[:, 1, :], [[-1, 8]], 1, S.gl)
-    iota(T.nn[:], [[0, 128]], 0, S.gl)
-    iota(T.ones[:], [[0, 128]], 1, S.gl)
-    iota(T.win[:], [[0, 416]], 0, S.gl)
-    iota(T.jr[:], [[1, 128]], 1, S.gh)
-    iota(T.jra[:], [[1, 128]], 129, S.gh)
+    iota(T.e_[:], [[2, 4]], 0, S.ge1)
+    i, nk = 0, 1
+    while i < N:
+        m = 1
+        while i + m < N and blocks[i + m] == blocks[i] + 2 * m:
+            m += 1
+        iota(T.kv[:, blocks[i]:blocks[i] + 2 * m - 1:2], [[CAPP, m]], DUMP + CAPP * i - 1, S.gk)
+        i, nk = i + m, nk + 1
+    iota(T.kv[:, N:32], [[0, 32 - N]], 0, S.gk)
+    iota(T.th[:, 1, :], [[-1, 8]], 1, S.gth)
+    iota(T.th[:, 0, :], [[-1, 8]], 0, S.gth)
+    iota(T.q_[:], [[0, 2], [1, 16]], 2, S.gq)
+    iota(T.win[:], [[0, 416]], 0, S.gw)
+    iota(T.jr[:], [[1, 128]], 2, S.gh)
+    iota(T.jra[:], [[1, 128]], 130, S.gh)
     iota(T.cap[:], [[0, 128]], CAPR, S.gh)
 
     op(v.memset(T.rtt[:, 32:512], 0.0))
     op(v.memset(T.xt[:, 0:8], 0.0))
-    op(v.memset(T.kv[:], 0.0))
     op(v.memset(T.sign[:], 1.0))
-    v.wait_ge(S.gi, 3)
+    v.wait_ge(S.gi, 1)
     ts(T.ii[:, 0:1], T.ip[:], 7, None, A.bitwise_and)
     ts(T.ii[:, 1:2], T.ip[:], 3, 1, A.logical_shift_right, A.bitwise_and)
     ts(T.ii[:, 2:3], T.ip[:], 112, None, A.bitwise_and)
     ts(T.ii[:, 3:4], T.ip[:], 31, None, A.bitwise_and)
     done()
-    op(v.tensor_copy(T.ff[:], T.ii[:]))
+    v.tensor_copy(T.ff[:], T.ii[:]).then_inc(S.sff, 1)
     op(v.memset(T.sign[:, 0:64:9], -1.0))
+    v.wait_ge(S.sff, 1)
+    v.wait_ge(S.ge1, 1)
     done()
     ts(T.ee[:], T.e_[:], T.ff[:, 1:2], None, A.add)
-    ts(T.dq[:, 0:1], T.ff[:, 1:2], 16.0, None, A.mult)
-    ts(T.dq[:, 1:2], T.ff[:, 1:2], 16.0, 1.0, A.mult, A.add)
     op(v.memset(T.sign[:, 0:64:8], 0.0))
     done()
     ts(T.lp[:, 0:4], T.ee[:], T.ff[:, 0:1], None, A.max)
     ts(T.lp[:, 4:8], T.ee[:], T.ff[:, 0:1], None, A.min)
-    ts(T.vals[:], T.q_[:], T.ff[:, 2:3], None, A.add)
-    for k in range(2):
-        ts(T.pr[:, k, 8:9], T.ff[:, 0:1], 2.0, T.dq[:, k:k + 1], A.mult, A.add)
-    for i, e in enumerate(blocks):
-        op(v.memset(T.kv[:, e:e + 1], 1.0 * DUMP + CAPP * i - 1))
     done()
-    op(v.transpose(T.kvt[:], T.kv[:]))
-    ts(T.kt[:], T.kv[:, 0:8], 1.0 * CAPP, None, A.add)
+    sc.wait_ge(S.sff, 1)
+    sc.activation(T.dq[:, 0:1], T.ff[:, 1:2], F.Copy, scale=16.0).then_inc(S.sdq, 1)
+    sc.activation(T.dq[:, 1:2], T.ff[:, 1:2], F.Copy, scale=16.0, bias=1.0).then_inc(S.sdq, 1)
+    sc.wait_ge(S.sdq, 2)
+    for k in range(2):
+        sc.activation(T.pr[:, k, 8:9], T.ff[:, 0:1], F.Identity, scale=2.0, bias=T.dq[:, k:k + 1]).then_inc(S.scn, 1)
 
     v.wait_ge(S.srt, 16)
     v.quantize_mx(T.rq[:], T.rs[:], T.rtt[:]).then_inc(S.srq, 1)
     v.wait_ge(S.srq, 1)
     v.tensor_copy(w32(T.rp, 0, 128), w32(T.rq, 0, 128).indirect(T.lp[:])).then_inc(S.srp, 1)
     sc.wait_ge(S.srq, 1)
+    sc.wait_ge(S.v, n[0])
     sc.activation(T.rps[:, 0:128], T.rs[:, 0:128].indirect(T.lp[:]), F.Copy).then_inc(S.srps, 1)
+    sc.wait_ge(S.gq, 1)
+    sc.activation(T.vals[:], T.q_[:], F.Identity, bias=T.ff[:, 2:3]).then_inc(S.scn, 1)
+    sc.wait_ge(S.gk, nk)
+    sc.activation(T.kt[:], T.kv[:, 0:8], F.Copy, bias=1.0 * CAPP).then_inc(S.scn, 1)
     v.wait_ge(S.sx, 16)
     v.quantize_mx(T.xq[:], T.xs[:], T.xt[:]).then_inc(S.sxq, 1)
     te.wait_ge(S.srp, 1)
@@ -208,9 +223,12 @@ def rank_program(g, core, T, topo):
     te.wait_ge(S.sxq, 1)
     te.matmul_mx(T.psb[:, 0:128], T.xq[:, 2:130], T.xs[:, 2:130], T.rp[:, 0:128], T.rps[:, 0:128], True, True).then_inc(S.mS, 1)
     sy.wait_ge(S.sxq, 1)
-    for q_, s_, a in ((T.hb, T.hbs, 0), (T.hab, T.habs, 0), (T.hab, T.habs, 256)):
-        sy.dma_start(cod(q_, a, a + 2), cod(T.xq, 0, 2)).then_inc(S.sz, 16)
-        sy.dma_start(s_[:, a:a + 2], T.xs[:, 0:2]).then_inc(S.sz, 16)
+    for q_, s_ in ((T.hb, T.hbs), (T.hab, T.habs)):
+        sy.dma_start(cod(q_, 0, 2), cod(T.xq, 0, 2)).then_inc(S.sz, 16)
+        sy.dma_start(s_[:, 0:2], T.xs[:, 0:2]).then_inc(S.sz, 16)
+    op(v.memset(T.nn[:], 0.0))
+    v.wait_ge(S.gk, nk)
+    op(v.transpose(T.kvt[:], T.kv[:]))
 
     v.wait_ge(S.mS, 1)
     op(v.tensor_copy(T.bs[:], T.psb[:, 64:128]))
@@ -218,29 +236,29 @@ def rank_program(g, core, T, topo):
     tt(T.gt[:], T.psb[:, 0:64], T.bs[:], A.is_gt)
     done()
     op(v.tensor_tensor_scan(T.rk[:], T.sign[:], T.gt[:], 0.0, A.mult, A.add))
-    v.wait_ge(S.gl, 5)
+    v.wait_ge(S.gth, 2)
     done()
-    for b in range(4):
-        for d in range(b + 1, 4):
-            tt(T.nn[32 * d:32 * d + 32, 32 * b:32 * b + 8], T.rk[32 * b:32 * b + 32, 7:64:8], T.th[32 * b:32 * b + 32, 1, :], A.is_le)
-    tt(T.nn[:, 96:104], T.rk[:, 7:64:8], T.th[:, 1, :], A.is_le)
+    for d, b, p, c in ((64, 0, 64, 0), (32, 0, 32, 0), (64, 32, 32, 32), (96, 0, 32, 32), (96, 64, 32, 64), (0, 0, 128, 96)):
+        tt(T.nn[d:d + p, c:c + 8], T.rk[b:b + p, 7:64:8], T.th[b:b + p, 1, :], A.is_le)
     done()
     op(v.transpose(T.nt[:], T.nn[:]))
     done()
-    op(v.tensor_tensor_scan(T.cs[:], T.ones[:], T.nt[:], T.kvt[:, 0:1], A.mult, A.add))
+    op(v.tensor_tensor_scan(T.cs[:], T.nt[:], T.nt[:], T.kvt[:, 0:1], A.add, A.max))
     tt(T.oh2[:, 0, :], T.rk[:, 7:64:8], T.th[:, 0, :], A.is_equal)
     tt(T.oh2[:, 1, :], T.rk[:, 7:64:8], T.th[:, 1, :], A.is_equal)
     done()
     op(v.transpose(T.ct[:], T.cs[:, 96:128]))
+    v.wait_ge(S.scn, 4)
     done()
     tt(T.un[:], T.ct[:, 0:8], T.kt[:], A.is_le)
-    for k in range(2):
-        tt(T.p1[:, k, :], T.oh2[:, k, :], T.ct[:, 0:8], A.mult)
+    done()
+    tt(T.c2_[:], T.un[:], T.ct[:, 0:8], A.mult)
     done()
     for k in range(2):
-        tt(T.pr[:, k, 0:8], T.p1[:, k, :], T.un[:], A.mult)
+        tt(T.pr[:, k, 0:8], T.oh2[:, k, :], T.c2_[:], A.mult)
     done()
     op(v.tensor_reduce(T.of[:], T.pr[:], X, A.max))
+    v.wait_ge(S.gw, 1)
     done()
     op(v.tensor_copy(T.win[:].indirect(T.of[:]), T.vals[:]))
     done()
@@ -255,26 +273,26 @@ def rank_program(g, core, T, topo):
         tt(T.ta[:, c], T.ot[:, 96 * a:96 * b:32], T.ot[:, 96 * a + 16:96 * b:32], A.add)
         done()
         tt(T.tb[0:64, c], T.ta[0:64, c], T.ta[64:128, c], A.add)
-        tt(T.tb[64:128, c], T.ta[64:128, c], T.ta[0:64, c], A.add)
         done()
         sem, k = S.sod2 if h else S.sod1, 0
-        for lo, hi, to in ([(12, 21, 12), (21, 24, 22)] if h else [(0, 12, 0)]):
-            for p, o in ((0, 32), (32, 0), (64, 96), (96, 64)):
-                v.tensor_tensor(T.od[p:p + 32, to:to + hi - lo], T.tb[p:p + 32, lo:hi], T.tb[o:o + 32, lo:hi], A.add).then_inc(sem, 1)
-                k += 1
+        runs = [(12, 21, 12), (21, 24, 22)] if h else [(0, 12, 0)]
+        for lo, hi, to in runs:
+            for p in (0, 32):
+                tt(T.od[p:p + 32, to:to + hi - lo], T.tb[0:32, lo:hi], T.tb[32:64, lo:hi], A.add)
+        done()
+        for lo, hi, to in runs:
+            v.tensor_copy(T.od[64:128, to:to + hi - lo], T.od[0:64, to:to + hi - lo]).then_inc(sem, 1)
+            k += 1
         v.wait_ge(sem, k)
         sc.wait_ge(sem, k)
+        sc.wait_ge(S.v, n[0])
         for a, b, c, d, q_, s_, s1, s2 in ([(half, own, 12, 21, T.xg, T.xgs, S.sg2, S.sg2s), (own, own + CAPP, 22, 25, T.lx, T.lxs, S.sg3, S.sg3s)]
                                            if h else [(0, half, 0, 12, T.xg, T.xgs, S.sg1, S.sg1s)]):
             v.tensor_copy(w32(q_, a, b), w32(T.xq, 0, 130).indirect(T.od[:, c:d])).then_inc(s1, 1)
             sc.activation(s_[:, a:b], T.xs[:, 0:130].indirect(T.od[:, c:d]), F.Copy).then_inc(s2, 1)
 
-    to_handers(False, T.xg, T.xgs, S.sg1, S.sg1s, S.hd, T.hx, T.hxs)
-    to_near(0, T.xg, T.xgs, S.sg2, S.sg2s, S.dsp, T.lx, T.lxs)
-
-    v.wait_ge(S.sw, 16)
-    for i in range(4):
-        v.quantize_mx(T.wq[:, 128 * i:128 * i + 128], T.ws[:, 128 * i:128 * i + 128], T.wt[:, 512 * i:512 * i + 512]).then_inc(S.swq, 1)
+    to_far(T.xg, T.xgs, S.sg1, S.sg1s, S.hd, T.hx, T.hxs)
+    to_near(0, T.xg, T.xgs, S.sg2, S.sg2s, S.dsp, T.lx, T.lxs, S.hd, T.hxs)
 
     op(v.memset(T.zst[:], 0.0))
     op(v.memset(T.z[:], 0.0))
@@ -298,20 +316,22 @@ def rank_program(g, core, T, topo):
     op(v.transpose(T.zt[:], T.zst[:]))
     done()
     for b in range(4):
-        op(v.tensor_copy(T.rz[0:32, :, 32 * b:32 * b + 32], T.zt[32 * b:32 * b + 32, :, :]))
-    done()
-    op(v.tensor_copy(T.rz[32:64, :, :], T.rz[0:32, :, :]))
-    done()
-    op(v.tensor_copy(T.rz[64:128, :, :], T.rz[0:64, :, :]))
-    done()
+        v.tensor_copy(T.rz[0:32, :, 32 * b:32 * b + 32], T.zt[32 * b:32 * b + 32, :, :]).then_inc(S.srz, 1)
+    sy.wait_ge(S.srz, 4)
+    for b in range(1, 4):
+        sy.dma_start(T.rz[32 * b:32 * b + 32, :, :], T.rz[0:32, :, :]).then_inc(S.srd, 16)
+
+    v.wait_ge(S.sw, 16)
+    for i in range(4):
+        v.quantize_mx(T.wq[:, 128 * i:128 * i + 128], T.ws[:, 128 * i:128 * i + 128], T.wt[:, 512 * i:512 * i + 512]).then_inc(S.swq, 1)
 
     def expert(h):
         a = half * (1 - h)
         ps, t0, rs = (T.psb, 4 * half, S.r2s) if h else (T.psa, 0, S.r1s)
         if h:
+            te.wait_ge(S.swq, 4)
             te.wait_ge(S.dcr, far_in)
         else:
-            te.wait_ge(S.swq, 4)
             te.wait_ge(S.sg3, 1)
             te.wait_ge(S.sg3s, 1)
             te.wait_ge(S.dsp, near_in)
@@ -330,14 +350,19 @@ def rank_program(g, core, T, topo):
         v.wait_ge(rs, 2)
         v.quantize_mx(T.hq[:, a:a + half], T.hqs[:, a:a + half], T.ht[:, t0:t0 + 4 * half]).then_inc(S.q2 if h else S.q1, 1)
 
+    expert(1)
+    to_far(T.hq, T.hqs, S.q2, S.q2, S.hret, T.hr, T.hrs)
     expert(0)
-    to_near(2, T.hq, T.hqs, S.q1, S.q1, S.rsp, T.hb, T.hbs)
+    to_near(2, T.hq, T.hqs, S.q1, S.q1, S.rsp, T.hb, T.hbs, S.hret, T.hrs)
+    sy.wait_ge(S.dsp, near_in)
+    sy.dma_start(T.vt[:], T.v[:]).then_inc(S.sv0, 16)
     sy.wait_ge(S.q1, 1)
     sy.dma_start(cod(T.hb, 2 + own, 2 + own + CAPP), cod(T.hq, own, own + CAPP)).then_inc(S.so, 16)
     sy.dma_start(T.hbs[:, 2 + own:2 + own + CAPP], T.hqs[:, own:own + CAPP]).then_inc(S.so, 16)
-    expert(1)
-    to_handers(True, T.hq, T.hqs, S.q2, S.q2, S.hret, T.hr, T.hrs)
 
+    v.wait_ge(S.srz, 4)
+    v.wait_ge(S.srd, 48)
+    op(v.memset(T.ut[:, 32:512], 0.0))
     for k in range(2):
         for d in range(2):
             op(v.tensor_copy(T.d2[:, k, :, d, :], T.rz[:, 3 + k, :]))
@@ -346,63 +371,74 @@ def rank_program(g, core, T, topo):
     op(v.transpose(T.dt[:], T.d2[:]))
     done()
     v.tensor_copy(T.oh[:], T.dt[:, 0:512:32]).then_inc(S.soh, 1)
-    v.wait_ge(S.suv, 32)
+    v.wait_ge(S.su0, 16)
     v.quantize_mx(T.uq[:], T.us[:], T.ut[:]).then_inc(S.suq, 1)
     v.wait_ge(S.suq, 1)
     v.tensor_copy(w32(T.up, 0, 128), w32(T.uq, 0, 128).indirect(T.lo[:])).then_inc(S.sup, 1)
     sc.wait_ge(S.suq, 1)
     sc.activation(T.ups[:, 0:128], T.us[:, 0:128].indirect(T.lo[:]), F.Copy).then_inc(S.sups, 1)
+    v.wait_ge(S.sv0, 16)
     v.quantize_mx(T.vq[:], T.vs[:], T.vt[:]).then_inc(S.svq, 1)
     v.wait_ge(S.gh, 3)
     ts(T.ka[:], T.rz[:, 0, :], -6.0, 7.0, A.mult, A.add)
     ts(T.kb[:], T.rz[:, 1, :], -7.0, None, A.mult)
     tt(T.pa[:], T.rz[:, 0, :], T.jr[:], A.mult)
     tt(T.pb[:], T.rz[:, 1, :], T.jra[:], A.mult)
-    op(v.memset(T.cc[:, 0:1], 0.0))
+    op(v.memset(T.cc[:, 0:8], 0.0))
     op(v.memset(T.wa[:], 0.0))
     ts(T.cw[:, 0:1], T.ff[:, 3:4], 2.0, 1.0, A.mult, A.add)
     ts(T.cw[:, 1:2], T.ff[:, 3:4], -1.0, 99.0, A.mult, A.add)
-    ts(T.cw[:, 2:3], T.ff[:, 3:4], 31.0, -100.0, A.is_equal, A.mult)
+    ts(T.cw[:, 2:3], T.ff[:, 3:4], 1.0 * (N - 1), -100.0, A.is_equal, A.mult)
     done()
     tt(T.kk[:], T.ka[:], T.kb[:], A.add)
-    tt(T.pp[:], T.pa[:], T.pb[:], A.add)
+    for d in range(2):
+        tt(T.pp[:, :, d, :], T.pa[:], T.pb[:], A.add)
+    done()
+    op(v.transpose(T.ppt[:], T.pp[:]))
     done()
 
     for q in (v, sc):
-        q.wait_ge(S.sz, 96)
+        q.wait_ge(S.sz, 64)
         q.wait_ge(S.soh, 1)
         q.wait_ge(S.so, 32)
         q.wait_ge(S.rsp, near_in)
         q.wait_ge(S.rcr, far_in)
-    v.tensor_copy(w32(T.hab, 1, 257), w32(T.hb, 0, 386).indirect(T.oh[:])).then_inc(S.shab, 1)
-    sc.activation(T.habs[:, 1:257], T.hbs[:, 0:386].indirect(T.oh[:]), F.Copy).then_inc(S.shabs, 1)
-    for s in (S.sup, S.sups, S.svq, S.shab, S.shabs):
+    for k, s1, s2 in ((1, S.sbb, S.sbbs), (0, S.sba, S.sbas)):
+        a = 2 + 128 * k
+        v.tensor_copy(w32(T.hab, a, a + 128), w32(T.hb, 0, 386).indirect(T.oh[:, 8 * k:8 * k + 8])).then_inc(s1, 1)
+        sc.activation(T.habs[:, a:a + 128], T.hbs[:, 0:386].indirect(T.oh[:, 8 * k:8 * k + 8]), F.Copy).then_inc(s2, 1)
+    for s in (S.sup, S.sups, S.svq, S.sbb, S.sbbs):
         te.wait_ge(s, 1)
-    te.matmul_mx(T.psa[:, 0:258], T.up[:, 0:128], T.ups[:, 0:128], T.hab[:, 0:258], T.habs[:, 0:258], True, True).then_inc(S.mq, 1)
-    te.matmul_mx(T.psa[:, 512:770], T.vq[:, 0:128], T.vs[:, 0:128], T.hab[:, 0:258], T.habs[:, 0:258], True, True).then_inc(S.my, 1)
-    v.wait_ge(S.mq, 1)
-    tt(T.qb[:], T.psa[:, 129:257], T.rz[:, 2, :], A.add)
+    te.matmul_mx(T.psa[:, 0:128], T.up[:, 0:128], T.ups[:, 0:128], T.hab[:, 130:258], T.habs[:, 130:258], True, True).then_inc(S.mqb, 1)
+    te.wait_ge(S.sba, 1)
+    te.wait_ge(S.sbas, 1)
+    te.matmul_mx(T.psa[:, 512:640], T.up[:, 0:128], T.ups[:, 0:128], T.hab[:, 2:130], T.habs[:, 2:130], True, True).then_inc(S.mqa, 1)
+    te.matmul_mx(T.psa[:, 1024:1282], T.vq[:, 0:128], T.vs[:, 0:128], T.hab[:, 0:258], T.habs[:, 0:258], True, True).then_inc(S.my, 1)
+    v.wait_ge(S.mqb, 1)
+    tt(T.qb[:], T.psa[:, 0:128], T.rz[:, 2, :], A.add)
+    v.wait_ge(S.mqa, 1)
     done()
-    tt(T.ge[:], T.psa[:, 1:129], T.qb[:], A.is_ge)
+    tt(T.ge[:], T.psa[:, 512:640], T.qb[:], A.is_ge)
     done()
     v.tensor_tensor(T.ww[:], T.ge[:], T.kk[:], A.is_equal).then_inc(S.sww, 1)
     v.wait_ge(S.sww, 1)
-    op(v.tensor_tensor_scan(T.cc[:, 1:129], T.ww[:], T.cap[:], 0.0, A.add, A.min))
+    op(v.tensor_tensor_scan(T.cc[:, 8:136], T.ww[:], T.cap[:], 0.0, A.add, A.min))
     done()
-    v.tensor_tensor(T.fl[:], T.cc[:, 1:129], T.cc[:, 0:128], A.subtract).then_inc(S.sfl, 1)
+    v.tensor_tensor(T.vv[:, :, 0, :], T.cc[:, 8:136], T.cc[:, 7:135], A.subtract).then_inc(S.sfl, 1)
     v.wait_ge(S.sfl, 1)
-    for d in range(2):
-        tt(T.vv[:, :, d, :], T.fl[:], T.pp[:], A.mult)
+    op(v.tensor_copy(T.vv[:, :, 1, :], T.vv[:, :, 0, :]))
     done()
     op(v.transpose(T.vvt[:], T.vv[:]))
     done()
-    v.tensor_reduce(T.oz[:], T.vvt[:, :, 0:8], X, A.max).then_inc(S.soz, 1)
+    tt(T.vz[:], T.vvt[:, :, 0:8], T.ppt[:, :, 0:8], A.mult)
+    done()
+    v.tensor_reduce(T.oz[:], T.vz[:], X, A.max).then_inc(S.soz, 1)
     sc.wait_ge(S.my, 1)
-    sc.activation(T.ya[:], T.psa[:, 512:770], F.Copy).then_inc(S.sya, 1)
+    sc.activation(T.ya[:], T.psa[:, 1024:1282], F.Copy).then_inc(S.sya, 1)
     sc.wait_ge(S.sww, 1)
-    sc.activation(T.g_[:], T.ww[:], F.Identity, scale=T.cw[:, 1:2], bias=T.cw[:, 2:3]).then_inc(S.sgg, 1)
+    sc.activation(T.gh[:, :, 0, :], T.ww[:], F.Identity, scale=T.cw[:, 1:2], bias=T.cw[:, 2:3]).then_inc(S.sgg, 1)
     sc.wait_ge(S.sfl, 1)
-    sc.activation(T.h_[:], T.fl[:], F.Copy, scale=T.cw[:, 0:1]).then_inc(S.sgg, 1)
+    sc.activation(T.gh[:, :, 1, :], T.vv[:, :, 0, :], F.Copy, scale=T.cw[:, 0:1]).then_inc(S.sgg, 1)
     v.wait_ge(S.soz, 1)
     v.tensor_copy(w32(T.zq, 0, 128), w32(T.hab, 0, 258).indirect(T.oz[:])).then_inc(S.szq, 1)
     sc.wait_ge(S.sya, 1)
@@ -410,11 +446,11 @@ def rank_program(g, core, T, topo):
     sc.activation(T.yb[:], T.ya[:, 0:258].indirect(T.oz[:]), F.Copy).then_inc(S.sy, 1)
     sc.activation(T.zs[:, 0:128], T.habs[:, 0:258].indirect(T.oz[:]), F.Copy).then_inc(S.szs, 1)
     v.wait_ge(S.sgg, 2)
-    tt(T.gg[:], T.g_[:], T.h_[:], A.add)
+    op(v.transpose(T.ght[:], T.gh[:]))
     done()
-    op(v.transpose(T.ggt[:], T.gg[:]))
+    tt(T.gg[:], T.ght[:, :, 0, 0:8], T.ght[:, :, 1, 0:8], A.add)
     done()
-    op(v.tensor_reduce(T.wa[:, 0:4], T.ggt[:], X, A.add))
+    op(v.tensor_reduce(T.wa[:, 0:4], T.gg[:], X, A.add))
     done()
     v.transpose(T.wb[:], T.wa[:]).then_inc(S.swn, 1)
     sy.wait_ge(S.szq, 1)

@@ -2,16 +2,16 @@ from concourse.bass import DstId, RemoteDMATransfer
 from concourse.mybir import dt, AluOpType as A, AxisListType, ActivationFunctionType as F
 
 C8, PL, BF, FP, I32, U16 = "float8_e4m3fn_x4", "uint8", "bfloat16", "float32", "int32", "uint16"
-CAPP, CAPR, DUMP = 48, 32, 32
+CAPP, CAPR, DUMP, TOK, ZC = 48, 32, 32, 128, 16
 BIG = 2.0 ** 98
 SHAPES = {
-    C8: "xq130 rq128 rp128 wq512 uq128 up128 vq128 xg336 hx96 lx384 hq384 hr96 hb386 hab258 zq128",
-    PL: "xs130 rs128 rps128 ws512 us128 ups128 vs128 xgs336 hxs96 lxs384 hqs384 hrs96 hbs386 habs258 zs128",
-    BF: "xt520 rtt512 wt2048 ut512 vt512 ht1536 vals32 nn128 nt128 win416 ot768 cap128 ge128 kk128 ww128 cc136",
-    FP: "yb128 ya258 ff4 jr128 jra128 e_4 ee4 q_32 kv32 kvt32 kt8 c2_8 sign64 z32 cw3 dq2 bs64 gt64 rk64 cs128 ct32 "
-        "un8 ta24 tb24 vm2 tk2 po2 mm3 ka128 kb128 pa128 pb128 dt512 qb128 wa32 wb32",
+    C8: "xq144 rq128 rp128 wq512 uq128 up128 vq128 xg336 he128 xe144 hx192 lx384 hq384 hr192 hb480 hab272 zq128",
+    PL: "xs144 rs128 rps128 ws512 us128 ups128 vs128 xgs336 hes128 xes144 hxs192 lxs384 hqs384 hrs192 hbs480 habs272 zs128",
+    BF: "xt576 rtt512 wt2048 ut512 vt512 ht1536 vals32 nn128 nt128 win416 ot768 cap128 ge128 kk128 ww128 cc136",
+    FP: "yb128 ya272 ff4 jr128 jra128 e_4 ee4 q_32 kv32 kvt32 kt8 c2_8 sign64 z32 cw3 cr1 dq2 bs64 gt64 rk64 cs128 ct32 "
+        "un8 ta24 tb24 vm2 tk2 mm1 ka128 kb128 pa128 pb128 dt512 qb128 wa32 wb32",
     I32: "ip1 ii4",
-    U16: "lp8 lo8 of2 od26 oh16 oz8",
+    U16: "lp8 lo8 of2 od26 oh16 oz8 le4",
 }
 
 
@@ -32,8 +32,8 @@ SCRATCH = {
 for _t, _s in SHAPES.items():
     for _w in _s.split():
         SCRATCH[_split(_w)[0]] = ("sbuf", [128, _split(_w)[1]], _t)
-SEMAPHORES = ("v gi ge1 gq gth gk gw gh sff sdq scn srt sx sw su0 sv0 srq srp srps sxq mS sod1 sod2 sg1 sg1s sg2 sg2s sg3 sg3s loc hd hret dsp dcr rsp rcr "
-              "suq sup sups swq sz so r1s r2s q1 q2 soh sba sbas sbb sbbs mqa mqb sww sfl sgg soz szq szs my sya sy swn fin svq srz srd "
+SEMAPHORES = ("v gi ge1 gq gth gk gh sff sdq scn srt sx sw su0 sv0 srq srp srps sxq mS sod1 sod2 sg1 sg1s sg2 sg2s sg3 sg3s loc he de dl sep seps hd hret dsp dcr rsp rcr "
+              "suq sup sups swq sz so r1s r2s q1 q2 soh sba sbas sbb sbbs mqa mqb sww sfl sgg soz szq szs my sya sy swn fin svq srz srd sz2 gz sza scw sd2 ska sp1 "
               "m0 m1 m2 m3 m4 m5 m6 m7").split()
 
 
@@ -52,6 +52,10 @@ def rank_program(g, core, T, topo):
     def pos(r, q):
         far, near = order(r)
         return (far + near + [r]).index(q)
+
+    def place(r, q):
+        far, near = order(r)
+        return (far + [r] + near).index(q)
 
     def handers(r):
         c = ranks[r]
@@ -72,21 +76,20 @@ def rank_program(g, core, T, topo):
     def w32(t, a, b):
         return t[:, a:b].bitcast(u32)
 
-    def direct(r, i):
-        es = topo.engines(ranks[r], ranks[order(r)[1][i]])
-        k = len(es) // 4
-        return es[k * i:k * i + k] if i < 2 else es[2 * k:]
+    def share(es, k):
+        m = len(es) // (k if k < 3 else 4)
+        return [es[m * i:m * i + m] if i < k - 1 else es[m * i:] for i in range(k)]
 
-    def upper(r):
-        es = topo.engines(ranks[r], ranks[order(r)[1][0]])
-        return es[len(es) // 2:]
+    def off(r):
+        return topo.engines(ranks[r], ranks[order(r)[1][0]])
 
     def inside(r, k):
-        es, off = topo.engines(ranks[r], handers(r)[k]), topo.engines(ranks[r], ranks[order(r)[1][0]])
-        if k == 4:
-            return [e for e in es if e not in off]
-        m = len(es) // 2
-        return es[m * (k % 2):m * (k % 2) + m]
+        es = topo.engines(ranks[r], handers(r)[k])
+        return [e for e in es if e not in off(r)] if k == 4 else share(es, 2)[k % 2]
+
+    def ahead(r, k):
+        es, m = topo.engines(ranks[r], handers(r)[k]), len(inside(r, k)) // 2
+        return inside(r, k) if k == 4 else es[m * k:m * k + m]
 
     rank = T.rank_of(core)
 
@@ -97,26 +100,36 @@ def rank_program(g, core, T, topo):
         r = mine[0]
         far, near = order(r)
         i = handers(r).index(core)
-        planes = i >= 2
-        to, s_out, s_back = (near[1:], S.dsp, S.rsp) if i == 4 else (far[2 * (i % 2):2 * (i % 2) + 2], S.dcr, S.rcr)
-        n = 0
-        for back, sem_in, sem_out, bc, bp, dc, dp in ((False, S.hd, s_out, T.hx, T.hxs, T.lx, T.lxs), (True, S.hret, s_back, T.hr, T.hrs, T.hb, T.hbs)):
-            g.wait_ge(sem_in, len(inside(r, i)))
+        n = [0]
+
+        def hand(planes, sem_in, cnt, sem, bc, bp, dc, dp, jobs):
+            g.wait_ge(sem_in, cnt)
             t = []
-            for k, q in enumerate(to):
-                es = topo.engines(core, ranks[q])[4 * k:4 * k + 4]
-                a = 2 * back + CAPP * pos(q, r)
-                t.append(send(ranks[q], es, sem_out, run(planes, bc, bp, CAPP * k, CAPP * k + CAPP), run(planes, dc, dp, a, a + CAPP)))
-                n += len(es)
+            for es, (q, a, b, m) in zip(share(topo.engines(core, ranks[jobs[0][0]]), len(jobs)), jobs):
+                t.append(send(ranks[q], es, sem, run(planes, bc, bp, a, a + m), run(planes, dc, dp, b, b + m)))
+                n[0] += len(es)
             g.remote_dma_fused(t, local_sem=S.loc)
-        g.wait_ge(S.loc, n)
+        m = TOK // 4
+        hand(i == 4, S.he, len(ahead(r, i)), S.de, T.he, T.hes, T.xe, T.xes, [(near[-1], 0, ZC, TOK) if i == 4 else (near[-1], 0, ZC + m * i, m)])
+        to, out, back, s_out, s_back = (near[:2], 2 * CAPP, CAPP, S.dsp, S.rsp) if i == 4 else (far[2 * (i % 2):2 * (i % 2) + 2], 0, 0, S.dcr, S.rcr)
+        hand(i >= 2, S.hd, len(inside(r, i)), s_out, T.hx, T.hxs, T.lx, T.lxs, [(q, out + CAPP * k, CAPP * place(q, r), CAPP) for k, q in enumerate(to)])
+        hand(i >= 2, S.hret, len(inside(r, i)), s_back, T.hr, T.hrs, T.hb, T.hbs, [(q, back + CAPP * k, ZC + CAPP * pos(q, r), CAPP) for k, q in enumerate(to)])
+        g.wait_ge(S.loc, n[0])
         return
 
     far, near = order(rank)
     blocks = far + near + [rank]
     half, own = CAPP * len(far), CAPP * (N - 1)
-    near_in = sum(len(direct(q, order(q)[1].index(rank))) + 4 for q in near)
-    far_in = 8 * len(far)
+    origin = [q for q in near if order(q)[1][-1] == rank][0]
+
+    def share_of(q, k):
+        i = order(q)[1].index(rank)
+        return len(share(off(q), k)[i]) if i < k else 0
+    ahead_in = sum(len(topo.engines(h, core)) for h in handers(origin))
+    list_in = len(off(origin))
+    near_in = sum(2 * share_of(q, 2) for q in near)
+    near_back = sum(share_of(q, 3) + (share_of(q, 2) or share_of(q, 3)) for q in near)
+    far_in = sum(2 * len(share(topo.engines(handers(q)[0], core), 2)[0]) for q in far)
     v, sc, te, sy = g.vector, g.scalar, g.tensor, g.sync
     n, nl = [0], [0]
 
@@ -133,8 +146,9 @@ def rank_program(g, core, T, topo):
     def ts(*a):
         op(v.tensor_scalar(*a))
 
-    def fused(t, sem):
-        g.wait_ge(sem, 1)
+    def fused(t, *sems):
+        for s in sems:
+            g.wait_ge(s, 1)
         g.remote_dma_fused([send(*a) for a in t], local_sem=S.loc)
         nl[0] += sum(len(a[1]) for a in t)
 
@@ -143,20 +157,17 @@ def rank_program(g, core, T, topo):
             fused([(handers(rank)[2 * planes + i], inside(rank, 2 * planes + i), sem, run(planes, bc, bp, 96 * i, 96 * i + 96), run(planes, dc, dp, 0, 96))
                    for i in range(2)], sem_p if planes else sem_c)
 
-    def to_near(base, bc, bp, sem_c, sem_p, sem, dc, dp, sem_h, hp):
+    def to_near(to, first, bc, dc, sem):
         t = []
-        for i, q in enumerate(near):
-            a, b = half + CAPP * i, base + CAPP * pos(q, rank)
-            t.append((ranks[q], direct(rank, i), sem, cod(bc, a, a + CAPP), cod(dc, b, b + CAPP)))
-        fused(t, sem_c)
-        fused([(handers(rank)[4], inside(rank, 4), sem_h, bp[:, half + CAPP:half + 3 * CAPP], hp[:, 0:96])], sem_p)
-        b = base + CAPP * pos(near[0], rank)
-        fused([(ranks[near[0]], upper(rank), sem, bp[:, half:half + CAPP], dp[:, b:b + CAPP])], sem_p)
+        for i, (q, b) in enumerate(to):
+            a = first + CAPP * i
+            t.append((ranks[q], share(off(rank), len(to))[i], sem, cod(bc, a, a + CAPP), cod(dc, b, b + CAPP)))
+        return t
 
     sc.dma_start(T.rtt[:, 0:32], T.rt[:, 0:32]).then_inc(S.srt, 16)
-    sy.dma_start(T.xt[:, 8:520], T.x[:]).then_inc(S.sx, 16)
+    sy.dma_start(T.xt[:, 4 * ZC:4 * ZC + 512], T.x[:]).then_inc(S.sx, 16)
     sc.dma_start(T.wt[:], T.w[:]).then_inc(S.sw, 16)
-    sy.dma_start(T.ut[:, 0:32], T.u[:, 0:32]).then_inc(S.su0, 16)
+    sy.dma_start(T.ut[:], T.u[:]).then_inc(S.su0, 16)
 
     def iota(out, pattern, base, sem):
         g.iota(out, pattern, base, 0, allow_small_or_imprecise_dtypes=True).then_inc(sem, 1)
@@ -172,14 +183,16 @@ def rank_program(g, core, T, topo):
     iota(T.kv[:, N:32], [[0, 32 - N]], 0, S.gk)
     iota(T.th[:, 1, :], [[-1, 8]], 1, S.gth)
     iota(T.th[:, 0, :], [[-1, 8]], 0, S.gth)
-    iota(T.q_[:], [[0, 2], [1, 16]], 2, S.gq)
-    iota(T.win[:], [[0, 416]], 0, S.gw)
-    iota(T.jr[:], [[1, 128]], 2, S.gh)
-    iota(T.jra[:], [[1, 128]], 130, S.gh)
-    iota(T.cap[:], [[0, 128]], CAPR, S.gh)
+    iota(T.q_[:], [[0, 2], [1, 16]], ZC, S.gq)
+    iota(T.zst[:, 0:2, :], [[0, 2], [0, 32]], 0, S.gz)
+    iota(T.z[:], [[0, 32]], ZC - DUMP, S.gz)
+
+    m = TOK // 4
+    fused([(handers(rank)[k], ahead(rank, k), S.he, cod(T.xq, ZC + m * k, ZC + m * k + m), cod(T.he, 0, m)) for k in range(4)], S.sxq)
+    fused([(handers(rank)[4], ahead(rank, 4), S.he, T.xs[:, ZC:ZC + TOK], T.hes[:, 0:TOK])])
 
     op(v.memset(T.rtt[:, 32:512], 0.0))
-    op(v.memset(T.xt[:, 0:8], 0.0))
+    op(v.memset(T.xt[:, 0:4 * ZC], 0.0))
     op(v.memset(T.sign[:], 1.0))
     v.wait_ge(S.gi, 1)
     ts(T.ii[:, 0:1], T.ip[:], 7, None, A.bitwise_and)
@@ -216,17 +229,19 @@ def rank_program(g, core, T, topo):
     sc.activation(T.vals[:], T.q_[:], F.Identity, bias=T.ff[:, 2:3]).then_inc(S.scn, 1)
     sc.wait_ge(S.gk, nk)
     sc.activation(T.kt[:], T.kv[:, 0:8], F.Copy, bias=1.0 * CAPP).then_inc(S.scn, 1)
+    sc.activation(T.cw[:, 0:1], T.ff[:, 3:4], F.Copy, scale=2.0, bias=1.0).then_inc(S.scw, 1)
+    sc.activation(T.cw[:, 1:2], T.ff[:, 3:4], F.Copy, scale=-1.0, bias=99.0).then_inc(S.scw, 1)
+    sc.activation(T.cr[:], T.ff[:, 3:4], F.Relu, scale=100.0, bias=-100.0 * (N - 2)).then_inc(S.scw, 1)
+    sc.wait_ge(S.scw, 3)
+    sc.activation(T.cw[:, 2:3], T.cr[:], F.Copy, scale=-1.0).then_inc(S.scw, 1)
     v.wait_ge(S.sx, 16)
     v.quantize_mx(T.xq[:], T.xs[:], T.xt[:]).then_inc(S.sxq, 1)
     te.wait_ge(S.srp, 1)
     te.wait_ge(S.srps, 1)
     te.wait_ge(S.sxq, 1)
-    te.matmul_mx(T.psb[:, 0:128], T.xq[:, 2:130], T.xs[:, 2:130], T.rp[:, 0:128], T.rps[:, 0:128], True, True).then_inc(S.mS, 1)
-    sy.wait_ge(S.sxq, 1)
-    for q_, s_ in ((T.hb, T.hbs), (T.hab, T.habs)):
-        sy.dma_start(cod(q_, 0, 2), cod(T.xq, 0, 2)).then_inc(S.sz, 16)
-        sy.dma_start(s_[:, 0:2], T.xs[:, 0:2]).then_inc(S.sz, 16)
+    te.matmul_mx(T.psb[:, 0:128], T.xq[:, ZC:ZC + TOK], T.xs[:, ZC:ZC + TOK], T.rp[:, 0:128], T.rps[:, 0:128], True, True).then_inc(S.mS, 1)
     op(v.memset(T.nn[:], 0.0))
+    op(v.memset(T.win[:], 0.0))
     v.wait_ge(S.gk, nk)
     op(v.transpose(T.kvt[:], T.kv[:]))
 
@@ -258,7 +273,6 @@ def rank_program(g, core, T, topo):
         tt(T.pr[:, k, 0:8], T.oh2[:, k, :], T.c2_[:], A.mult)
     done()
     op(v.tensor_reduce(T.of[:], T.pr[:], X, A.max))
-    v.wait_ge(S.gw, 1)
     done()
     op(v.tensor_copy(T.win[:].indirect(T.of[:]), T.vals[:]))
     done()
@@ -286,37 +300,44 @@ def rank_program(g, core, T, topo):
         v.wait_ge(sem, k)
         sc.wait_ge(sem, k)
         sc.wait_ge(S.v, n[0])
-        for a, b, c, d, q_, s_, s1, s2 in ([(half, own, 12, 21, T.xg, T.xgs, S.sg2, S.sg2s), (own, own + CAPP, 22, 25, T.lx, T.lxs, S.sg3, S.sg3s)]
+        for a, b, c, d, q_, s_, s1, s2 in ([(half, half + 2 * CAPP, 12, 18, T.xg, T.xgs, S.sg2, S.sg2s), (half, half + CAPP, 22, 25, T.lx, T.lxs, S.sg3, S.sg3s)]
                                            if h else [(0, half, 0, 12, T.xg, T.xgs, S.sg1, S.sg1s)]):
-            v.tensor_copy(w32(q_, a, b), w32(T.xq, 0, 130).indirect(T.od[:, c:d])).then_inc(s1, 1)
-            sc.activation(s_[:, a:b], T.xs[:, 0:130].indirect(T.od[:, c:d]), F.Copy).then_inc(s2, 1)
+            v.tensor_copy(w32(q_, a, b), w32(T.xq, 0, ZC + TOK).indirect(T.od[:, c:d])).then_inc(s1, 1)
+            sc.activation(s_[:, a:b], T.xs[:, 0:ZC + TOK].indirect(T.od[:, c:d]), F.Copy).then_inc(s2, 1)
+    listed = (sem, k, n[0])
 
     to_far(T.xg, T.xgs, S.sg1, S.sg1s, S.hd, T.hx, T.hxs)
-    to_near(0, T.xg, T.xgs, S.sg2, S.sg2s, S.dsp, T.lx, T.lxs, S.hd, T.hxs)
+    fused(to_near([(q, CAPP * place(q, rank)) for q in near[:2]], half, T.xg, T.lx, S.dsp)
+          + [(handers(rank)[4], inside(rank, 4), S.hd, T.xgs[:, half - 2 * CAPP:half + 2 * CAPP], T.hxs[:, 0:4 * CAPP])], S.sg2, S.sg2s)
+    g.wait_ge(listed[0], listed[1])
+    g.wait_ge(S.v, listed[2])
+    fused([(ranks[near[2]], off(rank), S.dl, T.od[:, 18:21], T.le[:, 0:3])])
+    iota(T.jr[:], [[1, 128]], ZC, S.gh)
+    iota(T.jra[:], [[1, 128]], ZC + TOK, S.gh)
+    iota(T.cc[:, 0:8], [[0, 8]], 0, S.gh)
+    iota(T.wa[:], [[0, 32]], 0, S.gh)
+    iota(T.cap[:], [[0, 128]], CAPR, S.gh)
 
-    op(v.memset(T.zst[:], 0.0))
-    op(v.memset(T.z[:], 0.0))
     op(v.tensor_reduce(T.vm[:], T.pr[:, :, 0:8], X, A.max))
-    done()
+    sc.wait_ge(S.v, n[0])
+    sc.wait_ge(S.gz, 2)
+    for k in range(2):
+        sc.activation(T.zst[:, 3 + k, :], T.z[:], F.Relu, bias=T.vm[:, k:k + 1]).then_inc(S.sza, 1)
+    v.wait_ge(S.gz, 2)
     for k in range(2):
         tt(T.zst[:, k, 0:8], T.oh2[:, k, :], T.un[:], A.mult)
-    ts(T.tk[:], T.vm[:], 0.0, None, A.is_gt)
-    ts(T.po[:], T.vm[:], 2.0 - DUMP, 0.0, A.add, A.max)
     done()
-    tt(T.mm[:, 0:1], T.tk[:, 0:1], T.tk[:, 1:2], A.mult)
-    for k in range(2):
-        ts(T.zst[:, 3 + k, :], T.z[:], T.po[:, k:k + 1], None, A.add)
+    ts(T.tk[:], T.vm[:], 0.0, BIG, A.is_gt, A.mult)
     done()
-    ts(T.mm[:, 1:2], T.tk[:, 0:1], 2.0, T.mm[:, 0:1], A.mult, A.subtract)
+    tt(T.mm[:, 0:1], T.tk[:, 1:2], T.tk[:, 0:1], A.subtract)
     done()
-    ts(T.mm[:, 2:3], T.mm[:, 1:2], -1.0, -BIG, A.add, A.mult)
-    done()
-    ts(T.zst[:, 2, :], T.z[:], T.mm[:, 2:3], None, A.add)
+    ts(T.zst[:, 2, :], T.z[:], 0.0, T.mm[:, 0:1], A.mult, A.add)
+    v.wait_ge(S.sza, 2)
     done()
     op(v.transpose(T.zt[:], T.zst[:]))
-    done()
+    sc.wait_ge(S.v, n[0])
     for b in range(4):
-        v.tensor_copy(T.rz[0:32, :, 32 * b:32 * b + 32], T.zt[32 * b:32 * b + 32, :, :]).then_inc(S.srz, 1)
+        sc.activation(T.rz[0:32, :, 32 * b:32 * b + 32], T.zt[32 * b:32 * b + 32, :, :], F.Copy).then_inc(S.srz, 1)
     sy.wait_ge(S.srz, 4)
     for b in range(1, 4):
         sy.dma_start(T.rz[32 * b:32 * b + 32, :, :], T.rz[0:32, :, :]).then_inc(S.srd, 16)
@@ -324,6 +345,20 @@ def rank_program(g, core, T, topo):
     v.wait_ge(S.sw, 16)
     for i in range(4):
         v.quantize_mx(T.wq[:, 128 * i:128 * i + 128], T.ws[:, 128 * i:128 * i + 128], T.wt[:, 512 * i:512 * i + 512]).then_inc(S.swq, 1)
+
+    a = CAPP * place(rank, origin)
+    op(v.memset(T.lo[:], 0))
+    done()
+    op(v.tensor_copy(w32(T.xe, 0, ZC), w32(T.xq, 0, ZC + TOK).indirect(T.lo[:, 0:1])))
+    sc.wait_ge(S.v, n[0])
+    sc.activation(T.xes[:, 0:ZC], T.xs[:, 0:ZC + TOK].indirect(T.lo[:, 0:1]), F.Copy).then_inc(S.sz, 1)
+    done()
+    sc.wait_ge(S.sz, 1)
+    for q in (v, sc):
+        q.wait_ge(S.de, ahead_in)
+        q.wait_ge(S.dl, list_in)
+    v.tensor_copy(w32(T.lx, a, a + CAPP), w32(T.xe, 0, ZC + TOK).indirect(T.le[:, 0:3])).then_inc(S.sep, 1)
+    sc.activation(T.lxs[:, a:a + CAPP], T.xes[:, 0:ZC + TOK].indirect(T.le[:, 0:3]), F.Copy).then_inc(S.seps, 1)
 
     def expert(h):
         a = half * (1 - h)
@@ -335,6 +370,8 @@ def rank_program(g, core, T, topo):
             te.wait_ge(S.sg3, 1)
             te.wait_ge(S.sg3s, 1)
             te.wait_ge(S.dsp, near_in)
+            te.wait_ge(S.sep, 1)
+            te.wait_ge(S.seps, 1)
         for i in range(4):
             te.matmul_mx(ps[:, 512 * i:512 * i + half], T.wq[:, 128 * i:128 * i + 128], T.ws[:, 128 * i:128 * i + 128],
                          T.lx[:, a:a + half], T.lxs[:, a:a + half], True, True).then_inc(S["m%d" % (4 * h + i)], 1)
@@ -353,67 +390,69 @@ def rank_program(g, core, T, topo):
     expert(1)
     to_far(T.hq, T.hqs, S.q2, S.q2, S.hret, T.hr, T.hrs)
     expert(0)
-    to_near(2, T.hq, T.hqs, S.q1, S.q1, S.rsp, T.hb, T.hbs, S.hret, T.hrs)
+    fused(to_near([(q, ZC + CAPP * pos(q, rank)) for q in near], half + CAPP, T.hq, T.hb, S.rsp)
+          + [(handers(rank)[4], inside(rank, 4), S.hret, T.hqs[:, half:2 * half], T.hrs[:, 0:half])], S.q1)
+    a, b = half + 3 * CAPP, ZC + CAPP * pos(near[2], rank)
+    fused([(ranks[near[2]], share(off(rank), 3)[2], S.rsp, T.hqs[:, a:a + CAPP], T.hbs[:, b:b + CAPP])])
     sy.wait_ge(S.dsp, near_in)
     sy.dma_start(T.vt[:], T.v[:]).then_inc(S.sv0, 16)
-    sy.wait_ge(S.q1, 1)
-    sy.dma_start(cod(T.hb, 2 + own, 2 + own + CAPP), cod(T.hq, own, own + CAPP)).then_inc(S.so, 16)
-    sy.dma_start(T.hbs[:, 2 + own:2 + own + CAPP], T.hqs[:, own:own + CAPP]).then_inc(S.so, 16)
 
-    v.wait_ge(S.srz, 4)
-    v.wait_ge(S.srd, 48)
-    op(v.memset(T.ut[:, 32:512], 0.0))
-    for k in range(2):
-        for d in range(2):
-            op(v.tensor_copy(T.d2[:, k, :, d, :], T.rz[:, 3 + k, :]))
-    op(v.memset(T.lo[:], 0))
-    done()
-    op(v.transpose(T.dt[:], T.d2[:]))
-    done()
-    v.tensor_copy(T.oh[:], T.dt[:, 0:512:32]).then_inc(S.soh, 1)
+    a = ZC + own
+    v.quantize_mx(T.hb[:, a:a + 128], T.hbs[:, a:a + 128], T.ht[:, 0:512]).then_inc(S.so, 1)
     v.wait_ge(S.su0, 16)
     v.quantize_mx(T.uq[:], T.us[:], T.ut[:]).then_inc(S.suq, 1)
+    for q_, s_ in ((T.hb, T.hbs), (T.hab, T.habs)):
+        op(v.tensor_copy(w32(q_, 0, ZC), w32(T.xq, 0, ZC + TOK).indirect(T.lo[:, 0:1])))
+        sc.activation(s_[:, 0:ZC], T.xs[:, 0:ZC + TOK].indirect(T.lo[:, 0:1]), F.Copy).then_inc(S.sz2, 1)
     v.wait_ge(S.suq, 1)
     v.tensor_copy(w32(T.up, 0, 128), w32(T.uq, 0, 128).indirect(T.lo[:])).then_inc(S.sup, 1)
+    sc.wait_ge(S.srz, 4)
+    sc.wait_ge(S.srd, 48)
+    for k in range(2):
+        for d in range(2):
+            sc.activation(T.d2[:, k, :, d, :], T.rz[:, 3 + k, :], F.Copy).then_inc(S.sd2, 1)
     sc.wait_ge(S.suq, 1)
     sc.activation(T.ups[:, 0:128], T.us[:, 0:128].indirect(T.lo[:]), F.Copy).then_inc(S.sups, 1)
-    v.wait_ge(S.sv0, 16)
-    v.quantize_mx(T.vq[:], T.vs[:], T.vt[:]).then_inc(S.svq, 1)
-    v.wait_ge(S.gh, 3)
-    ts(T.ka[:], T.rz[:, 0, :], -6.0, 7.0, A.mult, A.add)
-    ts(T.kb[:], T.rz[:, 1, :], -7.0, None, A.mult)
+    sc.activation(T.ka[:], T.rz[:, 0, :], F.Copy, scale=-6.0, bias=7.0).then_inc(S.ska, 1)
+    sc.activation(T.kb[:], T.rz[:, 1, :], F.Copy, scale=-7.0).then_inc(S.ska, 1)
+    v.wait_ge(S.srz, 4)
+    v.wait_ge(S.srd, 48)
+    v.wait_ge(S.gh, 5)
     tt(T.pa[:], T.rz[:, 0, :], T.jr[:], A.mult)
     tt(T.pb[:], T.rz[:, 1, :], T.jra[:], A.mult)
-    op(v.memset(T.cc[:, 0:8], 0.0))
-    op(v.memset(T.wa[:], 0.0))
-    ts(T.cw[:, 0:1], T.ff[:, 3:4], 2.0, 1.0, A.mult, A.add)
-    ts(T.cw[:, 1:2], T.ff[:, 3:4], -1.0, 99.0, A.mult, A.add)
-    ts(T.cw[:, 2:3], T.ff[:, 3:4], 1.0 * (N - 1), -100.0, A.is_equal, A.mult)
+    v.wait_ge(S.sd2, 4)
+    op(v.transpose(T.dt[:], T.d2[:]))
     done()
+    tt(T.pp[:, :, 0, :], T.pa[:], T.pb[:], A.add)
+    sc.wait_ge(S.v, n[0])
+    sc.activation(T.pp[:, :, 1, :], T.pp[:, :, 0, :], F.Copy).then_inc(S.sp1, 1)
+    v.tensor_copy(T.oh[:], T.dt[:, 0:512:32]).then_inc(S.soh, 1)
+    v.wait_ge(S.sv0, 16)
+    v.quantize_mx(T.vq[:], T.vs[:], T.vt[:]).then_inc(S.svq, 1)
+    v.wait_ge(S.ska, 2)
     tt(T.kk[:], T.ka[:], T.kb[:], A.add)
-    for d in range(2):
-        tt(T.pp[:, :, d, :], T.pa[:], T.pb[:], A.add)
+    v.wait_ge(S.sp1, 1)
     done()
     op(v.transpose(T.ppt[:], T.pp[:]))
     done()
 
     for q in (v, sc):
-        q.wait_ge(S.sz, 64)
         q.wait_ge(S.soh, 1)
-        q.wait_ge(S.so, 32)
-        q.wait_ge(S.rsp, near_in)
+        q.wait_ge(S.so, 1)
+        q.wait_ge(S.rsp, near_back)
         q.wait_ge(S.rcr, far_in)
+    sc.wait_ge(S.sz2, 2)
     for k, s1, s2 in ((1, S.sbb, S.sbbs), (0, S.sba, S.sbas)):
-        a = 2 + 128 * k
-        v.tensor_copy(w32(T.hab, a, a + 128), w32(T.hb, 0, 386).indirect(T.oh[:, 8 * k:8 * k + 8])).then_inc(s1, 1)
-        sc.activation(T.habs[:, a:a + 128], T.hbs[:, 0:386].indirect(T.oh[:, 8 * k:8 * k + 8]), F.Copy).then_inc(s2, 1)
+        a = ZC + TOK * k
+        v.tensor_copy(w32(T.hab, a, a + 128), w32(T.hb, 0, 480).indirect(T.oh[:, 8 * k:8 * k + 8])).then_inc(s1, 1)
+        sc.activation(T.habs[:, a:a + 128], T.hbs[:, 0:480].indirect(T.oh[:, 8 * k:8 * k + 8]), F.Copy).then_inc(s2, 1)
     for s in (S.sup, S.sups, S.svq, S.sbb, S.sbbs):
         te.wait_ge(s, 1)
-    te.matmul_mx(T.psa[:, 0:128], T.up[:, 0:128], T.ups[:, 0:128], T.hab[:, 130:258], T.habs[:, 130:258], True, True).then_inc(S.mqb, 1)
+    te.matmul_mx(T.psa[:, 0:128], T.up[:, 0:128], T.ups[:, 0:128], T.hab[:, ZC + TOK:ZC + 2 * TOK], T.habs[:, ZC + TOK:ZC + 2 * TOK], True, True).then_inc(S.mqb, 1)
     te.wait_ge(S.sba, 1)
     te.wait_ge(S.sbas, 1)
-    te.matmul_mx(T.psa[:, 512:640], T.up[:, 0:128], T.ups[:, 0:128], T.hab[:, 2:130], T.habs[:, 2:130], True, True).then_inc(S.mqa, 1)
-    te.matmul_mx(T.psa[:, 1024:1282], T.vq[:, 0:128], T.vs[:, 0:128], T.hab[:, 0:258], T.habs[:, 0:258], True, True).then_inc(S.my, 1)
+    te.matmul_mx(T.psa[:, 512:640], T.up[:, 0:128], T.ups[:, 0:128], T.hab[:, ZC:ZC + TOK], T.habs[:, ZC:ZC + TOK], True, True).then_inc(S.mqa, 1)
+    te.matmul_mx(T.psa[:, 1024:1296], T.vq[:, 0:128], T.vs[:, 0:128], T.hab[:, 0:272], T.habs[:, 0:272], True, True).then_inc(S.my, 1)
     v.wait_ge(S.mqb, 1)
     tt(T.qb[:], T.psa[:, 0:128], T.rz[:, 2, :], A.add)
     v.wait_ge(S.mqa, 1)
@@ -434,17 +473,18 @@ def rank_program(g, core, T, topo):
     done()
     v.tensor_reduce(T.oz[:], T.vz[:], X, A.max).then_inc(S.soz, 1)
     sc.wait_ge(S.my, 1)
-    sc.activation(T.ya[:], T.psa[:, 1024:1282], F.Copy).then_inc(S.sya, 1)
+    sc.activation(T.ya[:], T.psa[:, 1024:1296], F.Copy).then_inc(S.sya, 1)
+    sc.wait_ge(S.scw, 4)
     sc.wait_ge(S.sww, 1)
     sc.activation(T.gh[:, :, 0, :], T.ww[:], F.Identity, scale=T.cw[:, 1:2], bias=T.cw[:, 2:3]).then_inc(S.sgg, 1)
     sc.wait_ge(S.sfl, 1)
     sc.activation(T.gh[:, :, 1, :], T.vv[:, :, 0, :], F.Copy, scale=T.cw[:, 0:1]).then_inc(S.sgg, 1)
     v.wait_ge(S.soz, 1)
-    v.tensor_copy(w32(T.zq, 0, 128), w32(T.hab, 0, 258).indirect(T.oz[:])).then_inc(S.szq, 1)
+    v.tensor_copy(w32(T.zq, 0, 128), w32(T.hab, 0, 272).indirect(T.oz[:])).then_inc(S.szq, 1)
     sc.wait_ge(S.sya, 1)
     sc.wait_ge(S.soz, 1)
-    sc.activation(T.yb[:], T.ya[:, 0:258].indirect(T.oz[:]), F.Copy).then_inc(S.sy, 1)
-    sc.activation(T.zs[:, 0:128], T.habs[:, 0:258].indirect(T.oz[:]), F.Copy).then_inc(S.szs, 1)
+    sc.activation(T.yb[:], T.ya[:, 0:272].indirect(T.oz[:]), F.Copy).then_inc(S.sy, 1)
+    sc.activation(T.zs[:, 0:128], T.habs[:, 0:272].indirect(T.oz[:]), F.Copy).then_inc(S.szs, 1)
     v.wait_ge(S.sgg, 2)
     op(v.transpose(T.ght[:], T.gh[:]))
     done()

@@ -5,13 +5,13 @@ C8, PL, BF, FP, I32, U16 = "float8_e4m3fn_x4", "uint8", "bfloat16", "float32", "
 CAPP, CAPR, DUMP, TOK, ZC = 48, 32, 32, 128, 16
 BIG = 2.0 ** 98
 SHAPES = {
-    C8: "xq144 rq128 rp128 wq512 uq128 up128 vq128 xg336 he128 xe144 hx192 lx384 hq384 hr192 hb480 hab272 zq128",
-    PL: "xs144 rs128 rps128 ws512 us128 ups128 vs128 xgs336 hes128 xes144 hxs192 lxs384 hqs384 hrs192 hbs480 habs272 zs128",
-    BF: "xt576 rtt512 wt2048 ut512 vt512 ht1536 vals32 nn128 nt128 win416 ot768 cap128 ge128 kk128 ww128 cc136",
-    FP: "yb128 ya272 ff4 jr128 jra128 e_4 ee4 q_32 kv32 kvt32 kt8 c2_8 sign64 z32 cw3 cr1 dq2 bs64 gt64 rk64 cs128 ct32 "
-        "un8 ta24 tb24 vm2 tk2 mm1 ka128 kb128 pa128 pb128 dt512 qb128 wa32 wb32",
+    C8: "xq144 rq128 rp128 wq512 uq128 up128 vq128 xg336 he128 xe144 hx192 lx336 hq336 hr192 hb480 hab272 zq128",
+    PL: "xs144 rs128 rps128 ws512 us128 ups128 vs128 xgs336 hes128 xes144 hxs192 lxs336 hqs336 hrs192 hbs480 habs272 zs128",
+    BF: "xt576 rtt512 wt2048 ut512 vt512 hto512 ht1344 vals32 nn128 nt128 win1056 ot768 ge128 kk128 ww128 cc128",
+    FP: "yb128 ya272 ff4 jr128 jra128 e_4 q_32 kv32 kvt32 kt8 ka8 c2_8 c3_8 sign64 z32 cw3 cr1 bs64 gt64 rk64 cs128 ct32 "
+        "un8 ta24 tb24 vm2 tk2 mm1 ra128 rb128 pa128 pb128 dt512 qb128 wa32 wb32",
     I32: "ip1 ii4",
-    U16: "lp8 lo8 of2 od26 oh16 oz8 le4",
+    U16: "lp8 lo8 of2 od24 oh16 oz8 le4",
 }
 
 
@@ -22,18 +22,20 @@ def _split(s):
 
 SCRATCH = {
     "th": ("sbuf", [128, 2, 8], FP), "oh2": ("sbuf", [128, 2, 8], FP),
-    "pr": ("sbuf", [128, 2, 9], FP), "dd": ("sbuf", [128, 8, 3, 2, 16], BF),
+    "pr": ("sbuf", [128, 2, 8], FP), "ph": ("sbuf", [128, 2, 8], FP), "dd": ("sbuf", [128, 8, 3, 2, 16], BF),
     "zst": ("sbuf", [128, 5, 32], FP), "zt": ("sbuf", [128, 5, 32], FP), "rz": ("sbuf", [128, 5, 128], FP),
     "d2": ("sbuf", [128, 2, 8, 2, 16], FP), "vv": ("sbuf", [128, 8, 2, 16], BF), "vvt": ("sbuf", [128, 8, 32], BF),
+    "lv": ("sbuf", [128, 8, 2, 16], BF), "lvt": ("sbuf", [128, 8, 32], BF), "wp": ("sbuf", [128, 8, 8], FP),
     "pp": ("sbuf", [128, 8, 2, 16], FP), "ppt": ("sbuf", [128, 8, 32], FP), "vz": ("sbuf", [128, 8, 8], FP),
-    "gh": ("sbuf", [128, 4, 2, 32], BF), "ght": ("sbuf", [128, 4, 2, 32], BF), "gg": ("sbuf", [128, 4, 8], FP),
+    "gh": ("sbuf", [128, 4, 2, 32], BF), "ght": ("sbuf", [128, 4, 2, 32], BF),
+    "gs": ("sbuf", [128, 4, 32], BF), "gst": ("sbuf", [128, 4, 32], BF),
     "psa": ("psum", [128, 2048], FP), "psb": ("psum", [128, 2048], FP),
 }
 for _t, _s in SHAPES.items():
     for _w in _s.split():
         SCRATCH[_split(_w)[0]] = ("sbuf", [128, _split(_w)[1]], _t)
-SEMAPHORES = ("v gi ge1 gq gth gk gh sff sdq scn srt sx sw su0 sv0 srq srp srps sxq mS sod1 sod2 sg1 sg1s sg2 sg2s sg3 sg3s loc he de dl sep seps hd hret dsp dcr rsp rcr "
-              "suq sup sups swq sz so r1s r2s q1 q2 soh sba sbas sbb sbbs mqa mqb sww sfl sgg soz szq szs my sya sy swn fin svq srz srd sz2 gz sza scw sd2 ska sp1 "
+SEMAPHORES = ("v f gi ge1 gq gth gk gh ga sff sff2 swz scn srt sx sw su0 sv0 srq srp srps sxq mS sdd sde sod1 sod2 sg1 sg1s sg2 sg2s loc he de dl sep seps hd hret dsp dcr rsp rcr "
+              "suq sup sups swq sz so mo sro r1s r2s q1 q2 soh sba sbas sbb sbbs mqa mqb sww scc sgg sgs soz szq szs my sya sy swn fin svq srz srd sz2 gz scw sd2 ska sp1 "
               "m0 m1 m2 m3 m4 m5 m6 m7").split()
 
 
@@ -55,7 +57,7 @@ def rank_program(g, core, T, topo):
 
     def place(r, q):
         far, near = order(r)
-        return (far + [r] + near).index(q)
+        return (far + near).index(q)
 
     def handers(r):
         c = ranks[r]
@@ -118,8 +120,8 @@ def rank_program(g, core, T, topo):
         return
 
     far, near = order(rank)
-    blocks = far + near + [rank]
-    half, own = CAPP * len(far), CAPP * (N - 1)
+    lists = far + [rank] + near
+    half, own, rest = CAPP * len(far), CAPP * (N - 1), CAPP * len(near)
     origin = [q for q in near if order(q)[1][-1] == rank][0]
 
     def share_of(q, k):
@@ -131,7 +133,7 @@ def rank_program(g, core, T, topo):
     near_back = sum(share_of(q, 3) + (share_of(q, 2) or share_of(q, 3)) for q in near)
     far_in = sum(2 * len(share(topo.engines(handers(q)[0], core), 2)[0]) for q in far)
     v, sc, te, sy = g.vector, g.scalar, g.tensor, g.sync
-    n, nl = [0], [0]
+    n, nf, nl = [0], [0], [0]
 
     def op(c):
         c.then_inc(S.v, 1)
@@ -139,6 +141,13 @@ def rank_program(g, core, T, topo):
 
     def done():
         v.wait_ge(S.v, n[0])
+
+    def fl(c):
+        c.then_inc(S.f, 1)
+        nf[0] += 1
+
+    def fdone():
+        v.wait_ge(S.f, nf[0])
 
     def tt(*a):
         op(v.tensor_tensor(*a))
@@ -171,68 +180,74 @@ def rank_program(g, core, T, topo):
 
     def iota(out, pattern, base, sem):
         g.iota(out, pattern, base, 0, allow_small_or_imprecise_dtypes=True).then_inc(sem, 1)
+
+    def columns(out, value, sem):
+        i, k = 0, 0
+        while i < N:
+            m = 1
+            while i + m < N and lists[i + m] == lists[i] + 2 * m and (m == 1 or value(lists[i + m]) - value(lists[i + m - 1]) == value(lists[i + 1]) - value(lists[i])):
+                m += 1
+            a, step = lists[i], value(lists[i + 1]) - value(lists[i]) if m > 1 else 0
+            iota(out[:, a:a + 2 * m - 1:2], [[step, m]], value(a), sem)
+            i, k = i + m, k + 1
+        return k
     g.iota(T.ip[:], [[0, 1]], 0, 1).then_inc(S.gi, 1)
     iota(T.e_[:], [[2, 4]], 0, S.ge1)
-    i, nk = 0, 1
-    while i < N:
-        m = 1
-        while i + m < N and blocks[i + m] == blocks[i] + 2 * m:
-            m += 1
-        iota(T.kv[:, blocks[i]:blocks[i] + 2 * m - 1:2], [[CAPP, m]], DUMP + CAPP * i - 1, S.gk)
-        i, nk = i + m, nk + 1
+    nk = columns(T.kv, lambda e: DUMP + TOK * lists.index(e) - 1, S.gk)
     iota(T.kv[:, N:32], [[0, 32 - N]], 0, S.gk)
+    nk += 1
     iota(T.th[:, 1, :], [[-1, 8]], 1, S.gth)
     iota(T.th[:, 0, :], [[-1, 8]], 0, S.gth)
     iota(T.q_[:], [[0, 2], [1, 16]], ZC, S.gq)
-    iota(T.zst[:, 0:2, :], [[0, 2], [0, 32]], 0, S.gz)
-    iota(T.z[:], [[0, 32]], ZC - DUMP, S.gz)
 
     m = TOK // 4
     fused([(handers(rank)[k], ahead(rank, k), S.he, cod(T.xq, ZC + m * k, ZC + m * k + m), cod(T.he, 0, m)) for k in range(4)], S.sxq)
     fused([(handers(rank)[4], ahead(rank, 4), S.he, T.xs[:, ZC:ZC + TOK], T.hes[:, 0:TOK])])
+    iota(T.zst[:, 0:2, :], [[0, 2], [0, 32]], 0, S.gz)
+    iota(T.z[:], [[0, 32]], ZC - DUMP, S.gz)
+    na = columns(T.ka, lambda e: CAPP * pos(rank, e) - TOK * lists.index(e), S.ga)
 
     op(v.memset(T.rtt[:, 32:512], 0.0))
-    op(v.memset(T.xt[:, 0:4 * ZC], 0.0))
-    op(v.memset(T.sign[:], 1.0))
     v.wait_ge(S.gi, 1)
     ts(T.ii[:, 0:1], T.ip[:], 7, None, A.bitwise_and)
     ts(T.ii[:, 1:2], T.ip[:], 3, 1, A.logical_shift_right, A.bitwise_and)
-    ts(T.ii[:, 2:3], T.ip[:], 112, None, A.bitwise_and)
-    ts(T.ii[:, 3:4], T.ip[:], 31, None, A.bitwise_and)
+    fl(v.memset(T.xt[:, 0:4 * ZC], 0.0))
+    fl(v.memset(T.sign[:], 1.0))
     done()
-    v.tensor_copy(T.ff[:], T.ii[:]).then_inc(S.sff, 1)
-    op(v.memset(T.sign[:, 0:64:9], -1.0))
-    v.wait_ge(S.sff, 1)
+    op(v.tensor_copy(T.ff[:, 0:2], T.ii[:, 0:2]))
+    fl(v.tensor_scalar(T.ii[:, 2:3], T.ip[:], 112, None, A.bitwise_and))
+    fl(v.tensor_scalar(T.ii[:, 3:4], T.ip[:], 31, None, A.bitwise_and))
     v.wait_ge(S.ge1, 1)
     done()
-    ts(T.ee[:], T.e_[:], T.ff[:, 1:2], None, A.add)
-    op(v.memset(T.sign[:, 0:64:8], 0.0))
-    done()
-    ts(T.lp[:, 0:4], T.ee[:], T.ff[:, 0:1], None, A.max)
-    ts(T.lp[:, 4:8], T.ee[:], T.ff[:, 0:1], None, A.min)
-    done()
-    sc.wait_ge(S.sff, 1)
-    sc.activation(T.dq[:, 0:1], T.ff[:, 1:2], F.Copy, scale=16.0).then_inc(S.sdq, 1)
-    sc.activation(T.dq[:, 1:2], T.ff[:, 1:2], F.Copy, scale=16.0, bias=1.0).then_inc(S.sdq, 1)
-    sc.wait_ge(S.sdq, 2)
-    for k in range(2):
-        sc.activation(T.pr[:, k, 8:9], T.ff[:, 0:1], F.Identity, scale=2.0, bias=T.dq[:, k:k + 1]).then_inc(S.scn, 1)
+    op(v.tensor_scalar(T.lp[:, 0:4], T.e_[:], T.ff[:, 1:2], T.ff[:, 0:1], A.add, A.max))
+    op(v.tensor_scalar(T.lp[:, 4:8], T.e_[:], T.ff[:, 1:2], T.ff[:, 0:1], A.add, A.min))
+    listed_pairs = n[0]
+    fdone()
+    v.tensor_copy(T.ff[:, 2:4], T.ii[:, 2:4]).then_inc(S.sff, 1)
+    fl(v.memset(T.sign[:, 0:64:9], -1.0))
 
     v.wait_ge(S.srt, 16)
+    done()
     v.quantize_mx(T.rq[:], T.rs[:], T.rtt[:]).then_inc(S.srq, 1)
+    fdone()
+    fl(v.memset(T.sign[:, 0:64:8], 0.0))
     v.wait_ge(S.srq, 1)
     v.tensor_copy(w32(T.rp, 0, 128), w32(T.rq, 0, 128).indirect(T.lp[:])).then_inc(S.srp, 1)
+    sc.wait_ge(S.v, 1)
+    sc.activation(T.win[:, 0:480], T.rtt[:, 32:512], F.Copy).then_inc(S.swz, 1)
     sc.wait_ge(S.srq, 1)
-    sc.wait_ge(S.v, n[0])
+    sc.wait_ge(S.v, listed_pairs)
     sc.activation(T.rps[:, 0:128], T.rs[:, 0:128].indirect(T.lp[:]), F.Copy).then_inc(S.srps, 1)
+    sc.activation(T.win[:, 480:960], T.rtt[:, 32:512], F.Copy).then_inc(S.swz, 1)
+    sc.activation(T.win[:, 960:1056], T.rtt[:, 32:128], F.Copy).then_inc(S.swz, 1)
+    sc.wait_ge(S.sff, 1)
     sc.wait_ge(S.gq, 1)
     sc.activation(T.vals[:], T.q_[:], F.Identity, bias=T.ff[:, 2:3]).then_inc(S.scn, 1)
     sc.wait_ge(S.gk, nk)
     sc.activation(T.kt[:], T.kv[:, 0:8], F.Copy, bias=1.0 * CAPP).then_inc(S.scn, 1)
-    sc.activation(T.cw[:, 0:1], T.ff[:, 3:4], F.Copy, scale=2.0, bias=1.0).then_inc(S.scw, 1)
-    sc.activation(T.cw[:, 1:2], T.ff[:, 3:4], F.Copy, scale=-1.0, bias=99.0).then_inc(S.scw, 1)
+    sc.activation(T.cw[:, 0:1], T.ff[:, 3:4], F.Copy, bias=0.5).then_inc(S.scw, 1)
     sc.activation(T.cr[:], T.ff[:, 3:4], F.Relu, scale=100.0, bias=-100.0 * (N - 2)).then_inc(S.scw, 1)
-    sc.wait_ge(S.scw, 3)
+    sc.wait_ge(S.scw, 2)
     sc.activation(T.cw[:, 2:3], T.cr[:], F.Copy, scale=-1.0).then_inc(S.scw, 1)
     v.wait_ge(S.sx, 16)
     v.quantize_mx(T.xq[:], T.xs[:], T.xt[:]).then_inc(S.sxq, 1)
@@ -241,98 +256,140 @@ def rank_program(g, core, T, topo):
     te.wait_ge(S.sxq, 1)
     te.matmul_mx(T.psb[:, 0:128], T.xq[:, ZC:ZC + TOK], T.xs[:, ZC:ZC + TOK], T.rp[:, 0:128], T.rps[:, 0:128], True, True).then_inc(S.mS, 1)
     op(v.memset(T.nn[:], 0.0))
-    op(v.memset(T.win[:], 0.0))
     v.wait_ge(S.gk, nk)
     op(v.transpose(T.kvt[:], T.kv[:]))
+    op(v.memset(T.lo[:], 0))
 
     v.wait_ge(S.mS, 1)
     op(v.tensor_copy(T.bs[:], T.psb[:, 64:128]))
     done()
     tt(T.gt[:], T.psb[:, 0:64], T.bs[:], A.is_gt)
+    fdone()
     done()
     op(v.tensor_tensor_scan(T.rk[:], T.sign[:], T.gt[:], 0.0, A.mult, A.add))
     v.wait_ge(S.gth, 2)
     done()
     for d, b, p, c in ((64, 0, 64, 0), (32, 0, 32, 0), (64, 32, 32, 32), (96, 0, 32, 32), (96, 64, 32, 64), (0, 0, 128, 96)):
         tt(T.nn[d:d + p, c:c + 8], T.rk[b:b + p, 7:64:8], T.th[b:b + p, 1, :], A.is_le)
+    for k in range(2):
+        fl(v.tensor_tensor(T.oh2[:, k, :], T.rk[:, 7:64:8], T.th[:, k, :], A.is_equal))
     done()
     op(v.transpose(T.nt[:], T.nn[:]))
     done()
     op(v.tensor_tensor_scan(T.cs[:], T.nt[:], T.nt[:], T.kvt[:, 0:1], A.add, A.max))
-    tt(T.oh2[:, 0, :], T.rk[:, 7:64:8], T.th[:, 0, :], A.is_equal)
-    tt(T.oh2[:, 1, :], T.rk[:, 7:64:8], T.th[:, 1, :], A.is_equal)
     done()
     op(v.transpose(T.ct[:], T.cs[:, 96:128]))
-    v.wait_ge(S.scn, 4)
-    done()
-    tt(T.un[:], T.ct[:, 0:8], T.kt[:], A.is_le)
-    done()
-    tt(T.c2_[:], T.un[:], T.ct[:, 0:8], A.mult)
+    fdone()
     done()
     for k in range(2):
-        tt(T.pr[:, k, 0:8], T.oh2[:, k, :], T.c2_[:], A.mult)
+        tt(T.pr[:, k, :], T.oh2[:, k, :], T.ct[:, 0:8], A.mult)
     done()
     op(v.tensor_reduce(T.of[:], T.pr[:], X, A.max))
+    v.wait_ge(S.scn, 2)
+    fl(v.tensor_tensor(T.un[:], T.ct[:, 0:8], T.kt[:], A.is_le))
+    v.wait_ge(S.swz, 3)
     done()
     op(v.tensor_copy(T.win[:].indirect(T.of[:]), T.vals[:]))
+    v.wait_ge(S.ga, na)
+    fl(v.tensor_tensor(T.c3_[:], T.ct[:, 0:8], T.ka[:], A.add))
     done()
-    for h in range(2):
-        a, b = 4 * h, 4 * h + 4
-        for d in range(2):
-            op(v.tensor_copy(T.dd[:, a:b, :, d, :], T.win[:, DUMP + CAPP * a:DUMP + CAPP * b]))
-        done()
-        op(v.transpose(T.ot[:, 96 * a:96 * b], T.dd[:, a:b]))
-        done()
-        c = slice(3 * a, 3 * b)
-        tt(T.ta[:, c], T.ot[:, 96 * a:96 * b:32], T.ot[:, 96 * a + 16:96 * b:32], A.add)
-        done()
-        tt(T.tb[0:64, c], T.ta[0:64, c], T.ta[64:128, c], A.add)
-        done()
-        sem, k = S.sod2 if h else S.sod1, 0
-        runs = [(12, 21, 12), (21, 24, 22)] if h else [(0, 12, 0)]
-        for lo, hi, to in runs:
-            for p in (0, 32):
-                tt(T.od[p:p + 32, to:to + hi - lo], T.tb[0:32, lo:hi], T.tb[32:64, lo:hi], A.add)
-        done()
-        for lo, hi, to in runs:
-            v.tensor_copy(T.od[64:128, to:to + hi - lo], T.od[0:64, to:to + hi - lo]).then_inc(sem, 1)
-            k += 1
-        v.wait_ge(sem, k)
-        sc.wait_ge(sem, k)
-        sc.wait_ge(S.v, n[0])
-        for a, b, c, d, q_, s_, s1, s2 in ([(half, half + 2 * CAPP, 12, 18, T.xg, T.xgs, S.sg2, S.sg2s), (half, half + CAPP, 22, 25, T.lx, T.lxs, S.sg3, S.sg3s)]
-                                           if h else [(0, half, 0, 12, T.xg, T.xgs, S.sg1, S.sg1s)]):
-            v.tensor_copy(w32(q_, a, b), w32(T.xq, 0, ZC + TOK).indirect(T.od[:, c:d])).then_inc(s1, 1)
-            sc.activation(s_[:, a:b], T.xs[:, 0:ZC + TOK].indirect(T.od[:, c:d]), F.Copy).then_inc(s2, 1)
-    listed = (sem, k, n[0])
+    scattered = n[0]
+
+    def lay(i, d):
+        return T.dd[:, i, :, d, :], T.win[:, DUMP + TOK * i:DUMP + TOK * i + CAPP]
+    sc.wait_ge(S.v, scattered)
+    for i in range(8):
+        if i != 3:
+            sc.activation(*lay(i, 1), F.Copy).then_inc(S.sde if i > 3 else S.sdd, 1)
+    for i in range(4):
+        op(v.tensor_copy(*lay(i, 0)))
+    op(v.tensor_copy(*lay(3, 1)))
+    fl(v.tensor_copy(*lay(4, 0)))
+    v.wait_ge(S.sdd, 3)
+    done()
+    op(v.transpose(T.ot[:, 0:384], T.dd[:, 0:4]))
+    fl(v.tensor_copy(*lay(5, 0)))
+    fl(v.tensor_copy(*lay(6, 0)))
+    done()
+    tt(T.ta[:, 0:12], T.ot[:, 0:384:32], T.ot[:, 16:384:32], A.add)
+    fl(v.tensor_copy(*lay(7, 0)))
+    done()
+    tt(T.tb[0:64, 0:12], T.ta[0:64, 0:12], T.ta[64:128, 0:12], A.add)
+    v.wait_ge(S.sde, 4)
+    fdone()
+    done()
+    for p in (0, 32):
+        tt(T.od[p:p + 32, 0:12], T.tb[0:32, 0:12], T.tb[32:64, 0:12], A.add)
+    done()
+    far_list = n[0]
+    v.tensor_copy(T.od[64:128, 0:12], T.od[0:64, 0:12]).then_inc(S.sod1, 1)
+    fl(v.transpose(T.ot[:, 384:768], T.dd[:, 4:8]))
+
+    def picked(lo, hi, a, s1, s2):
+        b = a + 16 * (hi - lo)
+        v.tensor_copy(w32(T.xg, a, b), w32(T.xq, 0, ZC + TOK).indirect(T.od[:, lo:hi])).then_inc(s1, 1)
+        sc.activation(T.xgs[:, a:b], T.xs[:, 0:ZC + TOK].indirect(T.od[:, lo:hi]), F.Copy).then_inc(s2, 1)
+    v.wait_ge(S.sod1, 1)
+    sc.wait_ge(S.sod1, 1)
+    sc.wait_ge(S.v, far_list)
+    picked(0, 12, 0, S.sg1, S.sg1s)
+    fdone()
+    tt(T.ta[:, 12:24], T.ot[:, 384:768:32], T.ot[:, 400:768:32], A.add)
+    fl(v.tensor_tensor(T.c2_[:], T.un[:], T.c3_[:], A.mult))
+    done()
+    tt(T.tb[0:64, 12:24], T.ta[0:64, 12:24], T.ta[64:128, 12:24], A.add)
+    done()
+    for p in (0, 32):
+        tt(T.od[p:p + 32, 12:24], T.tb[0:32, 12:24], T.tb[32:64, 12:24], A.add)
+    done()
+    near_list = n[0]
+    v.tensor_copy(T.od[64:128, 12:24], T.od[0:64, 12:24]).then_inc(S.sod2, 1)
+    v.wait_ge(S.sod2, 1)
+    sc.wait_ge(S.sod2, 1)
+    sc.wait_ge(S.v, near_list)
+    picked(12, 21, half, S.sg2, S.sg2s)
 
     to_far(T.xg, T.xgs, S.sg1, S.sg1s, S.hd, T.hx, T.hxs)
-    fused(to_near([(q, CAPP * place(q, rank)) for q in near[:2]], half, T.xg, T.lx, S.dsp)
-          + [(handers(rank)[4], inside(rank, 4), S.hd, T.xgs[:, half - 2 * CAPP:half + 2 * CAPP], T.hxs[:, 0:4 * CAPP])], S.sg2, S.sg2s)
-    g.wait_ge(listed[0], listed[1])
-    g.wait_ge(S.v, listed[2])
-    fused([(ranks[near[2]], off(rank), S.dl, T.od[:, 18:21], T.le[:, 0:3])])
+    g.wait_ge(S.sod2, 1)
+    g.wait_ge(S.v, near_list)
+    fused([(ranks[near[2]], off(rank), S.dl, T.od[:, 21:24], T.le[:, 0:3])])
+    fused(to_near([(q, CAPP * place(q, rank)) for q in near[:2]], half + CAPP, T.xg, T.lx, S.dsp)
+          + [(handers(rank)[4], inside(rank, 4), S.hd, T.xgs[:, half - CAPP:half + 3 * CAPP], T.hxs[:, 0:4 * CAPP])], S.sg2, S.sg2s)
     iota(T.jr[:], [[1, 128]], ZC, S.gh)
     iota(T.jra[:], [[1, 128]], ZC + TOK, S.gh)
-    iota(T.cc[:, 0:8], [[0, 8]], 0, S.gh)
     iota(T.wa[:], [[0, 32]], 0, S.gh)
-    iota(T.cap[:], [[0, 128]], CAPR, S.gh)
 
-    op(v.tensor_reduce(T.vm[:], T.pr[:, :, 0:8], X, A.max))
-    sc.wait_ge(S.v, n[0])
-    sc.wait_ge(S.gz, 2)
+    v.wait_ge(S.sw, 16)
+    for i in range(4):
+        v.quantize_mx(T.wq[:, 128 * i:128 * i + 128], T.ws[:, 128 * i:128 * i + 128], T.wt[:, 512 * i:512 * i + 512]).then_inc(S.swq, 1)
+
+    te.wait_ge(S.sg2, 1)
+    te.wait_ge(S.sg2s, 1)
+    for i in range(4):
+        te.wait_ge(S.swq, i + 1)
+        te.matmul_mx(T.psa[:, 512 * i:512 * i + 128], T.wq[:, 128 * i:128 * i + 128], T.ws[:, 128 * i:128 * i + 128],
+                     T.xg[:, half:half + 128], T.xgs[:, half:half + 128], True, True).then_inc(S.mo, 1)
+    for i in range(4):
+        sc.wait_ge(S.mo, i + 1)
+        sc.activation(T.hto[:, i:512:4], T.psa[:, 512 * i:512 * i + 128], F.Relu, scale=0.0625).then_inc(S.sro, 1)
+
+    fdone()
     for k in range(2):
-        sc.activation(T.zst[:, 3 + k, :], T.z[:], F.Relu, bias=T.vm[:, k:k + 1]).then_inc(S.sza, 1)
+        tt(T.ph[:, k, :], T.oh2[:, k, :], T.c2_[:], A.mult)
     v.wait_ge(S.gz, 2)
     for k in range(2):
-        tt(T.zst[:, k, 0:8], T.oh2[:, k, :], T.un[:], A.mult)
+        fl(v.tensor_tensor(T.zst[:, k, 0:8], T.oh2[:, k, :], T.un[:], A.mult))
+    done()
+    op(v.tensor_reduce(T.vm[:], T.ph[:], X, A.max))
     done()
     ts(T.tk[:], T.vm[:], 0.0, BIG, A.is_gt, A.mult)
+    for k in range(2):
+        fl(v.tensor_scalar(T.zst[:, 3 + k, :], T.z[:], T.vm[:, k:k + 1], 0.0, A.add, A.max))
     done()
     tt(T.mm[:, 0:1], T.tk[:, 1:2], T.tk[:, 0:1], A.subtract)
     done()
     ts(T.zst[:, 2, :], T.z[:], 0.0, T.mm[:, 0:1], A.mult, A.add)
-    v.wait_ge(S.sza, 2)
+    fdone()
     done()
     op(v.transpose(T.zt[:], T.zst[:]))
     sc.wait_ge(S.v, n[0])
@@ -342,16 +399,11 @@ def rank_program(g, core, T, topo):
     for b in range(1, 4):
         sy.dma_start(T.rz[32 * b:32 * b + 32, :, :], T.rz[0:32, :, :]).then_inc(S.srd, 16)
 
-    v.wait_ge(S.sw, 16)
-    for i in range(4):
-        v.quantize_mx(T.wq[:, 128 * i:128 * i + 128], T.ws[:, 128 * i:128 * i + 128], T.wt[:, 512 * i:512 * i + 512]).then_inc(S.swq, 1)
-
     a = CAPP * place(rank, origin)
-    op(v.memset(T.lo[:], 0))
-    done()
     op(v.tensor_copy(w32(T.xe, 0, ZC), w32(T.xq, 0, ZC + TOK).indirect(T.lo[:, 0:1])))
-    sc.wait_ge(S.v, n[0])
     sc.activation(T.xes[:, 0:ZC], T.xs[:, 0:ZC + TOK].indirect(T.lo[:, 0:1]), F.Copy).then_inc(S.sz, 1)
+    v.wait_ge(S.sro, 4)
+    v.quantize_mx(T.hb[:, ZC + own:ZC + own + 128], T.hbs[:, ZC + own:ZC + own + 128], T.hto[:]).then_inc(S.so, 1)
     done()
     sc.wait_ge(S.sz, 1)
     for q in (v, sc):
@@ -361,44 +413,41 @@ def rank_program(g, core, T, topo):
     sc.activation(T.lxs[:, a:a + CAPP], T.xes[:, 0:ZC + TOK].indirect(T.le[:, 0:3]), F.Copy).then_inc(S.seps, 1)
 
     def expert(h):
-        a = half * (1 - h)
-        ps, t0, rs = (T.psb, 4 * half, S.r2s) if h else (T.psa, 0, S.r1s)
+        a, m = (0, half) if h else (half, rest)
+        ps, t0, rs = (T.psb, 0, S.r2s) if h else (T.psa, 4 * half, S.r1s)
         if h:
-            te.wait_ge(S.swq, 4)
             te.wait_ge(S.dcr, far_in)
         else:
-            te.wait_ge(S.sg3, 1)
-            te.wait_ge(S.sg3s, 1)
+            te.wait_ge(S.sro, 4)
             te.wait_ge(S.dsp, near_in)
             te.wait_ge(S.sep, 1)
             te.wait_ge(S.seps, 1)
         for i in range(4):
-            te.matmul_mx(ps[:, 512 * i:512 * i + half], T.wq[:, 128 * i:128 * i + 128], T.ws[:, 128 * i:128 * i + 128],
-                         T.lx[:, a:a + half], T.lxs[:, a:a + half], True, True).then_inc(S["m%d" % (4 * h + i)], 1)
+            te.matmul_mx(ps[:, 512 * i:512 * i + m], T.wq[:, 128 * i:128 * i + 128], T.ws[:, 128 * i:128 * i + 128],
+                         T.lx[:, a:a + m], T.lxs[:, a:a + m], True, True).then_inc(S["m%d" % (4 * h + i)], 1)
         for i in range(4):
-            src, dst = ps[:, 512 * i:512 * i + half], T.ht[:, t0 + i:t0 + 4 * half:4]
-            q = sc if i % 2 else v
+            src, dst = ps[:, 512 * i:512 * i + m], T.ht[:, t0 + i:t0 + 4 * m:4]
+            vec = i == 3 or h and i == 1
+            q = v if vec else sc
             q.wait_ge(S["m%d" % (4 * h + i)], 1)
-            if i % 2:
-                sc.activation(dst, src, F.Relu, scale=0.0625).then_inc(rs, 1)
-            else:
+            if vec:
                 ts(dst, src, 0.0, 0.0625, A.max, A.mult)
+            else:
+                sc.activation(dst, src, F.Relu, scale=0.0625).then_inc(rs, 1)
+        v.wait_ge(rs, 2 if h else 3)
         done()
-        v.wait_ge(rs, 2)
-        v.quantize_mx(T.hq[:, a:a + half], T.hqs[:, a:a + half], T.ht[:, t0:t0 + 4 * half]).then_inc(S.q2 if h else S.q1, 1)
+        v.quantize_mx(T.hq[:, a:a + m], T.hqs[:, a:a + m], T.ht[:, t0:t0 + 4 * m]).then_inc(S.q2 if h else S.q1, 1)
 
     expert(1)
     to_far(T.hq, T.hqs, S.q2, S.q2, S.hret, T.hr, T.hrs)
     expert(0)
-    fused(to_near([(q, ZC + CAPP * pos(q, rank)) for q in near], half + CAPP, T.hq, T.hb, S.rsp)
-          + [(handers(rank)[4], inside(rank, 4), S.hret, T.hqs[:, half:2 * half], T.hrs[:, 0:half])], S.q1)
-    a, b = half + 3 * CAPP, ZC + CAPP * pos(near[2], rank)
+    fused(to_near([(q, ZC + CAPP * pos(q, rank)) for q in near], half, T.hq, T.hb, S.rsp)
+          + [(handers(rank)[4], inside(rank, 4), S.hret, T.hqs[:, half - CAPP:half + rest], T.hrs[:, 0:half])], S.q1)
+    a, b = half + 2 * CAPP, ZC + CAPP * pos(near[2], rank)
     fused([(ranks[near[2]], share(off(rank), 3)[2], S.rsp, T.hqs[:, a:a + CAPP], T.hbs[:, b:b + CAPP])])
     sy.wait_ge(S.dsp, near_in)
     sy.dma_start(T.vt[:], T.v[:]).then_inc(S.sv0, 16)
 
-    a = ZC + own
-    v.quantize_mx(T.hb[:, a:a + 128], T.hbs[:, a:a + 128], T.ht[:, 0:512]).then_inc(S.so, 1)
     v.wait_ge(S.su0, 16)
     v.quantize_mx(T.uq[:], T.us[:], T.ut[:]).then_inc(S.suq, 1)
     for q_, s_ in ((T.hb, T.hbs), (T.hab, T.habs)):
@@ -413,11 +462,11 @@ def rank_program(g, core, T, topo):
             sc.activation(T.d2[:, k, :, d, :], T.rz[:, 3 + k, :], F.Copy).then_inc(S.sd2, 1)
     sc.wait_ge(S.suq, 1)
     sc.activation(T.ups[:, 0:128], T.us[:, 0:128].indirect(T.lo[:]), F.Copy).then_inc(S.sups, 1)
-    sc.activation(T.ka[:], T.rz[:, 0, :], F.Copy, scale=-6.0, bias=7.0).then_inc(S.ska, 1)
-    sc.activation(T.kb[:], T.rz[:, 1, :], F.Copy, scale=-7.0).then_inc(S.ska, 1)
+    sc.activation(T.ra[:], T.rz[:, 0, :], F.Copy, scale=-6.0, bias=7.0).then_inc(S.ska, 1)
+    sc.activation(T.rb[:], T.rz[:, 1, :], F.Copy, scale=-7.0).then_inc(S.ska, 1)
     v.wait_ge(S.srz, 4)
     v.wait_ge(S.srd, 48)
-    v.wait_ge(S.gh, 5)
+    v.wait_ge(S.gh, 3)
     tt(T.pa[:], T.rz[:, 0, :], T.jr[:], A.mult)
     tt(T.pb[:], T.rz[:, 1, :], T.jra[:], A.mult)
     v.wait_ge(S.sd2, 4)
@@ -430,7 +479,7 @@ def rank_program(g, core, T, topo):
     v.wait_ge(S.sv0, 16)
     v.quantize_mx(T.vq[:], T.vs[:], T.vt[:]).then_inc(S.svq, 1)
     v.wait_ge(S.ska, 2)
-    tt(T.kk[:], T.ka[:], T.kb[:], A.add)
+    tt(T.kk[:], T.ra[:], T.rb[:], A.add)
     v.wait_ge(S.sp1, 1)
     done()
     op(v.transpose(T.ppt[:], T.pp[:]))
@@ -461,36 +510,45 @@ def rank_program(g, core, T, topo):
     done()
     v.tensor_tensor(T.ww[:], T.ge[:], T.kk[:], A.is_equal).then_inc(S.sww, 1)
     v.wait_ge(S.sww, 1)
-    op(v.tensor_tensor_scan(T.cc[:, 8:136], T.ww[:], T.cap[:], 0.0, A.add, A.min))
+    v.tensor_tensor_scan(T.cc[:], T.ww[:], T.ww[:], 0.0, A.add, A.max).then_inc(S.scc, 1)
+    for d in range(2):
+        fl(v.tensor_copy(T.vv[:, :, d, :], T.ww[:]))
+    v.wait_ge(S.scc, 1)
+    for d in range(2):
+        ts(T.lv[:, :, d, :], T.cc[:], 1.0 * CAPR, None, A.is_le)
+    fdone()
+    fl(v.transpose(T.vvt[:], T.vv[:]))
     done()
-    v.tensor_tensor(T.vv[:, :, 0, :], T.cc[:, 8:136], T.cc[:, 7:135], A.subtract).then_inc(S.sfl, 1)
-    v.wait_ge(S.sfl, 1)
-    op(v.tensor_copy(T.vv[:, :, 1, :], T.vv[:, :, 0, :]))
+    op(v.transpose(T.lvt[:], T.lv[:]))
+    fdone()
+    fl(v.tensor_tensor(T.wp[:], T.vvt[:, :, 0:8], T.ppt[:, :, 0:8], A.mult))
+    v.wait_ge(S.sgg, 2)
+    op(v.transpose(T.ght[:], T.gh[:]))
+    fdone()
     done()
-    op(v.transpose(T.vvt[:], T.vv[:]))
-    done()
-    tt(T.vz[:], T.vvt[:, :, 0:8], T.ppt[:, :, 0:8], A.mult)
-    done()
+    fl(v.tensor_tensor(T.vz[:], T.wp[:], T.lvt[:, :, 0:8], A.mult))
+    v.wait_ge(S.sgs, 1)
+    op(v.transpose(T.gst[:], T.gs[:]))
+    fdone()
     v.tensor_reduce(T.oz[:], T.vz[:], X, A.max).then_inc(S.soz, 1)
+    done()
+    tt(T.ght[:, :, 0, 8:16], T.ght[:, :, 1, 0:8], T.gst[:, :, 0:8], A.mult)
     sc.wait_ge(S.my, 1)
     sc.activation(T.ya[:], T.psa[:, 1024:1296], F.Copy).then_inc(S.sya, 1)
-    sc.wait_ge(S.scw, 4)
+    sc.wait_ge(S.scw, 3)
     sc.wait_ge(S.sww, 1)
-    sc.activation(T.gh[:, :, 0, :], T.ww[:], F.Identity, scale=T.cw[:, 1:2], bias=T.cw[:, 2:3]).then_inc(S.sgg, 1)
-    sc.wait_ge(S.sfl, 1)
-    sc.activation(T.gh[:, :, 1, :], T.vv[:, :, 0, :], F.Copy, scale=T.cw[:, 0:1]).then_inc(S.sgg, 1)
+    sc.activation(T.gh[:, :, 0, :], T.ww[:], F.Identity, scale=99.5, bias=T.cw[:, 2:3]).then_inc(S.sgg, 1)
+    sc.activation(T.gh[:, :, 1, :], T.ww[:], F.Copy, scale=T.cw[:, 0:1]).then_inc(S.sgg, 1)
+    sc.wait_ge(S.scc, 1)
+    sc.activation(T.gs[:], T.cc[:], F.Sign, scale=-1.0, bias=CAPR + 0.5).then_inc(S.sgs, 1)
     v.wait_ge(S.soz, 1)
     v.tensor_copy(w32(T.zq, 0, 128), w32(T.hab, 0, 272).indirect(T.oz[:])).then_inc(S.szq, 1)
+    v.tensor_copy(T.zs[:, 0:128], T.habs[:, 0:272].indirect(T.oz[:])).then_inc(S.szs, 1)
     sc.wait_ge(S.sya, 1)
     sc.wait_ge(S.soz, 1)
     sc.activation(T.yb[:], T.ya[:, 0:272].indirect(T.oz[:]), F.Copy).then_inc(S.sy, 1)
-    sc.activation(T.zs[:, 0:128], T.habs[:, 0:272].indirect(T.oz[:]), F.Copy).then_inc(S.szs, 1)
-    v.wait_ge(S.sgg, 2)
-    op(v.transpose(T.ght[:], T.gh[:]))
     done()
-    tt(T.gg[:], T.ght[:, :, 0, 0:8], T.ght[:, :, 1, 0:8], A.add)
-    done()
-    op(v.tensor_reduce(T.wa[:, 0:4], T.gg[:], X, A.add))
+    op(v.tensor_reduce(T.wa[:, 0:4], T.ght[:, :, 0, 0:16], X, A.add))
     done()
     v.transpose(T.wb[:], T.wa[:]).then_inc(S.swn, 1)
     sy.wait_ge(S.szq, 1)

from concourse.bass import DstId, RemoteDMATransfer
from concourse.mybir import dt, AluOpType as A, AxisListType, ActivationFunctionType as F

C8, PL, BF, FP, I32, U16 = "float8_e4m3fn_x4", "uint8", "bfloat16", "float32", "int32", "uint16"
CAPP, CAPR, DUMP, TOK, ZC = 48, 32, 32, 128, 16
BIG = 2.0 ** 98
SHAPES = {
    C8: "xq144 rq128 rp128 wq512 uq128 up128 vq128 xg336 he128 xe144 hx192 lx336 hq336 hr192 hb480 hab272 zq128",
    PL: "xs144 rs128 rps128 ws512 us128 ups128 vs128 xgs336 hes128 xes144 hxs192 lxs336 hqs336 hrs192 hbs480 habs272 zs128",
    BF: "xt576 rtt512 wt2048 ut512 vt512 hto512 ht1344 vals32 nn128 nt128 win1056 ot768 ge128 kk128 ww128 cc128",
    FP: "yb128 ya272 ff4 jr128 jra128 e_4 q_32 kv32 kvt32 kt8 ka8 c2_8 c3_8 sign64 z32 cw3 cr1 bs64 gt64 rk64 cs128 ct32 "
        "un8 ta24 tb24 vm2 tk2 mm1 ra128 rb128 pa128 pb128 dt512 qb128 wa32 wb32",
    I32: "ip1 ii4",
    U16: "lp8 lo8 of2 od24 oh16 oz8 le4",
}


def _split(s):
    k = len(s.rstrip("0123456789"))
    return s[:k], int(s[k:])


SCRATCH = {
    "th": ("sbuf", [128, 2, 8], FP), "oh2": ("sbuf", [128, 2, 8], FP),
    "pr": ("sbuf", [128, 2, 8], FP), "ph": ("sbuf", [128, 2, 8], FP), "dd": ("sbuf", [128, 8, 3, 2, 16], BF),
    "zst": ("sbuf", [128, 5, 32], FP), "zt": ("sbuf", [128, 5, 32], FP), "rz": ("sbuf", [128, 5, 128], FP),
    "d2": ("sbuf", [128, 2, 8, 2, 16], FP), "vv": ("sbuf", [128, 8, 2, 16], BF), "vvt": ("sbuf", [128, 8, 32], BF),
    "lv": ("sbuf", [128, 8, 2, 16], BF), "lvt": ("sbuf", [128, 8, 32], BF), "wp": ("sbuf", [128, 8, 8], FP),
    "pp": ("sbuf", [128, 8, 2, 16], FP), "ppt": ("sbuf", [128, 8, 32], FP), "vz": ("sbuf", [128, 8, 8], FP),
    "gh": ("sbuf", [128, 4, 2, 32], BF), "ght": ("sbuf", [128, 4, 2, 32], BF),
    "gs": ("sbuf", [128, 4, 32], BF), "gst": ("sbuf", [128, 4, 32], BF),
    "psa": ("psum", [128, 2048], FP), "psb": ("psum", [128, 2048], FP),
}
for _t, _s in SHAPES.items():
    for _w in _s.split():
        SCRATCH[_split(_w)[0]] = ("sbuf", [128, _split(_w)[1]], _t)
SEMAPHORES = ("v f gi ge1 gq gth gk gh ga sff sff2 swz scn srt sx sw su0 sv0 srq srp srps sxq mS sdd sde sod1 sod2 sg1 sg1s sg2 sg2s loc he de dl sep seps hd hret dsp dcr rsp rcr "
              "suq sup sups swq sz so mo sro r1s r2s q1 q2 soh sba sbas sbb sbbs mqa mqb sww scc sgg sgs soz szq szs my sya sy swn fin svq srz srd sz2 gz scw sd2 ska sp1 "
              "m0 m1 m2 m3 m4 m5 m6 m7").split()


def rank_program(g, core, T, topo):
    S = T.sem
    ranks = list(T.cores)
    N = len(ranks)
    u8, u32, X = dt.uint8, dt.uint32, AxisListType.X

    def order(r):
        rot = [(r + k) % N for k in range(1, N)]
        far = [q for q in rot if not topo.may_write(ranks[r], ranks[q])]
        near = [q for q in rot if topo.may_write(ranks[r], ranks[q])]
        return far, near

    def pos(r, q):
        far, near = order(r)
        return (far + near + [r]).index(q)

    def place(r, q):
        far, near = order(r)
        return (far + near).index(q)

    def handers(r):
        c = ranks[r]
        can = [h for h in topo.cores_of(c) if h != c and all(topo.may_write(h, ranks[q]) for q in order(r)[0])]
        can = sorted(can, key=lambda h: (topo.die(h) == topo.die(c), h))[:4]
        return can + [h for h in topo.cores_of(c) if h != c and topo.die(h) == topo.die(c) and h not in can][:1]

    def send(dst_core, es, sem, src, dst):
        rid, pid = topo.addr(dst_core, core)
        return RemoteDMATransfer(dst_ids=[DstId(rid=rid, pnc=pid)], dma_engine_mask=sum(1 << e for e in es), remote_sem=sem, src=src, dst=dst)

    def cod(t, a, b):
        return t[:, a:b].bitcast(u8)

    def run(planes, c, p, a, b):
        return p[:, a:b] if planes else cod(c, a, b)

    def w32(t, a, b):
        return t[:, a:b].bitcast(u32)

    def share(es, k):
        m = len(es) // (k if k < 3 else 4)
        return [es[m * i:m * i + m] if i < k - 1 else es[m * i:] for i in range(k)]

    def off(r):
        return topo.engines(ranks[r], ranks[order(r)[1][0]])

    def inside(r, k):
        es = topo.engines(ranks[r], handers(r)[k])
        return [e for e in es if e not in off(r)] if k == 4 else share(es, 2)[k % 2]

    def ahead(r, k):
        es, m = topo.engines(ranks[r], handers(r)[k]), len(inside(r, k)) // 2
        return inside(r, k) if k == 4 else es[m * k:m * k + m]

    rank = T.rank_of(core)

    if rank is None:
        mine = [r for r in range(N) if ranks[r] in topo.cores_of(core)]
        if not mine or core not in handers(mine[0]):
            return
        r = mine[0]
        far, near = order(r)
        i = handers(r).index(core)
        n = [0]

        def hand(planes, sem_in, cnt, sem, bc, bp, dc, dp, jobs):
            g.wait_ge(sem_in, cnt)
            t = []
            for es, (q, a, b, m) in zip(share(topo.engines(core, ranks[jobs[0][0]]), len(jobs)), jobs):
                t.append(send(ranks[q], es, sem, run(planes, bc, bp, a, a + m), run(planes, dc, dp, b, b + m)))
                n[0] += len(es)
            g.remote_dma_fused(t, local_sem=S.loc)
        m = TOK // 4
        hand(i == 4, S.he, len(ahead(r, i)), S.de, T.he, T.hes, T.xe, T.xes, [(near[-1], 0, ZC, TOK) if i == 4 else (near[-1], 0, ZC + m * i, m)])
        to, out, back, s_out, s_back = (near[:2], 2 * CAPP, CAPP, S.dsp, S.rsp) if i == 4 else (far[2 * (i % 2):2 * (i % 2) + 2], 0, 0, S.dcr, S.rcr)
        hand(i >= 2, S.hd, len(inside(r, i)), s_out, T.hx, T.hxs, T.lx, T.lxs, [(q, out + CAPP * k, CAPP * place(q, r), CAPP) for k, q in enumerate(to)])
        hand(i >= 2, S.hret, len(inside(r, i)), s_back, T.hr, T.hrs, T.hb, T.hbs, [(q, back + CAPP * k, ZC + CAPP * pos(q, r), CAPP) for k, q in enumerate(to)])
        g.wait_ge(S.loc, n[0])
        return

    far, near = order(rank)
    lists = far + [rank] + near
    half, own, rest = CAPP * len(far), CAPP * (N - 1), CAPP * len(near)
    origin = [q for q in near if order(q)[1][-1] == rank][0]

    def share_of(q, k):
        i = order(q)[1].index(rank)
        return len(share(off(q), k)[i]) if i < k else 0
    ahead_in = sum(len(topo.engines(h, core)) for h in handers(origin))
    list_in = len(off(origin))
    near_in = sum(2 * share_of(q, 2) for q in near)
    near_back = sum(share_of(q, 3) + (share_of(q, 2) or share_of(q, 3)) for q in near)
    far_in = sum(2 * len(share(topo.engines(handers(q)[0], core), 2)[0]) for q in far)
    v, sc, te, sy = g.vector, g.scalar, g.tensor, g.sync
    n, nf, nl = [0], [0], [0]

    def op(c):
        c.then_inc(S.v, 1)
        n[0] += 1

    def done():
        v.wait_ge(S.v, n[0])

    def fl(c):
        c.then_inc(S.f, 1)
        nf[0] += 1

    def fdone():
        v.wait_ge(S.f, nf[0])

    def tt(*a):
        op(v.tensor_tensor(*a))

    def ts(*a):
        op(v.tensor_scalar(*a))

    def fused(t, *sems):
        for s in sems:
            g.wait_ge(s, 1)
        g.remote_dma_fused([send(*a) for a in t], local_sem=S.loc)
        nl[0] += sum(len(a[1]) for a in t)

    def to_far(bc, bp, sem_c, sem_p, sem, dc, dp):
        for planes in (False, True):
            fused([(handers(rank)[2 * planes + i], inside(rank, 2 * planes + i), sem, run(planes, bc, bp, 96 * i, 96 * i + 96), run(planes, dc, dp, 0, 96))
                   for i in range(2)], sem_p if planes else sem_c)

    def to_near(to, first, bc, dc, sem):
        t = []
        for i, (q, b) in enumerate(to):
            a = first + CAPP * i
            t.append((ranks[q], share(off(rank), len(to))[i], sem, cod(bc, a, a + CAPP), cod(dc, b, b + CAPP)))
        return t

    sc.dma_start(T.rtt[:, 0:32], T.rt[:, 0:32]).then_inc(S.srt, 16)
    sy.dma_start(T.xt[:, 4 * ZC:4 * ZC + 512], T.x[:]).then_inc(S.sx, 16)
    sc.dma_start(T.wt[:], T.w[:]).then_inc(S.sw, 16)
    sy.dma_start(T.ut[:], T.u[:]).then_inc(S.su0, 16)

    def iota(out, pattern, base, sem):
        g.iota(out, pattern, base, 0, allow_small_or_imprecise_dtypes=True).then_inc(sem, 1)

    def columns(out, value, sem):
        i, k = 0, 0
        while i < N:
            m = 1
            while i + m < N and lists[i + m] == lists[i] + 2 * m and (m == 1 or value(lists[i + m]) - value(lists[i + m - 1]) == value(lists[i + 1]) - value(lists[i])):
                m += 1
            a, step = lists[i], value(lists[i + 1]) - value(lists[i]) if m > 1 else 0
            iota(out[:, a:a + 2 * m - 1:2], [[step, m]], value(a), sem)
            i, k = i + m, k + 1
        return k
    g.iota(T.ip[:], [[0, 1]], 0, 1).then_inc(S.gi, 1)
    iota(T.e_[:], [[2, 4]], 0, S.ge1)
    nk = columns(T.kv, lambda e: DUMP + TOK * lists.index(e) - 1, S.gk)
    iota(T.kv[:, N:32], [[0, 32 - N]], 0, S.gk)
    nk += 1
    iota(T.th[:, 1, :], [[-1, 8]], 1, S.gth)
    iota(T.th[:, 0, :], [[-1, 8]], 0, S.gth)
    iota(T.q_[:], [[0, 2], [1, 16]], ZC, S.gq)

    m = TOK // 4
    fused([(handers(rank)[k], ahead(rank, k), S.he, cod(T.xq, ZC + m * k, ZC + m * k + m), cod(T.he, 0, m)) for k in range(4)], S.sxq)
    fused([(handers(rank)[4], ahead(rank, 4), S.he, T.xs[:, ZC:ZC + TOK], T.hes[:, 0:TOK])])
    iota(T.zst[:, 0:2, :], [[0, 2], [0, 32]], 0, S.gz)
    iota(T.z[:], [[0, 32]], ZC - DUMP, S.gz)
    na = columns(T.ka, lambda e: CAPP * pos(rank, e) - TOK * lists.index(e), S.ga)

    op(v.memset(T.rtt[:, 32:512], 0.0))
    v.wait_ge(S.gi, 1)
    ts(T.ii[:, 0:1], T.ip[:], 7, None, A.bitwise_and)
    ts(T.ii[:, 1:2], T.ip[:], 3, 1, A.logical_shift_right, A.bitwise_and)
    fl(v.memset(T.xt[:, 0:4 * ZC], 0.0))
    fl(v.memset(T.sign[:], 1.0))
    done()
    op(v.tensor_copy(T.ff[:, 0:2], T.ii[:, 0:2]))
    fl(v.tensor_scalar(T.ii[:, 2:3], T.ip[:], 112, None, A.bitwise_and))
    fl(v.tensor_scalar(T.ii[:, 3:4], T.ip[:], 31, None, A.bitwise_and))
    v.wait_ge(S.ge1, 1)
    done()
    op(v.tensor_scalar(T.lp[:, 0:4], T.e_[:], T.ff[:, 1:2], T.ff[:, 0:1], A.add, A.max))
    op(v.tensor_scalar(T.lp[:, 4:8], T.e_[:], T.ff[:, 1:2], T.ff[:, 0:1], A.add, A.min))
    listed_pairs = n[0]
    fdone()
    v.tensor_copy(T.ff[:, 2:4], T.ii[:, 2:4]).then_inc(S.sff, 1)
    fl(v.memset(T.sign[:, 0:64:9], -1.0))

    v.wait_ge(S.srt, 16)
    done()
    v.quantize_mx(T.rq[:], T.rs[:], T.rtt[:]).then_inc(S.srq, 1)
    fdone()
    fl(v.memset(T.sign[:, 0:64:8], 0.0))
    v.wait_ge(S.srq, 1)
    v.tensor_copy(w32(T.rp, 0, 128), w32(T.rq, 0, 128).indirect(T.lp[:])).then_inc(S.srp, 1)
    sc.wait_ge(S.v, 1)
    sc.activation(T.win[:, 0:480], T.rtt[:, 32:512], F.Copy).then_inc(S.swz, 1)
    sc.wait_ge(S.srq, 1)
    sc.wait_ge(S.v, listed_pairs)
    sc.activation(T.rps[:, 0:128], T.rs[:, 0:128].indirect(T.lp[:]), F.Copy).then_inc(S.srps, 1)
    sc.activation(T.win[:, 480:960], T.rtt[:, 32:512], F.Copy).then_inc(S.swz, 1)
    sc.activation(T.win[:, 960:1056], T.rtt[:, 32:128], F.Copy).then_inc(S.swz, 1)
    sc.wait_ge(S.sff, 1)
    sc.wait_ge(S.gq, 1)
    sc.activation(T.vals[:], T.q_[:], F.Identity, bias=T.ff[:, 2:3]).then_inc(S.scn, 1)
    sc.wait_ge(S.gk, nk)
    sc.activation(T.kt[:], T.kv[:, 0:8], F.Copy, bias=1.0 * CAPP).then_inc(S.scn, 1)
    sc.activation(T.cw[:, 0:1], T.ff[:, 3:4], F.Copy, bias=0.5).then_inc(S.scw, 1)
    sc.activation(T.cr[:], T.ff[:, 3:4], F.Relu, scale=100.0, bias=-100.0 * (N - 2)).then_inc(S.scw, 1)
    sc.wait_ge(S.scw, 2)
    sc.activation(T.cw[:, 2:3], T.cr[:], F.Copy, scale=-1.0).then_inc(S.scw, 1)
    v.wait_ge(S.sx, 16)
    v.quantize_mx(T.xq[:], T.xs[:], T.xt[:]).then_inc(S.sxq, 1)
    te.wait_ge(S.srp, 1)
    te.wait_ge(S.srps, 1)
    te.wait_ge(S.sxq, 1)
    te.matmul_mx(T.psb[:, 0:128], T.xq[:, ZC:ZC + TOK], T.xs[:, ZC:ZC + TOK], T.rp[:, 0:128], T.rps[:, 0:128], True, True).then_inc(S.mS, 1)
    op(v.memset(T.nn[:], 0.0))
    v.wait_ge(S.gk, nk)
    op(v.transpose(T.kvt[:], T.kv[:]))
    op(v.memset(T.lo[:], 0))

    v.wait_ge(S.mS, 1)
    op(v.tensor_copy(T.bs[:], T.psb[:, 64:128]))
    done()
    tt(T.gt[:], T.psb[:, 0:64], T.bs[:], A.is_gt)
    fdone()
    done()
    op(v.tensor_tensor_scan(T.rk[:], T.sign[:], T.gt[:], 0.0, A.mult, A.add))
    v.wait_ge(S.gth, 2)
    done()
    for d, b, p, c in ((64, 0, 64, 0), (32, 0, 32, 0), (64, 32, 32, 32), (96, 0, 32, 32), (96, 64, 32, 64), (0, 0, 128, 96)):
        tt(T.nn[d:d + p, c:c + 8], T.rk[b:b + p, 7:64:8], T.th[b:b + p, 1, :], A.is_le)
    for k in range(2):
        fl(v.tensor_tensor(T.oh2[:, k, :], T.rk[:, 7:64:8], T.th[:, k, :], A.is_equal))
    done()
    op(v.transpose(T.nt[:], T.nn[:]))
    done()
    op(v.tensor_tensor_scan(T.cs[:], T.nt[:], T.nt[:], T.kvt[:, 0:1], A.add, A.max))
    done()
    op(v.transpose(T.ct[:], T.cs[:, 96:128]))
    fdone()
    done()
    for k in range(2):
        tt(T.pr[:, k, :], T.oh2[:, k, :], T.ct[:, 0:8], A.mult)
    done()
    op(v.tensor_reduce(T.of[:], T.pr[:], X, A.max))
    v.wait_ge(S.scn, 2)
    fl(v.tensor_tensor(T.un[:], T.ct[:, 0:8], T.kt[:], A.is_le))
    v.wait_ge(S.swz, 3)
    done()
    op(v.tensor_copy(T.win[:].indirect(T.of[:]), T.vals[:]))
    v.wait_ge(S.ga, na)
    fl(v.tensor_tensor(T.c3_[:], T.ct[:, 0:8], T.ka[:], A.add))
    done()
    scattered = n[0]

    def lay(i, d):
        return T.dd[:, i, :, d, :], T.win[:, DUMP + TOK * i:DUMP + TOK * i + CAPP]
    sc.wait_ge(S.v, scattered)
    for i in range(8):
        if i != 3:
            sc.activation(*lay(i, 1), F.Copy).then_inc(S.sde if i > 3 else S.sdd, 1)
    for i in range(4):
        op(v.tensor_copy(*lay(i, 0)))
    op(v.tensor_copy(*lay(3, 1)))
    fl(v.tensor_copy(*lay(4, 0)))
    v.wait_ge(S.sdd, 3)
    done()
    op(v.transpose(T.ot[:, 0:384], T.dd[:, 0:4]))
    fl(v.tensor_copy(*lay(5, 0)))
    fl(v.tensor_copy(*lay(6, 0)))
    done()
    tt(T.ta[:, 0:12], T.ot[:, 0:384:32], T.ot[:, 16:384:32], A.add)
    fl(v.tensor_copy(*lay(7, 0)))
    done()
    tt(T.tb[0:64, 0:12], T.ta[0:64, 0:12], T.ta[64:128, 0:12], A.add)
    v.wait_ge(S.sde, 4)
    fdone()
    done()
    for p in (0, 32):
        tt(T.od[p:p + 32, 0:12], T.tb[0:32, 0:12], T.tb[32:64, 0:12], A.add)
    done()
    far_list = n[0]
    v.tensor_copy(T.od[64:128, 0:12], T.od[0:64, 0:12]).then_inc(S.sod1, 1)
    fl(v.transpose(T.ot[:, 384:768], T.dd[:, 4:8]))

    def picked(lo, hi, a, s1, s2):
        b = a + 16 * (hi - lo)
        v.tensor_copy(w32(T.xg, a, b), w32(T.xq, 0, ZC + TOK).indirect(T.od[:, lo:hi])).then_inc(s1, 1)
        sc.activation(T.xgs[:, a:b], T.xs[:, 0:ZC + TOK].indirect(T.od[:, lo:hi]), F.Copy).then_inc(s2, 1)
    v.wait_ge(S.sod1, 1)
    sc.wait_ge(S.sod1, 1)
    sc.wait_ge(S.v, far_list)
    picked(0, 12, 0, S.sg1, S.sg1s)
    fdone()
    tt(T.ta[:, 12:24], T.ot[:, 384:768:32], T.ot[:, 400:768:32], A.add)
    fl(v.tensor_tensor(T.c2_[:], T.un[:], T.c3_[:], A.mult))
    done()
    tt(T.tb[0:64, 12:24], T.ta[0:64, 12:24], T.ta[64:128, 12:24], A.add)
    done()
    for p in (0, 32):
        tt(T.od[p:p + 32, 12:24], T.tb[0:32, 12:24], T.tb[32:64, 12:24], A.add)
    done()
    near_list = n[0]
    v.tensor_copy(T.od[64:128, 12:24], T.od[0:64, 12:24]).then_inc(S.sod2, 1)
    v.wait_ge(S.sod2, 1)
    sc.wait_ge(S.sod2, 1)
    sc.wait_ge(S.v, near_list)
    picked(12, 21, half, S.sg2, S.sg2s)

    to_far(T.xg, T.xgs, S.sg1, S.sg1s, S.hd, T.hx, T.hxs)
    g.wait_ge(S.sod2, 1)
    g.wait_ge(S.v, near_list)
    fused([(ranks[near[2]], off(rank), S.dl, T.od[:, 21:24], T.le[:, 0:3])])
    fused(to_near([(q, CAPP * place(q, rank)) for q in near[:2]], half + CAPP, T.xg, T.lx, S.dsp)
          + [(handers(rank)[4], inside(rank, 4), S.hd, T.xgs[:, half - CAPP:half + 3 * CAPP], T.hxs[:, 0:4 * CAPP])], S.sg2, S.sg2s)
    iota(T.jr[:], [[1, 128]], ZC, S.gh)
    iota(T.jra[:], [[1, 128]], ZC + TOK, S.gh)
    iota(T.wa[:], [[0, 32]], 0, S.gh)

    v.wait_ge(S.sw, 16)
    for i in range(4):
        v.quantize_mx(T.wq[:, 128 * i:128 * i + 128], T.ws[:, 128 * i:128 * i + 128], T.wt[:, 512 * i:512 * i + 512]).then_inc(S.swq, 1)

    te.wait_ge(S.sg2, 1)
    te.wait_ge(S.sg2s, 1)
    for i in range(4):
        te.wait_ge(S.swq, i + 1)
        te.matmul_mx(T.psa[:, 512 * i:512 * i + 128], T.wq[:, 128 * i:128 * i + 128], T.ws[:, 128 * i:128 * i + 128],
                     T.xg[:, half:half + 128], T.xgs[:, half:half + 128], True, True).then_inc(S.mo, 1)
    for i in range(4):
        sc.wait_ge(S.mo, i + 1)
        sc.activation(T.hto[:, i:512:4], T.psa[:, 512 * i:512 * i + 128], F.Relu, scale=0.0625).then_inc(S.sro, 1)

    fdone()
    for k in range(2):
        tt(T.ph[:, k, :], T.oh2[:, k, :], T.c2_[:], A.mult)
    v.wait_ge(S.gz, 2)
    for k in range(2):
        fl(v.tensor_tensor(T.zst[:, k, 0:8], T.oh2[:, k, :], T.un[:], A.mult))
    done()
    op(v.tensor_reduce(T.vm[:], T.ph[:], X, A.max))
    done()
    ts(T.tk[:], T.vm[:], 0.0, BIG, A.is_gt, A.mult)
    for k in range(2):
        fl(v.tensor_scalar(T.zst[:, 3 + k, :], T.z[:], T.vm[:, k:k + 1], 0.0, A.add, A.max))
    done()
    tt(T.mm[:, 0:1], T.tk[:, 1:2], T.tk[:, 0:1], A.subtract)
    done()
    ts(T.zst[:, 2, :], T.z[:], 0.0, T.mm[:, 0:1], A.mult, A.add)
    fdone()
    done()
    op(v.transpose(T.zt[:], T.zst[:]))
    sc.wait_ge(S.v, n[0])
    for b in range(4):
        sc.activation(T.rz[0:32, :, 32 * b:32 * b + 32], T.zt[32 * b:32 * b + 32, :, :], F.Copy).then_inc(S.srz, 1)
    sy.wait_ge(S.srz, 4)
    for b in range(1, 4):
        sy.dma_start(T.rz[32 * b:32 * b + 32, :, :], T.rz[0:32, :, :]).then_inc(S.srd, 16)

    a = CAPP * place(rank, origin)
    op(v.tensor_copy(w32(T.xe, 0, ZC), w32(T.xq, 0, ZC + TOK).indirect(T.lo[:, 0:1])))
    sc.activation(T.xes[:, 0:ZC], T.xs[:, 0:ZC + TOK].indirect(T.lo[:, 0:1]), F.Copy).then_inc(S.sz, 1)
    v.wait_ge(S.sro, 4)
    v.quantize_mx(T.hb[:, ZC + own:ZC + own + 128], T.hbs[:, ZC + own:ZC + own + 128], T.hto[:]).then_inc(S.so, 1)
    done()
    sc.wait_ge(S.sz, 1)
    for q in (v, sc):
        q.wait_ge(S.de, ahead_in)
        q.wait_ge(S.dl, list_in)
    v.tensor_copy(w32(T.lx, a, a + CAPP), w32(T.xe, 0, ZC + TOK).indirect(T.le[:, 0:3])).then_inc(S.sep, 1)
    sc.activation(T.lxs[:, a:a + CAPP], T.xes[:, 0:ZC + TOK].indirect(T.le[:, 0:3]), F.Copy).then_inc(S.seps, 1)

    def expert(h):
        a, m = (0, half) if h else (half, rest)
        ps, t0, rs = (T.psb, 0, S.r2s) if h else (T.psa, 4 * half, S.r1s)
        if h:
            te.wait_ge(S.dcr, far_in)
        else:
            te.wait_ge(S.sro, 4)
            te.wait_ge(S.dsp, near_in)
            te.wait_ge(S.sep, 1)
            te.wait_ge(S.seps, 1)
        for i in range(4):
            te.matmul_mx(ps[:, 512 * i:512 * i + m], T.wq[:, 128 * i:128 * i + 128], T.ws[:, 128 * i:128 * i + 128],
                         T.lx[:, a:a + m], T.lxs[:, a:a + m], True, True).then_inc(S["m%d" % (4 * h + i)], 1)
        for i in range(4):
            src, dst = ps[:, 512 * i:512 * i + m], T.ht[:, t0 + i:t0 + 4 * m:4]
            vec = i == 3 or h and i == 1
            q = v if vec else sc
            q.wait_ge(S["m%d" % (4 * h + i)], 1)
            if vec:
                ts(dst, src, 0.0, 0.0625, A.max, A.mult)
            else:
                sc.activation(dst, src, F.Relu, scale=0.0625).then_inc(rs, 1)
        v.wait_ge(rs, 2 if h else 3)
        done()
        v.quantize_mx(T.hq[:, a:a + m], T.hqs[:, a:a + m], T.ht[:, t0:t0 + 4 * m]).then_inc(S.q2 if h else S.q1, 1)

    expert(1)
    to_far(T.hq, T.hqs, S.q2, S.q2, S.hret, T.hr, T.hrs)
    expert(0)
    fused(to_near([(q, ZC + CAPP * pos(q, rank)) for q in near], half, T.hq, T.hb, S.rsp)
          + [(handers(rank)[4], inside(rank, 4), S.hret, T.hqs[:, half - CAPP:half + rest], T.hrs[:, 0:half])], S.q1)
    a, b = half + 2 * CAPP, ZC + CAPP * pos(near[2], rank)
    fused([(ranks[near[2]], share(off(rank), 3)[2], S.rsp, T.hqs[:, a:a + CAPP], T.hbs[:, b:b + CAPP])])
    sy.wait_ge(S.dsp, near_in)
    sy.dma_start(T.vt[:], T.v[:]).then_inc(S.sv0, 16)

    v.wait_ge(S.su0, 16)
    v.quantize_mx(T.uq[:], T.us[:], T.ut[:]).then_inc(S.suq, 1)
    for q_, s_ in ((T.hb, T.hbs), (T.hab, T.habs)):
        op(v.tensor_copy(w32(q_, 0, ZC), w32(T.xq, 0, ZC + TOK).indirect(T.lo[:, 0:1])))
        sc.activation(s_[:, 0:ZC], T.xs[:, 0:ZC + TOK].indirect(T.lo[:, 0:1]), F.Copy).then_inc(S.sz2, 1)
    v.wait_ge(S.suq, 1)
    v.tensor_copy(w32(T.up, 0, 128), w32(T.uq, 0, 128).indirect(T.lo[:])).then_inc(S.sup, 1)
    sc.wait_ge(S.srz, 4)
    sc.wait_ge(S.srd, 48)
    for k in range(2):
        for d in range(2):
            sc.activation(T.d2[:, k, :, d, :], T.rz[:, 3 + k, :], F.Copy).then_inc(S.sd2, 1)
    sc.wait_ge(S.suq, 1)
    sc.activation(T.ups[:, 0:128], T.us[:, 0:128].indirect(T.lo[:]), F.Copy).then_inc(S.sups, 1)
    sc.activation(T.ra[:], T.rz[:, 0, :], F.Copy, scale=-6.0, bias=7.0).then_inc(S.ska, 1)
    sc.activation(T.rb[:], T.rz[:, 1, :], F.Copy, scale=-7.0).then_inc(S.ska, 1)
    v.wait_ge(S.srz, 4)
    v.wait_ge(S.srd, 48)
    v.wait_ge(S.gh, 3)
    tt(T.pa[:], T.rz[:, 0, :], T.jr[:], A.mult)
    tt(T.pb[:], T.rz[:, 1, :], T.jra[:], A.mult)
    v.wait_ge(S.sd2, 4)
    op(v.transpose(T.dt[:], T.d2[:]))
    done()
    tt(T.pp[:, :, 0, :], T.pa[:], T.pb[:], A.add)
    sc.wait_ge(S.v, n[0])
    sc.activation(T.pp[:, :, 1, :], T.pp[:, :, 0, :], F.Copy).then_inc(S.sp1, 1)
    v.tensor_copy(T.oh[:], T.dt[:, 0:512:32]).then_inc(S.soh, 1)
    v.wait_ge(S.sv0, 16)
    v.quantize_mx(T.vq[:], T.vs[:], T.vt[:]).then_inc(S.svq, 1)
    v.wait_ge(S.ska, 2)
    tt(T.kk[:], T.ra[:], T.rb[:], A.add)
    v.wait_ge(S.sp1, 1)
    done()
    op(v.transpose(T.ppt[:], T.pp[:]))
    done()

    for q in (v, sc):
        q.wait_ge(S.soh, 1)
        q.wait_ge(S.so, 1)
        q.wait_ge(S.rsp, near_back)
        q.wait_ge(S.rcr, far_in)
    sc.wait_ge(S.sz2, 2)
    for k, s1, s2 in ((1, S.sbb, S.sbbs), (0, S.sba, S.sbas)):
        a = ZC + TOK * k
        v.tensor_copy(w32(T.hab, a, a + 128), w32(T.hb, 0, 480).indirect(T.oh[:, 8 * k:8 * k + 8])).then_inc(s1, 1)
        sc.activation(T.habs[:, a:a + 128], T.hbs[:, 0:480].indirect(T.oh[:, 8 * k:8 * k + 8]), F.Copy).then_inc(s2, 1)
    for s in (S.sup, S.sups, S.svq, S.sbb, S.sbbs):
        te.wait_ge(s, 1)
    te.matmul_mx(T.psa[:, 0:128], T.up[:, 0:128], T.ups[:, 0:128], T.hab[:, ZC + TOK:ZC + 2 * TOK], T.habs[:, ZC + TOK:ZC + 2 * TOK], True, True).then_inc(S.mqb, 1)
    te.wait_ge(S.sba, 1)
    te.wait_ge(S.sbas, 1)
    te.matmul_mx(T.psa[:, 512:640], T.up[:, 0:128], T.ups[:, 0:128], T.hab[:, ZC:ZC + TOK], T.habs[:, ZC:ZC + TOK], True, True).then_inc(S.mqa, 1)
    te.matmul_mx(T.psa[:, 1024:1296], T.vq[:, 0:128], T.vs[:, 0:128], T.hab[:, 0:272], T.habs[:, 0:272], True, True).then_inc(S.my, 1)
    v.wait_ge(S.mqb, 1)
    tt(T.qb[:], T.psa[:, 0:128], T.rz[:, 2, :], A.add)
    v.wait_ge(S.mqa, 1)
    done()
    tt(T.ge[:], T.psa[:, 512:640], T.qb[:], A.is_ge)
    done()
    v.tensor_tensor(T.ww[:], T.ge[:], T.kk[:], A.is_equal).then_inc(S.sww, 1)
    v.wait_ge(S.sww, 1)
    v.tensor_tensor_scan(T.cc[:], T.ww[:], T.ww[:], 0.0, A.add, A.max).then_inc(S.scc, 1)
    for d in range(2):
        fl(v.tensor_copy(T.vv[:, :, d, :], T.ww[:]))
    v.wait_ge(S.scc, 1)
    for d in range(2):
        ts(T.lv[:, :, d, :], T.cc[:], 1.0 * CAPR, None, A.is_le)
    fdone()
    fl(v.transpose(T.vvt[:], T.vv[:]))
    done()
    op(v.transpose(T.lvt[:], T.lv[:]))
    fdone()
    fl(v.tensor_tensor(T.wp[:], T.vvt[:, :, 0:8], T.ppt[:, :, 0:8], A.mult))
    v.wait_ge(S.sgg, 2)
    op(v.transpose(T.ght[:], T.gh[:]))
    fdone()
    done()
    fl(v.tensor_tensor(T.vz[:], T.wp[:], T.lvt[:, :, 0:8], A.mult))
    v.wait_ge(S.sgs, 1)
    op(v.transpose(T.gst[:], T.gs[:]))
    fdone()
    v.tensor_reduce(T.oz[:], T.vz[:], X, A.max).then_inc(S.soz, 1)
    done()
    tt(T.ght[:, :, 0, 8:16], T.ght[:, :, 1, 0:8], T.gst[:, :, 0:8], A.mult)
    sc.wait_ge(S.my, 1)
    sc.activation(T.ya[:], T.psa[:, 1024:1296], F.Copy).then_inc(S.sya, 1)
    sc.wait_ge(S.scw, 3)
    sc.wait_ge(S.sww, 1)
    sc.activation(T.gh[:, :, 0, :], T.ww[:], F.Identity, scale=99.5, bias=T.cw[:, 2:3]).then_inc(S.sgg, 1)
    sc.activation(T.gh[:, :, 1, :], T.ww[:], F.Copy, scale=T.cw[:, 0:1]).then_inc(S.sgg, 1)
    sc.wait_ge(S.scc, 1)
    sc.activation(T.gs[:], T.cc[:], F.Sign, scale=-1.0, bias=CAPR + 0.5).then_inc(S.sgs, 1)
    v.wait_ge(S.soz, 1)
    v.tensor_copy(w32(T.zq, 0, 128), w32(T.hab, 0, 272).indirect(T.oz[:])).then_inc(S.szq, 1)
    v.tensor_copy(T.zs[:, 0:128], T.habs[:, 0:272].indirect(T.oz[:])).then_inc(S.szs, 1)
    sc.wait_ge(S.sya, 1)
    sc.wait_ge(S.soz, 1)
    sc.activation(T.yb[:], T.ya[:, 0:272].indirect(T.oz[:]), F.Copy).then_inc(S.sy, 1)
    done()
    op(v.tensor_reduce(T.wa[:, 0:4], T.ght[:, :, 0, 0:16], X, A.add))
    done()
    v.transpose(T.wb[:], T.wa[:]).then_inc(S.swn, 1)
    sy.wait_ge(S.szq, 1)
    sy.dma_start(T.oc[:, 0:512], cod(T.zq, 0, 128)).then_inc(S.fin, 16)
    sy.wait_ge(S.sy, 1)
    sy.dma_start(T.y[:], T.yb[:]).then_inc(S.fin, 16)
    for k in range(4):
        q = sc if k % 2 else sy
        q.wait_ge(S.szs, 1)
        q.dma_start(T.osc[4 * k:4 * k + 4, 0:128], T.zs[32 * k:32 * k + 4, 0:128]).then_inc(S.fin, 16)
    sy.wait_ge(S.swn, 1)
    sy.dma_start(T.wn[0:1, 0:128], T.wb[0:4, 0:32]).then_inc(S.fin, 16)
    sy.wait_ge(S.fin, 112)
    g.wait_ge(S.loc, nl[0])
